import numpy as np
import ml_dtypes


def mxq(x, axis, fmt="e4m3"):
    dtype, down = {"e4m3": (ml_dtypes.float8_e4m3fn, 7), "e5m2": (ml_dtypes.float8_e5m2, 14)}[fmt]
    v = np.moveaxis(np.asarray(x, np.float32).astype(ml_dtypes.bfloat16).astype(np.float64), axis, -1)
    blocks = v.reshape(v.shape[:-1] + (-1, 32))
    amax = np.abs(blocks).max(-1, keepdims=True)
    byte = np.maximum(np.where(amax > 0, np.frexp(amax)[1] - 1 + 127, 0) - down, 1)
    scale = np.exp2(byte - 127.0)
    codes = (blocks / scale).astype(np.float32).astype(dtype).astype(np.float64)
    return np.moveaxis((codes * scale).reshape(v.shape), -1, axis)


WIDE = False


def mx_kscale(k):
    if not WIDE:
        return np.ones(k)
    levels = np.array([30, -30])
    if k % 512:
        return np.exp2(np.random.permutation(np.resize(levels, k // 32))).repeat(32)
    a = np.empty((k // 512, 16))
    for p in range(k // 512):
        a[p, :8] = np.random.permutation(np.resize(levels, 8))
        for g in range(8):
            far = levels[np.abs(levels - a[p, g]) >= 10]
            a[p, g + 8] = far[np.random.randint(len(far))]
    return np.exp2(a.ravel()).repeat(32)


def f64(x):
    return np.asarray(x).astype(np.float64)


def striped(idx):
    return np.tile(idx.reshape(-1, 16).T, (8, 1)).astype(np.uint16)


def unstriped(offs):
    return offs[:16].T.reshape(-1).astype(np.int64)


E2M1 = np.array([0.0, 0.5, 1.0, 1.5, 2.0, 3.0, 4.0, 6.0, -0.0, -0.5, -1.0, -1.5, -2.0, -3.0, -4.0, -6.0])


def pack_weight(w, fmt):
    k, n = w.shape
    w = f64(np.asarray(w, np.float32).astype(ml_dtypes.bfloat16)).reshape(k // 32, 32, n)
    amax = np.abs(w).max(1)
    if fmt == "e4m3":
        byte = np.frexp(amax)[1] - 1 + 127 - 7
    else:
        mant, ex = np.frexp(amax / 6.0)
        byte = np.where(mant > 0.5, ex, ex - 1) + 127
    byte = np.clip(np.where(amax > 0, byte, 1), 1, 254)
    scaled = (w * np.exp2(127.0 - byte)[:, None, :]).reshape(k, n).astype(np.float32)
    by_word = np.ascontiguousarray(scaled.reshape(k // 512, 128, 4, n).transpose(0, 1, 3, 2))
    if fmt == "e4m3":
        words = by_word.astype(ml_dtypes.float8_e4m3fn).view(np.uint8)
    else:
        c = by_word.astype(ml_dtypes.float4_e2m1fn).view(np.uint8) & 0xF
        words = (c[..., 0::2] | (c[..., 1::2] << 4)).reshape(k // 512, 128, 2 * n)
    return np.ascontiguousarray(words), np.ascontiguousarray(byte.astype(np.uint8).reshape(k // 512, 16, n))


def unpack_weight(words, scales, fmt):
    g, _, n = scales.shape
    words = np.ascontiguousarray(words).reshape(g, 128, n, -1)
    if fmt == "e4m3":
        vals = words.view(ml_dtypes.float8_e4m3fn).astype(np.float64)
    else:
        nib = np.empty((g, 128, n, 4), np.uint8)
        nib[..., 0::2] = words & 0xF
        nib[..., 1::2] = words >> 4
        vals = E2M1[nib]
    vals = vals * np.repeat(np.exp2(scales.astype(np.float64) - 127.0), 8, axis=1)[..., None]
    return vals.transpose(0, 1, 3, 2).reshape(g * 512, n)


K, T, E, C, N = 384, 2048, 4, 512, 1024


def by_expert(wq, xq):
    return np.concatenate([wq[e].T @ xq[:, e * C:(e + 1) * C] for e in range(E)], axis=1)


def setup_inputs():
    n = np.random.standard_normal
    s = mx_kscale(N)[:, None]
    w = [pack_weight(m, "e2m1") for m in n((E, N, K)) / np.sqrt(N) / s[None]]
    return {
        "dyT": (n((N, T)) * s).astype(np.float32),
        "w_words": np.stack([m[0] for m in w]),
        "w_scales": np.stack([m[1] for m in w]),
        "gate": np.tile(np.random.uniform(0.2, 1.0, E * C), (N, 1)).astype(np.float32),
        "offs": striped(np.random.permutation(T)[:E * C]),
    }


def reference(dyT, w_words, w_scales, gate, offs):
    idx = unstriped(offs)
    w = np.stack([unpack_weight(w_words[e], w_scales[e], "e2m1") for e in range(E)])
    gq = mxq(f64(gate) * f64(dyT)[:, idx], 0, "e5m2")
    dx = by_expert(w, gq)
    out = np.zeros((K, T))
    out[:, idx] = dx
    return out

@@ -1,0 +1,165 @@
+from contextlib import ExitStack
+
+import concourse.mybir as mybir
+
+K, T, E, C, N = 384, 2048, 4, 512, 1024
+FLOPS = 2 * K * N * E * C
+BYTES = 4 * N * T + 2 * E * N * K // 4 + E * N // 32 * K + 4 * T + 2 * 128 * T // 16 + 4 * K * T
+
+F32 = mybir.dt.float32
+BF16 = mybir.dt.bfloat16
+I32 = mybir.dt.int32
+U32 = mybir.dt.uint32
+U16 = mybir.dt.uint16
+U8 = mybir.dt.uint8
+FP8X4 = mybir.dt.float8_e5m2_x4
+FP4X4 = mybir.dt.float4_e2m1fn_x4
+MULT = mybir.AluOpType.mult
+
+P = 128
+PACK = 4
+PASSES = N // (P * PACK)
+KT = K // P
+GROUPS = E * PASSES
+PAIR = 2 * C
+FIRST = 256
+PAIRS = E // 2
+
+
+def tile_moe_bdx_lin_none_kernel(tc, dyT, w_words, w_scales, gate, offs, out):
+    nc = tc.nc
+    with ExitStack() as ctx:
+        held = ctx.enter_context(tc.tile_pool(name="held", bufs=1))
+        gath = ctx.enter_context(tc.tile_pool(name="gath", bufs=3))
+        psum = ctx.enter_context(tc.psum_pool(name="psum", bufs=8))
+
+        offsets = held.tile([P, T // 16], U16, name="offsets")
+        gates = held.tile([P, T], F32, name="gates")
+        dy = [[held.tile([P, T], F32, name=f"dy{a}{t}") for t in range(PACK)] for a in range(PASSES)]
+        words = held.tile([P, GROUPS * 2 * K], U8, name="words", align_bytes=64)
+        wplanes = held.tile([P, GROUPS * K], U8, name="wplanes", align_bytes=64)
+        outs = [held.tile([P, T], F32, name=f"outs{kt}") for kt in range(KT)]
+        codes = [held.tile([P, T], U32, name=f"codes{a}", align_bytes=64) for a in range(PASSES)]
+        planes = [held.tile([P, T], U8, name=f"planes{a}", align_bytes=64) for a in range(PASSES)]
+
+        dy_rows = dyT.rearrange("(a p t) c -> a t p c", a=PASSES, p=P, t=PACK)
+
+        nc.vector.memset(wplanes[:].bitcast(I32), 0)
+
+        nc.scalar.dma_start(dy[0][0][:], dy_rows[0, 0])
+        nc.sync.dma_start(offsets[:], offs)
+        nc.sync.dma_start(gates[:, 0:FIRST], gate[0:P, 0:FIRST])
+        nc.sync.dma_start(gates[:, FIRST:PAIR], gate[0:P, FIRST:PAIR])
+        nc.sync.dma_start(gates[:, PAIR:T], gate[0:P, PAIR:T])
+        for a in range(PASSES):
+            for t in range(PACK):
+                if a + t > 0:
+                    nc.sync.dma_start(dy[a][t][:], dy_rows[a, t])
+        nc.sync.dma_start(
+            words[:].bitcast(I32).rearrange("p (g b) -> p g b", g=GROUPS),
+            w_words.bitcast(I32).rearrange("e a p b -> p (e a) b"),
+        )
+        for q in range(4):
+            nc.sync.dma_start(
+                wplanes[32 * q : 32 * q + 4, :].bitcast(I32).rearrange("p (g k) -> p g k", g=GROUPS),
+                w_scales.bitcast(I32).rearrange("e a f k -> f (e a) k")[4 * q : 4 * q + 4, :, :],
+            )
+
+        def gather(g4, a, t, pair, lo, hi):
+            s0 = pair * PAIR + lo
+            s1 = pair * PAIR + hi
+            nc.vector.tensor_tensor(
+                g4[:, t, lo:hi],
+                dy[a][t][:].indirect(offsets[:, s0 // 16 : s1 // 16]),
+                gates[:, s0:s1],
+                MULT,
+            )
+
+        def interleave(g4):
+            grouped = gath.tile([P, PAIR, PACK], BF16, name="grouped", bufs=3, align_bytes=64)
+            for half in range(2):
+                cols = slice(half * C, (half + 1) * C)
+                nc.scalar.copy(
+                    grouped[:, cols, :].rearrange("p (c i) t -> p c t i", i=4),
+                    g4[:, :, cols].rearrange("p t (c i) -> p c t i", i=4),
+                )
+            return grouped
+
+        def quantise(grouped, a, pair):
+            cols = slice(pair * PAIR, (pair + 1) * PAIR)
+            nc.vector.quantize_mx(
+                out=codes[a][:, cols].bitcast(FP8X4),
+                scales=planes[a][:, cols],
+                in_=grouped[:].rearrange("p n t -> p (n t)"),
+            )
+
+        def new_g4():
+            g4 = gath.tile([P, PACK, PAIR], F32, name="g4")
+            return g4
+
+        def products(pair, kts):
+            ys = []
+            for kt in kts:
+                y = held.tile([P, PAIR], F32, name=f"y{pair}{kt}")
+                ys.append(y)
+                accs = [psum.tile([P, C], F32, name="acc") for half in range(2)]
+                for a in range(PASSES):
+                    for half in range(2):
+                        e = 2 * pair + half
+                        cols = slice(e * C, (e + 1) * C)
+                        w0 = (e * PASSES + a) * K + P * kt
+                        nc.tensor.matmul_mx(
+                            out=accs[half][:],
+                            lhsT=words[:, 2 * w0 : 2 * (w0 + P)].bitcast(FP4X4),
+                            lhsT_scale=wplanes[:, w0 : w0 + P],
+                            rhs=codes[a][:, cols].bitcast(FP8X4),
+                            rhs_scale=planes[a][:, cols],
+                            start=(a == 0),
+                            stop=(a == PASSES - 1),
+                        )
+                for half in range(2):
+                    nc.scalar.copy(y[:, half * C : (half + 1) * C], accs[half][:])
+            return ys
+
+        def scatter(ys, pair, kt):
+            nc.vector.tensor_copy(
+                outs[kt][:].indirect(offsets[:, pair * PAIR // 16 : (pair + 1) * PAIR // 16]), ys[kt][:]
+            )
+
+        g00 = new_g4()
+        g01 = new_g4()
+        gather(g00, 0, 0, 0, 0, FIRST)
+        gather(g00, 0, 0, 0, FIRST, PAIR)
+        gather(g01, 0, 0, 1, 0, PAIR)
+        gather(g00, 0, 1, 0, 0, PAIR)
+        gather(g01, 0, 1, 1, 0, PAIR)
+        gather(g00, 0, 2, 0, 0, PAIR)
+        gather(g00, 0, 3, 0, 0, PAIR)
+        b00 = interleave(g00)
+        g10 = new_g4()
+        for t in range(PACK):
+            gather(g10, 1, t, 0, 0, PAIR)
+        b10 = interleave(g10)
+        quantise(b00, 0, 0)
+        gather(g01, 0, 2, 1, 0, PAIR)
+        gather(g01, 0, 3, 1, 0, PAIR)
+        b01 = interleave(g01)
+        quantise(b10, 1, 0)
+        y0 = products(0, (0,))
+        g11 = new_g4()
+        for t in range(PACK):
+            gather(g11, 1, t, 1, 0, PAIR)
+        quantise(b01, 0, 1)
+        b11 = interleave(g11)
+        y0 += products(0, (1, 2))
+
+        scatter(y0, 0, 0)
+        quantise(b11, 1, 1)
+        y1 = products(1, range(KT))
+        scatter(y0, 0, 1)
+        scatter(y0, 0, 2)
+        for kt in range(KT):
+            scatter(y1, 1, kt)
+            rows = slice(kt * P, (kt + 1) * P)
+            nc.sync.dma_start(out[rows, 0:PAIR], outs[kt][:, 0:PAIR])
+            nc.scalar.dma_start(out[rows, PAIR:T], outs[kt][:, PAIR:T])

@@ -30,30 +30,32 @@ def tile_moe_bdx_lin_none_kernel(tc, dyT, w_words, w_scales, gate, offs, out):
     nc = tc.nc
     with ExitStack() as ctx:
         held = ctx.enter_context(tc.tile_pool(name="held", bufs=1))
-        gath = ctx.enter_context(tc.tile_pool(name="gath", bufs=3))
         psum = ctx.enter_context(tc.psum_pool(name="psum", bufs=8))
 
         offsets = held.tile([P, T // 16], U16, name="offsets")
-        gates = held.tile([P, T], F32, name="gates")
+        gates = [
+            held.tile([P, PAIR], F32, name="gates0", tag="early", align_bytes=64),
+            held.tile([P, PAIR], F32, name="gates1"),
+        ]
         dy = [[held.tile([P, T], F32, name=f"dy{a}{t}") for t in range(PACK)] for a in range(PASSES)]
         words = held.tile([P, GROUPS * 2 * K], U8, name="words", align_bytes=64)
         wplanes = held.tile([P, GROUPS * K], U8, name="wplanes", align_bytes=64)
         outs = [held.tile([P, T], F32, name=f"outs{kt}") for kt in range(KT)]
-        codes = [held.tile([P, T], U32, name=f"codes{a}", align_bytes=64) for a in range(PASSES)]
+        codes = [None, held.tile([P, T], U32, name="codes1", align_bytes=64)]
         planes = [held.tile([P, T], U8, name=f"planes{a}", align_bytes=64) for a in range(PASSES)]
 
         dy_rows = dyT.rearrange("(a p t) c -> a t p c", a=PASSES, p=P, t=PACK)
 
         nc.vector.memset(wplanes[:].bitcast(I32), 0)
 
-        nc.scalar.dma_start(dy[0][0][:], dy_rows[0, 0])
         nc.sync.dma_start(offsets[:], offs)
-        nc.sync.dma_start(gates[:, 0:FIRST], gate[0:P, 0:FIRST])
-        nc.sync.dma_start(gates[:, FIRST:PAIR], gate[0:P, FIRST:PAIR])
-        nc.sync.dma_start(gates[:, PAIR:T], gate[0:P, PAIR:T])
+        nc.sync.dma_start(gates[0][:, 0:FIRST], gate[0:P, 0:FIRST])
+        nc.sync.dma_start(dy[0][0][:], dy_rows[0, 0])
+        nc.sync.dma_start(gates[0][:, FIRST:PAIR], gate[0:P, FIRST:PAIR])
+        nc.sync.dma_start(gates[1][:], gate[0:P, PAIR:T])
         for a in range(PASSES):
             for t in range(PACK):
-                if a + t > 0:
+                if 0 < PACK * a + t < 7:
                     nc.sync.dma_start(dy[a][t][:], dy_rows[a, t])
         nc.sync.dma_start(
             words[:].bitcast(I32).rearrange("p (g b) -> p g b", g=GROUPS),
@@ -64,6 +66,7 @@ def tile_moe_bdx_lin_none_kernel(tc, dyT, w_words, w_scales, gate, offs, out):
                 wplanes[32 * q : 32 * q + 4, :].bitcast(I32).rearrange("p (g k) -> p g k", g=GROUPS),
                 w_scales.bitcast(I32).rearrange("e a f k -> f (e a) k")[4 * q : 4 * q + 4, :, :],
             )
+        nc.sync.dma_start(dy[1][3][:], dy_rows[1, 3])
 
         def gather(g4, a, t, pair, lo, hi):
             s0 = pair * PAIR + lo
@@ -71,36 +74,29 @@ def tile_moe_bdx_lin_none_kernel(tc, dyT, w_words, w_scales, gate, offs, out):
             nc.vector.tensor_tensor(
                 g4[:, t, lo:hi],
                 dy[a][t][:].indirect(offsets[:, s0 // 16 : s1 // 16]),
-                gates[:, s0:s1],
+                gates[pair][:, lo:hi],
                 MULT,
             )
 
-        def interleave(g4):
-            grouped = gath.tile([P, PAIR, PACK], BF16, name="grouped", bufs=3, align_bytes=64)
+        def interleave(g4, grouped):
             for half in range(2):
                 cols = slice(half * C, (half + 1) * C)
                 nc.scalar.copy(
-                    grouped[:, cols, :].rearrange("p (c i) t -> p c t i", i=4),
+                    grouped.rearrange("p (n t) -> p n t", t=PACK)[:, cols, :].rearrange("p (c i) t -> p c t i", i=4),
                     g4[:, :, cols].rearrange("p t (c i) -> p c t i", i=4),
                 )
-            return grouped
 
         def quantise(grouped, a, pair):
             cols = slice(pair * PAIR, (pair + 1) * PAIR)
-            nc.vector.quantize_mx(
-                out=codes[a][:, cols].bitcast(FP8X4),
-                scales=planes[a][:, cols],
-                in_=grouped[:].rearrange("p n t -> p (n t)"),
-            )
-
-        def new_g4():
-            g4 = gath.tile([P, PACK, PAIR], F32, name="g4")
-            return g4
+            nc.vector.quantize_mx(out=codes[a][:, cols].bitcast(FP8X4), scales=planes[a][:, cols], in_=grouped)
 
         def products(pair, kts):
             ys = []
             for kt in kts:
-                y = held.tile([P, PAIR], F32, name=f"y{pair}{kt}")
+                if (pair, kt) == (0, KT - 1):
+                    y = shared[:, 0:PAIR]
+                else:
+                    y = held.tile([P, PAIR], F32, name=f"y{pair}{kt}")[:]
                 ys.append(y)
                 accs = [psum.tile([P, C], F32, name="acc") for half in range(2)]
                 for a in range(PASSES):
@@ -123,38 +119,44 @@ def tile_moe_bdx_lin_none_kernel(tc, dyT, w_words, w_scales, gate, offs, out):
 
         def scatter(ys, pair, kt):
             nc.vector.tensor_copy(
-                outs[kt][:].indirect(offsets[:, pair * PAIR // 16 : (pair + 1) * PAIR // 16]), ys[kt][:]
+                outs[kt][:].indirect(offsets[:, pair * PAIR // 16 : (pair + 1) * PAIR // 16]), ys[kt]
             )
 
-        g00 = new_g4()
-        g01 = new_g4()
+        g00 = held.tile([P, PACK, PAIR], F32, name="g00")
+        g01 = held.tile([P, PACK, PAIR], F32, name="g01")
+        g10 = held.tile([P, PACK, PAIR], F32, name="g10")
+        shared = held.tile([P, PACK * PAIR], F32, name="shared", align_bytes=64)
+        g11 = shared[:].rearrange("p (t c) -> p t c", t=PACK)
+        b01 = shared[:, 0 : 2 * PAIR].bitcast(BF16)
+        b10 = shared[:, 2 * PAIR : 4 * PAIR].bitcast(BF16)
+        b00 = held.tile([P, PACK * PAIR], BF16, name="b00", align_bytes=64)
+        b11 = held.tile([P, PACK * PAIR], BF16, name="b11", align_bytes=64)
+
         gather(g00, 0, 0, 0, 0, FIRST)
         gather(g00, 0, 0, 0, FIRST, PAIR)
         gather(g01, 0, 0, 1, 0, PAIR)
-        gather(g00, 0, 1, 0, 0, PAIR)
-        gather(g01, 0, 1, 1, 0, PAIR)
-        gather(g00, 0, 2, 0, 0, PAIR)
-        gather(g00, 0, 3, 0, 0, PAIR)
-        b00 = interleave(g00)
-        g10 = new_g4()
+        for t in range(1, PACK):
+            gather(g00, 0, t, 0, 0, PAIR)
+            gather(g01, 0, t, 1, 0, PAIR)
+        interleave(g00, b00[:])
+        interleave(g01, b01)
         for t in range(PACK):
             gather(g10, 1, t, 0, 0, PAIR)
-        b10 = interleave(g10)
-        quantise(b00, 0, 0)
-        gather(g01, 0, 2, 1, 0, PAIR)
-        gather(g01, 0, 3, 1, 0, PAIR)
-        b01 = interleave(g01)
-        quantise(b10, 1, 0)
-        y0 = products(0, (0,))
-        g11 = new_g4()
-        for t in range(PACK):
-            gather(g11, 1, t, 1, 0, PAIR)
+        interleave(g10, b10)
+        codes[0] = held.tile([P, T], U32, name="codes0", tag="early", align_bytes=64)
+        quantise(b00[:], 0, 0)
         quantise(b01, 0, 1)
-        b11 = interleave(g11)
+        gather(g11, 1, 0, 1, 0, PAIR)
+        gather(g11, 1, 1, 1, 0, PAIR)
+        quantise(b10, 1, 0)
+        gather(g11, 1, 2, 1, 0, PAIR)
+        gather(g11, 1, 3, 1, 0, PAIR)
+        y0 = products(0, (0,))
+        interleave(g11, b11[:])
         y0 += products(0, (1, 2))
 
         scatter(y0, 0, 0)
-        quantise(b11, 1, 1)
+        quantise(b11[:], 1, 1)
         y1 = products(1, range(KT))
         scatter(y0, 0, 1)
         scatter(y0, 0, 2)

@@ -1,6 +1,7 @@
 from contextlib import ExitStack
 
 import concourse.mybir as mybir
+from concourse.masks import make_identity
 
 K, T, E, C, N = 384, 2048, 4, 512, 1024
 FLOPS = 2 * K * N * E * C
@@ -22,7 +23,7 @@ PASSES = N // (P * PACK)
 KT = K // P
 GROUPS = E * PASSES
 PAIR = 2 * C
-FIRST = 256
+FIRST = 512
 PAIRS = E // 2
 
 
@@ -48,11 +49,25 @@ def tile_moe_bdx_lin_none_kernel(tc, dyT, w_words, w_scales, gate, offs, out):
 
         nc.vector.memset(wplanes[:].bitcast(I32), 0)
 
+        gate_cols = held.tile([P, E, 8], F32, name="gate_cols")
+        gate_row = gate[0, :].rearrange("(e p i) -> p e i", e=E, p=P, i=4)
+        nc.scalar.dma_start(gate_cols[:, 0:2, 0:4], gate_row[:, 0:2, :])
         nc.sync.dma_start(offsets[:], offs)
-        nc.sync.dma_start(gates[0][:, 0:FIRST], gate[0:P, 0:FIRST])
         nc.sync.dma_start(dy[0][0][:], dy_rows[0, 0])
-        nc.sync.dma_start(gates[0][:, FIRST:PAIR], gate[0:P, FIRST:PAIR])
-        nc.sync.dma_start(gates[1][:], gate[0:P, PAIR:T])
+        nc.sync.dma_start(gate_cols[:, 2:4, 0:4], gate_row[:, 2:4, :])
+        identity = held.tile([P, P], F32, name="identity")
+        make_identity(nc, identity[:])
+        for e in range(E):
+            spread = psum.tile([P, C], F32, name="acc")
+            for i in range(4):
+                nc.tensor.transpose(
+                    spread[:, i * P : (i + 1) * P], gate_cols[:, e, i : i + 1].to_broadcast([P, P]), identity[:]
+                )
+            nc.scalar.copy(
+                gates[e // 2][:, (e % 2) * C : (e % 2 + 1) * C].rearrange("m (p i) -> m p i", i=4),
+                spread[:].rearrange("m (i p) -> m p i", i=4),
+            )
+
         for a in range(PASSES):
             for t in range(PACK):
                 if 0 < PACK * a + t < 7:
@@ -144,8 +159,8 @@ def tile_moe_bdx_lin_none_kernel(tc, dyT, w_words, w_scales, gate, offs, out):
             gather(g10, 1, t, 0, 0, PAIR)
         interleave(g10, b10)
         codes[0] = held.tile([P, T], U32, name="codes0", tag="early", align_bytes=64)
-        quantise(b00[:], 0, 0)
         quantise(b01, 0, 1)
+        quantise(b00[:], 0, 0)
         gather(g11, 1, 0, 1, 0, PAIR)
         gather(g11, 1, 1, 1, 0, PAIR)
         quantise(b10, 1, 0)

@@ -42,7 +42,10 @@ def tile_moe_bdx_lin_none_kernel(tc, dyT, w_words, w_scales, gate, offs, out):
         words = held.tile([P, GROUPS * 2 * K], U8, name="words", align_bytes=64)
         wplanes = held.tile([P, GROUPS * K], U8, name="wplanes", align_bytes=64)
         outs = [held.tile([P, T], F32, name=f"outs{kt}") for kt in range(KT)]
-        codes = [None, held.tile([P, T], U32, name="codes1", align_bytes=64)]
+        codes = {
+            quarter: held.tile([P, PAIR], U32, name="codes%d%d" % quarter, align_bytes=64)
+            for quarter in ((0, 0), (1, 0), (1, 1))
+        }
         planes = [held.tile([P, T], U8, name=f"planes{a}", align_bytes=64) for a in range(PASSES)]
 
         dy_rows = dyT.rearrange("(a p t) c -> a t p c", a=PASSES, p=P, t=PACK)
@@ -103,7 +106,7 @@ def tile_moe_bdx_lin_none_kernel(tc, dyT, w_words, w_scales, gate, offs, out):
 
         def quantise(grouped, a, pair):
             cols = slice(pair * PAIR, (pair + 1) * PAIR)
-            nc.vector.quantize_mx(out=codes[a][:, cols].bitcast(FP8X4), scales=planes[a][:, cols], in_=grouped)
+            nc.vector.quantize_mx(out=codes[a, pair][:].bitcast(FP8X4), scales=planes[a][:, cols], in_=grouped)
 
         def products(pair, kts):
             ys = []
@@ -123,7 +126,7 @@ def tile_moe_bdx_lin_none_kernel(tc, dyT, w_words, w_scales, gate, offs, out):
                             out=accs[half][:],
                             lhsT=words[:, 2 * w0 : 2 * (w0 + P)].bitcast(FP4X4),
                             lhsT_scale=wplanes[:, w0 : w0 + P],
-                            rhs=codes[a][:, cols].bitcast(FP8X4),
+                            rhs=codes[a, pair][:, half * C : (half + 1) * C].bitcast(FP8X4),
                             rhs_scale=planes[a][:, cols],
                             start=(a == 0),
                             stop=(a == PASSES - 1),
@@ -139,12 +142,9 @@ def tile_moe_bdx_lin_none_kernel(tc, dyT, w_words, w_scales, gate, offs, out):
 
         g00 = held.tile([P, PACK, PAIR], F32, name="g00")
         g01 = held.tile([P, PACK, PAIR], F32, name="g01")
-        g10 = held.tile([P, PACK, PAIR], F32, name="g10")
-        shared = held.tile([P, PACK * PAIR], F32, name="shared", align_bytes=64)
-        g11 = shared[:].rearrange("p (t c) -> p t c", t=PACK)
-        b01 = shared[:, 0 : 2 * PAIR].bitcast(BF16)
-        b10 = shared[:, 2 * PAIR : 4 * PAIR].bitcast(BF16)
+        g10 = held.tile([P, PACK, PAIR], F32, name="g10", tag="late", align_bytes=64)
         b00 = held.tile([P, PACK * PAIR], BF16, name="b00", align_bytes=64)
+        b01 = held.tile([P, PACK * PAIR], BF16, name="b01", align_bytes=64)
         b11 = held.tile([P, PACK * PAIR], BF16, name="b11", align_bytes=64)
 
         gather(g00, 0, 0, 0, 0, FIRST)
@@ -154,18 +154,20 @@ def tile_moe_bdx_lin_none_kernel(tc, dyT, w_words, w_scales, gate, offs, out):
             gather(g00, 0, t, 0, 0, PAIR)
             gather(g01, 0, t, 1, 0, PAIR)
         interleave(g00, b00[:])
-        interleave(g01, b01)
+        interleave(g01, b01[:])
         for t in range(PACK):
             gather(g10, 1, t, 0, 0, PAIR)
+        shared = held.tile([P, (PACK + 1) * PAIR], F32, name="shared", tag="early", align_bytes=64)
+        g11 = shared[:, 0 : PACK * PAIR].rearrange("p (t c) -> p t c", t=PACK)
+        b10 = shared[:, 3 * PAIR : 5 * PAIR].bitcast(BF16)
         interleave(g10, b10)
-        codes[0] = held.tile([P, T], U32, name="codes0", tag="early", align_bytes=64)
-        quantise(b01, 0, 1)
         quantise(b00[:], 0, 0)
-        gather(g11, 1, 0, 1, 0, PAIR)
-        gather(g11, 1, 1, 1, 0, PAIR)
+        for t in range(PACK - 1):
+            gather(g11, 1, t, 1, 0, PAIR)
         quantise(b10, 1, 0)
-        gather(g11, 1, 2, 1, 0, PAIR)
-        gather(g11, 1, 3, 1, 0, PAIR)
+        codes[0, 1] = held.tile([P, PAIR], U32, name="codes01", tag="late", align_bytes=64)
+        quantise(b01[:], 0, 1)
+        gather(g11, 1, PACK - 1, 1, 0, PAIR)
         y0 = products(0, (0,))
         interleave(g11, b11[:])
         y0 += products(0, (1, 2))

@@ -75,16 +75,22 @@ def tile_moe_bdx_lin_none_kernel(tc, dyT, w_words, w_scales, gate, offs, out):
             for t in range(PACK):
                 if 0 < PACK * a + t < 7:
                     nc.sync.dma_start(dy[a][t][:], dy_rows[a, t])
-        nc.sync.dma_start(
-            words[:].bitcast(I32).rearrange("p (g b) -> p g b", g=GROUPS),
-            w_words.bitcast(I32).rearrange("e a p b -> p (e a) b"),
-        )
-        for q in range(4):
+
+        def load_scales(q):
             nc.sync.dma_start(
                 wplanes[32 * q : 32 * q + 4, :].bitcast(I32).rearrange("p (g k) -> p g k", g=GROUPS),
                 w_scales.bitcast(I32).rearrange("e a f k -> f (e a) k")[4 * q : 4 * q + 4, :, :],
             )
+
+        for q in range(2):
+            load_scales(q)
         nc.sync.dma_start(dy[1][3][:], dy_rows[1, 3])
+        nc.sync.dma_start(
+            words[:].bitcast(I32).rearrange("p (g b) -> p g b", g=GROUPS),
+            w_words.bitcast(I32).rearrange("e a p b -> p (e a) b"),
+        )
+        for q in range(2, 4):
+            load_scales(q)
 
         def gather(g4, a, t, pair, lo, hi):
             s0 = pair * PAIR + lo
@@ -151,10 +157,10 @@ def tile_moe_bdx_lin_none_kernel(tc, dyT, w_words, w_scales, gate, offs, out):
         gather(g00, 0, 0, 0, FIRST, PAIR)
         gather(g01, 0, 0, 1, 0, PAIR)
         for t in range(1, PACK):
-            gather(g00, 0, t, 0, 0, PAIR)
             gather(g01, 0, t, 1, 0, PAIR)
-        interleave(g00, b00[:])
+            gather(g00, 0, t, 0, 0, PAIR)
         interleave(g01, b01[:])
+        interleave(g00, b00[:])
         for t in range(PACK):
             gather(g10, 1, t, 0, 0, PAIR)
         shared = held.tile([P, (PACK + 1) * PAIR], F32, name="shared", tag="early", align_bytes=64)

@@ -54,7 +54,7 @@ def tile_moe_bdx_lin_none_kernel(tc, dyT, w_words, w_scales, gate, offs, out):
 
         gate_cols = held.tile([P, E, 8], F32, name="gate_cols")
         gate_row = gate[0, :].rearrange("(e p i) -> p e i", e=E, p=P, i=4)
-        nc.scalar.dma_start(gate_cols[:, 0:2, 0:4], gate_row[:, 0:2, :])
+        nc.sync.dma_start(gate_cols[:, 0:2, 0:4], gate_row[:, 0:2, :])
         nc.sync.dma_start(offsets[:], offs)
         nc.sync.dma_start(dy[0][0][:], dy_rows[0, 0])
         nc.sync.dma_start(gate_cols[:, 2:4, 0:4], gate_row[:, 2:4, :])
@@ -110,9 +110,12 @@ def tile_moe_bdx_lin_none_kernel(tc, dyT, w_words, w_scales, gate, offs, out):
                     g4[:, :, cols].rearrange("p t (c i) -> p c t i", i=4),
                 )
 
-        def quantise(grouped, a, pair):
-            cols = slice(pair * PAIR, (pair + 1) * PAIR)
-            nc.vector.quantize_mx(out=codes[a, pair][:].bitcast(FP8X4), scales=planes[a][:, cols], in_=grouped)
+        def quantise(grouped, a, pair, lo=0, hi=PAIR):
+            nc.vector.quantize_mx(
+                out=codes[a, pair][:, lo:hi].bitcast(FP8X4),
+                scales=planes[a][:, pair * PAIR + lo : pair * PAIR + hi],
+                in_=grouped[:, PACK * lo : PACK * hi],
+            )
 
         def products(pair, kts):
             ys = []
@@ -170,7 +173,8 @@ def tile_moe_bdx_lin_none_kernel(tc, dyT, w_words, w_scales, gate, offs, out):
         quantise(b00[:], 0, 0)
         for t in range(PACK - 1):
             gather(g11, 1, t, 1, 0, PAIR)
-        quantise(b10, 1, 0)
+        quantise(b10, 1, 0, 0, C)
+        quantise(b10, 1, 0, C, PAIR)
         codes[0, 1] = held.tile([P, PAIR], U32, name="codes01", tag="late", align_bytes=64)
         quantise(b01[:], 0, 1)
         gather(g11, 1, PACK - 1, 1, 0, PAIR)

@@ -22,9 +22,13 @@ PACK = 4
 PASSES = N // (P * PACK)
 KT = K // P
 GROUPS = E * PASSES
-PAIR = 2 * C
-FIRST = 512
-PAIRS = E // 2
+HALF = 2 * C
+PER_COLUMN = 16
+RUN = C // P
+LINE = 4
+QUADRANTS = 4
+MX_ALIGN = 64
+EARLY_SCALE_LOADS = 1
 
 
 def tile_moe_bdx_lin_none_kernel(tc, dyT, w_words, w_scales, gate, offs, out):
@@ -33,162 +37,160 @@ def tile_moe_bdx_lin_none_kernel(tc, dyT, w_words, w_scales, gate, offs, out):
         held = ctx.enter_context(tc.tile_pool(name="held", bufs=1))
         psum = ctx.enter_context(tc.psum_pool(name="psum", bufs=8))
 
-        offsets = held.tile([P, T // 16], U16, name="offsets")
+        offsets = held.tile([P, T // PER_COLUMN], U16, name="offsets")
         gates = [
-            held.tile([P, PAIR], F32, name="gates0", tag="early", align_bytes=64),
-            held.tile([P, PAIR], F32, name="gates1"),
+            held.tile([P, HALF], F32, name="gates0", tag="gates0_then_last", align_bytes=MX_ALIGN),
+            held.tile([P, HALF], F32, name="gates1"),
         ]
         dy = [[held.tile([P, T], F32, name=f"dy{a}{t}") for t in range(PACK)] for a in range(PASSES)]
-        words = held.tile([P, GROUPS * 2 * K], U8, name="words", align_bytes=64)
-        wplanes = held.tile([P, GROUPS * K], U8, name="wplanes", align_bytes=64)
+        words = held.tile([P, GROUPS * 2 * K], U8, name="words", align_bytes=MX_ALIGN)
+        word_scales = held.tile([P, GROUPS * K], U8, name="word_scales", align_bytes=MX_ALIGN)
         outs = [held.tile([P, T], F32, name=f"outs{kt}") for kt in range(KT)]
         codes = {
-            quarter: held.tile([P, PAIR], U32, name="codes%d%d" % quarter, align_bytes=64)
+            quarter: held.tile([P, HALF], U32, name="codes%d%d" % quarter, align_bytes=MX_ALIGN)
             for quarter in ((0, 0), (1, 0), (1, 1))
         }
-        planes = [held.tile([P, T], U8, name=f"planes{a}", align_bytes=64) for a in range(PASSES)]
+        code_scales = [held.tile([P, T], U8, name=f"code_scales{a}", align_bytes=MX_ALIGN) for a in range(PASSES)]
 
         dy_rows = dyT.rearrange("(a p t) c -> a t p c", a=PASSES, p=P, t=PACK)
 
-        nc.vector.memset(wplanes[:].bitcast(I32), 0)
+        nc.vector.memset(word_scales[:].bitcast(I32), 0)
 
-        gate_cols = held.tile([P, E, 8], F32, name="gate_cols")
-        gate_row = gate[0, :].rearrange("(e p i) -> p e i", e=E, p=P, i=4)
-        nc.sync.dma_start(gate_cols[:, 0:2, 0:4], gate_row[:, 0:2, :])
+        gate_cols = held.tile([P, E, 2 * RUN], F32, name="gate_cols")
+        gate_row = gate[0, :].rearrange("(e p i) -> p e i", e=E, p=P, i=RUN)
+        nc.sync.dma_start(gate_cols[:, 0 : E // 2, 0:RUN], gate_row[:, 0 : E // 2, :])
         nc.sync.dma_start(offsets[:], offs)
         nc.sync.dma_start(dy[0][0][:], dy_rows[0, 0])
-        nc.sync.dma_start(gate_cols[:, 2:4, 0:4], gate_row[:, 2:4, :])
+        nc.sync.dma_start(gate_cols[:, E // 2 : E, 0:RUN], gate_row[:, E // 2 : E, :])
+
         identity = held.tile([P, P], F32, name="identity")
         make_identity(nc, identity[:])
         for e in range(E):
-            spread = psum.tile([P, C], F32, name="acc")
-            for i in range(4):
+            spread = psum.tile([P, C], F32, name="bank")
+            for i in range(RUN):
                 nc.tensor.transpose(
                     spread[:, i * P : (i + 1) * P], gate_cols[:, e, i : i + 1].to_broadcast([P, P]), identity[:]
                 )
             nc.scalar.copy(
-                gates[e // 2][:, (e % 2) * C : (e % 2 + 1) * C].rearrange("m (p i) -> m p i", i=4),
-                spread[:].rearrange("m (i p) -> m p i", i=4),
+                gates[e // 2][:, (e % 2) * C : (e % 2 + 1) * C].rearrange("m (p i) -> m p i", i=RUN),
+                spread[:].rearrange("m (i p) -> m p i", i=RUN),
             )
-
-        for a in range(PASSES):
-            for t in range(PACK):
-                if 0 < PACK * a + t < 7:
-                    nc.sync.dma_start(dy[a][t][:], dy_rows[a, t])
 
         def load_scales(q):
             nc.sync.dma_start(
-                wplanes[32 * q : 32 * q + 4, :].bitcast(I32).rearrange("p (g k) -> p g k", g=GROUPS),
+                word_scales[32 * q : 32 * q + 4, :].bitcast(I32).rearrange("p (g k) -> p g k", g=GROUPS),
                 w_scales.bitcast(I32).rearrange("e a f k -> f (e a) k")[4 * q : 4 * q + 4, :, :],
             )
 
-        for q in range(2):
+        later_tiles = [(a, t) for a in range(PASSES) for t in range(PACK)][1:]
+        for a, t in later_tiles[:-1]:
+            nc.sync.dma_start(dy[a][t][:], dy_rows[a, t])
+        for q in range(EARLY_SCALE_LOADS):
             load_scales(q)
-        nc.sync.dma_start(dy[1][3][:], dy_rows[1, 3])
+        nc.sync.dma_start(dy[PASSES - 1][PACK - 1][:], dy_rows[PASSES - 1, PACK - 1])
         nc.sync.dma_start(
             words[:].bitcast(I32).rearrange("p (g b) -> p g b", g=GROUPS),
             w_words.bitcast(I32).rearrange("e a p b -> p (e a) b"),
         )
-        for q in range(2, 4):
+        for q in range(EARLY_SCALE_LOADS, QUADRANTS):
             load_scales(q)
 
-        def gather(g4, a, t, pair, lo, hi):
-            s0 = pair * PAIR + lo
-            s1 = pair * PAIR + hi
+        def listed(half, lo, hi):
+            return offsets[:, (half * HALF + lo) // PER_COLUMN : (half * HALF + hi) // PER_COLUMN]
+
+        def gather(planes, a, t, half, lo=0, hi=HALF):
             nc.vector.tensor_tensor(
-                g4[:, t, lo:hi],
-                dy[a][t][:].indirect(offsets[:, s0 // 16 : s1 // 16]),
-                gates[pair][:, lo:hi],
-                MULT,
+                planes[:, t, lo:hi], dy[a][t][:].indirect(listed(half, lo, hi)), gates[half][:, lo:hi], MULT
             )
 
-        def interleave(g4, grouped):
-            for half in range(2):
-                cols = slice(half * C, (half + 1) * C)
+        def interleave(planes, rounded, experts=(0, 1)):
+            for j in experts:
+                cols = slice(j * C, (j + 1) * C)
                 nc.scalar.copy(
-                    grouped.rearrange("p (n t) -> p n t", t=PACK)[:, cols, :].rearrange("p (c i) t -> p c t i", i=4),
-                    g4[:, :, cols].rearrange("p t (c i) -> p c t i", i=4),
+                    rounded.rearrange("p (c t) -> p c t", t=PACK)[:, cols, :].rearrange("p (c i) t -> p c t i", i=LINE),
+                    planes[:, :, cols].rearrange("p t (c i) -> p c t i", i=LINE),
                 )
 
-        def quantise(grouped, a, pair, lo=0, hi=PAIR):
+        def quantise(rounded, a, half, lo=0, hi=HALF):
             nc.vector.quantize_mx(
-                out=codes[a, pair][:, lo:hi].bitcast(FP8X4),
-                scales=planes[a][:, pair * PAIR + lo : pair * PAIR + hi],
-                in_=grouped[:, PACK * lo : PACK * hi],
+                out=codes[a, half][:, lo:hi].bitcast(FP8X4),
+                scales=code_scales[a][:, half * HALF + lo : half * HALF + hi],
+                in_=rounded[:, PACK * lo : PACK * hi],
             )
 
-        def products(pair, kts):
-            ys = []
-            for kt in kts:
-                if (pair, kt) == (0, KT - 1):
-                    y = shared[:, 0:PAIR]
-                else:
-                    y = held.tile([P, PAIR], F32, name=f"y{pair}{kt}")[:]
-                ys.append(y)
-                accs = [psum.tile([P, C], F32, name="acc") for half in range(2)]
-                for a in range(PASSES):
-                    for half in range(2):
-                        e = 2 * pair + half
-                        cols = slice(e * C, (e + 1) * C)
-                        w0 = (e * PASSES + a) * K + P * kt
-                        nc.tensor.matmul_mx(
-                            out=accs[half][:],
-                            lhsT=words[:, 2 * w0 : 2 * (w0 + P)].bitcast(FP4X4),
-                            lhsT_scale=wplanes[:, w0 : w0 + P],
-                            rhs=codes[a, pair][:, half * C : (half + 1) * C].bitcast(FP8X4),
-                            rhs_scale=planes[a][:, cols],
-                            start=(a == 0),
-                            stop=(a == PASSES - 1),
-                        )
-                for half in range(2):
-                    nc.scalar.copy(y[:, half * C : (half + 1) * C], accs[half][:])
-            return ys
+        def products(half, kt, dx):
+            banks = [psum.tile([P, C], F32, name="bank") for j in range(2)]
+            for a in range(PASSES):
+                for j in range(2):
+                    e = 2 * half + j
+                    w0 = (e * PASSES + a) * K + P * kt
+                    nc.tensor.matmul_mx(
+                        out=banks[j][:],
+                        lhsT=words[:, 2 * w0 : 2 * (w0 + P)].bitcast(FP4X4),
+                        lhsT_scale=word_scales[:, w0 : w0 + P],
+                        rhs=codes[a, half][:, j * C : (j + 1) * C].bitcast(FP8X4),
+                        rhs_scale=code_scales[a][:, e * C : (e + 1) * C],
+                        start=(a == 0),
+                        stop=(a == PASSES - 1),
+                    )
+            for j in range(2):
+                nc.scalar.copy(dx[:, j * C : (j + 1) * C], banks[j][:])
+            return dx
 
-        def scatter(ys, pair, kt):
-            nc.vector.tensor_copy(
-                outs[kt][:].indirect(offsets[:, pair * PAIR // 16 : (pair + 1) * PAIR // 16]), ys[kt]
-            )
+        def new_dx(half, kt):
+            return held.tile([P, HALF], F32, name=f"dx{half}{kt}")[:]
 
-        g00 = held.tile([P, PACK, PAIR], F32, name="g00")
-        g01 = held.tile([P, PACK, PAIR], F32, name="g01")
-        g10 = held.tile([P, PACK, PAIR], F32, name="g10", tag="late", align_bytes=64)
-        b00 = held.tile([P, PACK * PAIR], BF16, name="b00", align_bytes=64)
-        b01 = held.tile([P, PACK * PAIR], BF16, name="b01", align_bytes=64)
-        b11 = held.tile([P, PACK * PAIR], BF16, name="b11", align_bytes=64)
+        def scatter(dx, half, kt):
+            nc.vector.tensor_copy(outs[kt][:].indirect(listed(half, 0, HALF)), dx)
 
-        gather(g00, 0, 0, 0, 0, FIRST)
-        gather(g00, 0, 0, 0, FIRST, PAIR)
-        gather(g01, 0, 0, 1, 0, PAIR)
+        planes00 = held.tile([P, PACK, HALF], F32, name="planes00")
+        planes01 = held.tile([P, PACK, HALF], F32, name="planes01")
+        planes10 = held.tile([P, PACK, HALF], F32, name="planes10", tag="planes10_then_codes01", align_bytes=MX_ALIGN)
+        rounded00 = held.tile([P, PACK * HALF], BF16, name="rounded00", align_bytes=MX_ALIGN)
+        rounded01 = held.tile([P, PACK * HALF], BF16, name="rounded01", align_bytes=MX_ALIGN)
+        rounded11 = held.tile([P, PACK * HALF], BF16, name="rounded11", align_bytes=MX_ALIGN)
+
+        gather(planes00, 0, 0, 0, 0, C)
+        gather(planes00, 0, 0, 0, C, HALF)
+        gather(planes01, 0, 0, 1)
         for t in range(1, PACK):
-            gather(g01, 0, t, 1, 0, PAIR)
-            gather(g00, 0, t, 0, 0, PAIR)
-        interleave(g01, b01[:])
-        interleave(g00, b00[:])
-        for t in range(PACK):
-            gather(g10, 1, t, 0, 0, PAIR)
-        shared = held.tile([P, (PACK + 1) * PAIR], F32, name="shared", tag="early", align_bytes=64)
-        g11 = shared[:, 0 : PACK * PAIR].rearrange("p (t c) -> p t c", t=PACK)
-        b10 = shared[:, 3 * PAIR : 5 * PAIR].bitcast(BF16)
-        interleave(g10, b10)
-        quantise(b00[:], 0, 0)
-        for t in range(PACK - 1):
-            gather(g11, 1, t, 1, 0, PAIR)
-        quantise(b10, 1, 0, 0, C)
-        quantise(b10, 1, 0, C, PAIR)
-        codes[0, 1] = held.tile([P, PAIR], U32, name="codes01", tag="late", align_bytes=64)
-        quantise(b01[:], 0, 1)
-        gather(g11, 1, PACK - 1, 1, 0, PAIR)
-        y0 = products(0, (0,))
-        interleave(g11, b11[:])
-        y0 += products(0, (1, 2))
+            gather(planes01, 0, t, 1)
+            gather(planes00, 0, t, 0)
+        interleave(planes01, rounded01[:])
+        interleave(planes00, rounded00[:])
 
-        scatter(y0, 0, 0)
-        quantise(b11[:], 1, 1)
-        y1 = products(1, range(KT))
-        scatter(y0, 0, 1)
-        scatter(y0, 0, 2)
+        for t in range(PACK):
+            gather(planes10, 1, t, 0)
+
+        last = held.tile([P, (PACK + 1) * HALF], F32, name="last", tag="gates0_then_last", align_bytes=MX_ALIGN)
+        planes11 = last[:, HALF : (PACK + 1) * HALF].rearrange("p (t c) -> p t c", t=PACK)
+        rounded10 = last[:, 0 : 2 * HALF].bitcast(BF16)
+        interleave(planes10, rounded10)
+
+        quantise(rounded00[:], 0, 0, 0, C)
+        quantise(rounded00[:], 0, 0, C, HALF)
+        for t in range(1, PACK):
+            gather(planes11, 1, t, 1)
+        quantise(rounded10, 1, 0, 0, C)
+        quantise(rounded10, 1, 0, C, HALF)
+        codes[0, 1] = held.tile([P, HALF], U32, name="codes01", tag="planes10_then_codes01", align_bytes=MX_ALIGN)
+        quantise(rounded01[:], 0, 1)
+        gather(planes11, 1, 0, 1)
+
+        dx00 = products(0, 0, new_dx(0, 0))
+        interleave(planes11, rounded11[:], (0,))
+        dx01 = products(0, 1, new_dx(0, 1))
+        interleave(planes11, rounded11[:], (1,))
+        dx02 = products(0, 2, planes11[:, 0, :])
+
+        scatter(dx00, 0, 0)
+        scatter(dx01, 0, 1)
+        quantise(rounded11[:], 1, 1)
+        dx1 = [products(1, kt, new_dx(1, kt)) for kt in range(KT)]
+        scatter(dx02, 0, 2)
+
         for kt in range(KT):
-            scatter(y1, 1, kt)
+            scatter(dx1[kt], 1, kt)
             rows = slice(kt * P, (kt + 1) * P)
-            nc.sync.dma_start(out[rows, 0:PAIR], outs[kt][:, 0:PAIR])
-            nc.scalar.dma_start(out[rows, PAIR:T], outs[kt][:, PAIR:T])
+            nc.sync.dma_start(out[rows, 0 : T // 2], outs[kt][:, 0 : T // 2])
+            nc.scalar.dma_start(out[rows, T // 2 : T], outs[kt][:, T // 2 : T])

@@ -28,40 +28,45 @@ RUN = C // P
 LINE = 4
 QUADRANTS = 4
 MX_ALIGN = 64
-EARLY_SCALE_LOADS = 1
+SPARE = 8
 
 
 def tile_moe_bdx_lin_none_kernel(tc, dyT, w_words, w_scales, gate, offs, out):
     nc = tc.nc
     with ExitStack() as ctx:
         held = ctx.enter_context(tc.tile_pool(name="held", bufs=1))
+        staged = ctx.enter_context(tc.tile_pool(name="staged", bufs=2))
         psum = ctx.enter_context(tc.psum_pool(name="psum", bufs=8))
 
         offsets = held.tile([P, T // PER_COLUMN], U16, name="offsets")
-        gates = [
-            held.tile([P, HALF], F32, name="gates0", tag="gates0_then_last", align_bytes=MX_ALIGN),
-            held.tile([P, HALF], F32, name="gates1"),
-        ]
-        dy = [[held.tile([P, T], F32, name=f"dy{a}{t}") for t in range(PACK)] for a in range(PASSES)]
+        gates = held.tile([P, T], F32, name="gates")
+        whole = [(0, 1), (0, 2), (0, 3), (1, 1), (1, 2)]
+        dy = {
+            (a, t): held.tile([P, T + SPARE if (a, t) in whole else T], F32, name=f"dy{a}{t}")
+            for a in range(PASSES)
+            for t in range(PACK)
+            if a or t
+        }
+        dy[0, 0] = held.tile([P, 2 * T], F32, name="dy00", tag="dy00_then_dx")
         words = held.tile([P, GROUPS * 2 * K], U8, name="words", align_bytes=MX_ALIGN)
         word_scales = held.tile([P, GROUPS * K], U8, name="word_scales", align_bytes=MX_ALIGN)
         outs = [held.tile([P, T], F32, name=f"outs{kt}") for kt in range(KT)]
-        codes = {
-            quarter: held.tile([P, HALF], U32, name="codes%d%d" % quarter, align_bytes=MX_ALIGN)
-            for quarter in ((0, 0), (1, 0), (1, 1))
-        }
+        codes = [held.tile([P, T], U32, name=f"codes{a}", align_bytes=MX_ALIGN) for a in range(PASSES)]
         code_scales = [held.tile([P, T], U8, name=f"code_scales{a}", align_bytes=MX_ALIGN) for a in range(PASSES)]
+        rounded = {0: held.tile([P, PACK * T], BF16, name="rounded0", align_bytes=MX_ALIGN)}
 
         dy_rows = dyT.rearrange("(a p t) c -> a t p c", a=PASSES, p=P, t=PACK)
 
         nc.vector.memset(word_scales[:].bitcast(I32), 0)
+        nc.vector.memset(dy[0, 0][:, T : 2 * T], 0.0)
+        for at in whole:
+            nc.vector.memset(dy[at][:, T : T + SPARE], 0.0)
 
         gate_cols = held.tile([P, E, 2 * RUN], F32, name="gate_cols")
         gate_row = gate[0, :].rearrange("(e p i) -> p e i", e=E, p=P, i=RUN)
-        nc.sync.dma_start(gate_cols[:, 0 : E // 2, 0:RUN], gate_row[:, 0 : E // 2, :])
+        nc.sync.dma_start(dy[0, 0][:, 0:T], dy_rows[0, 0])
         nc.sync.dma_start(offsets[:], offs)
-        nc.sync.dma_start(dy[0][0][:], dy_rows[0, 0])
-        nc.sync.dma_start(gate_cols[:, E // 2 : E, 0:RUN], gate_row[:, E // 2 : E, :])
+        nc.sync.dma_start(gate_cols[:, :, 0:RUN], gate_row)
 
         identity = held.tile([P, P], F32, name="identity")
         make_identity(nc, identity[:])
@@ -72,125 +77,150 @@ def tile_moe_bdx_lin_none_kernel(tc, dyT, w_words, w_scales, gate, offs, out):
                     spread[:, i * P : (i + 1) * P], gate_cols[:, e, i : i + 1].to_broadcast([P, P]), identity[:]
                 )
             nc.scalar.copy(
-                gates[e // 2][:, (e % 2) * C : (e % 2 + 1) * C].rearrange("m (p i) -> m p i", i=RUN),
+                gates[:, e * C : (e + 1) * C].rearrange("m (p i) -> m p i", i=RUN),
                 spread[:].rearrange("m (i p) -> m p i", i=RUN),
             )
 
-        def load_scales(q):
+        for a, t in whole + [(1, 0), (1, 3)]:
+            nc.sync.dma_start(dy[a, t][:, 0:T], dy_rows[a, t])
+        nc.sync.dma_start(
+            words[:].bitcast(I32).rearrange("p (g b) -> p g b", g=GROUPS),
+            w_words.bitcast(I32).rearrange("e a p b -> p (e a) b"),
+        )
+        for q in range(QUADRANTS):
             nc.sync.dma_start(
                 word_scales[32 * q : 32 * q + 4, :].bitcast(I32).rearrange("p (g k) -> p g k", g=GROUPS),
                 w_scales.bitcast(I32).rearrange("e a f k -> f (e a) k")[4 * q : 4 * q + 4, :, :],
             )
 
-        later_tiles = [(a, t) for a in range(PASSES) for t in range(PACK)][1:]
-        for a, t in later_tiles[:-1]:
-            nc.sync.dma_start(dy[a][t][:], dy_rows[a, t])
-        for q in range(EARLY_SCALE_LOADS):
-            load_scales(q)
-        nc.sync.dma_start(dy[PASSES - 1][PACK - 1][:], dy_rows[PASSES - 1, PACK - 1])
-        nc.sync.dma_start(
-            words[:].bitcast(I32).rearrange("p (g b) -> p g b", g=GROUPS),
-            w_words.bitcast(I32).rearrange("e a p b -> p (e a) b"),
-        )
-        for q in range(EARLY_SCALE_LOADS, QUADRANTS):
-            load_scales(q)
+        def listed(lo, hi):
+            return offsets[:, lo * C // PER_COLUMN : hi * C // PER_COLUMN]
 
-        def listed(half, lo, hi):
-            return offsets[:, (half * HALF + lo) // PER_COLUMN : (half * HALF + hi) // PER_COLUMN]
+        starts = {
+            (0, 0): (0, T, 2 * T, 3 * T),
+            (0, 1): (0, T, 2 * T, 3 * T),
+            (1, 0): (C, C + T, C + 2 * T, C + 3 * T),
+            (1, 1): (-HALF, C + T, C + 2 * T, 4 * T),
+        }
+        planes = [
+            held.tile([P, PACK * T], F32, name="planes0", tag="planes0_then_rounded1", align_bytes=MX_ALIGN),
+            held.tile([P, 22 * C], F32, name="planes1"),
+        ]
 
-        def gather(planes, a, t, half, lo=0, hi=HALF):
+        def gather(a, t, lo, hi):
+            at = starts[a, lo // 2][t]
             nc.vector.tensor_tensor(
-                planes[:, t, lo:hi], dy[a][t][:].indirect(listed(half, lo, hi)), gates[half][:, lo:hi], MULT
+                planes[a][:, at + lo * C : at + hi * C],
+                dy[a, t][:].indirect(listed(lo, hi)),
+                gates[:, lo * C : hi * C],
+                MULT,
             )
 
-        def interleave(planes, rounded, experts=(0, 1)):
-            for j in experts:
-                cols = slice(j * C, (j + 1) * C)
-                nc.scalar.copy(
-                    rounded.rearrange("p (c t) -> p c t", t=PACK)[:, cols, :].rearrange("p (c i) t -> p c t i", i=LINE),
-                    planes[:, :, cols].rearrange("p t (c i) -> p c t i", i=LINE),
-                )
+        def interleave(a, e):
+            at = starts[a, e // 2]
+            first, single, pair = at[0] // C + e, (at[1] - at[0]) // C, (at[2] - at[0]) // C
+            pairs = planes[a][:, 0 : 2 * pair * C].rearrange("p (u b s) -> p u b s", u=2, s=C)
+            src = pairs[:, :, first : first + single + 1 : single, :]
+            nc.scalar.copy(
+                rounded[a][:, PACK * e * C : PACK * (e + 1) * C].rearrange("p (c i u v) -> p c u v i", i=LINE, u=2, v=2),
+                src.rearrange("p u v (c i) -> p c u v i", i=LINE),
+            )
 
-        def quantise(rounded, a, half, lo=0, hi=HALF):
+        def quantise(a, lo, hi):
             nc.vector.quantize_mx(
-                out=codes[a, half][:, lo:hi].bitcast(FP8X4),
-                scales=code_scales[a][:, half * HALF + lo : half * HALF + hi],
-                in_=rounded[:, PACK * lo : PACK * hi],
+                out=codes[a][:, lo * C : hi * C].bitcast(FP8X4),
+                scales=code_scales[a][:, lo * C : hi * C],
+                in_=rounded[a][:, PACK * lo * C : PACK * hi * C],
             )
 
-        def products(half, kt, dx):
-            banks = [psum.tile([P, C], F32, name="bank") for j in range(2)]
+        def product(e, kt, dx):
+            bank = psum.tile([P, C], F32, name="bank")
             for a in range(PASSES):
-                for j in range(2):
-                    e = 2 * half + j
-                    w0 = (e * PASSES + a) * K + P * kt
-                    nc.tensor.matmul_mx(
-                        out=banks[j][:],
-                        lhsT=words[:, 2 * w0 : 2 * (w0 + P)].bitcast(FP4X4),
-                        lhsT_scale=word_scales[:, w0 : w0 + P],
-                        rhs=codes[a, half][:, j * C : (j + 1) * C].bitcast(FP8X4),
-                        rhs_scale=code_scales[a][:, e * C : (e + 1) * C],
-                        start=(a == 0),
-                        stop=(a == PASSES - 1),
-                    )
-            for j in range(2):
-                nc.scalar.copy(dx[:, j * C : (j + 1) * C], banks[j][:])
-            return dx
+                w0 = (e * PASSES + a) * K + P * kt
+                nc.tensor.matmul_mx(
+                    out=bank[:],
+                    lhsT=words[:, 2 * w0 : 2 * (w0 + P)].bitcast(FP4X4),
+                    lhsT_scale=word_scales[:, w0 : w0 + P],
+                    rhs=codes[a][:, e * C : (e + 1) * C].bitcast(FP8X4),
+                    rhs_scale=code_scales[a][:, e * C : (e + 1) * C],
+                    start=(a == 0),
+                    stop=(a == PASSES - 1),
+                )
+            nc.scalar.copy(dx, bank[:])
 
-        def new_dx(half, kt):
-            return held.tile([P, HALF], F32, name=f"dx{half}{kt}")[:]
+        def scatter(dx, kt, lo, hi):
+            nc.vector.tensor_copy(outs[kt][:].indirect(listed(lo, hi)), dx)
 
-        def scatter(dx, half, kt):
-            nc.vector.tensor_copy(outs[kt][:].indirect(listed(half, 0, HALF)), dx)
-
-        planes00 = held.tile([P, PACK, HALF], F32, name="planes00")
-        planes01 = held.tile([P, PACK, HALF], F32, name="planes01")
-        planes10 = held.tile([P, PACK, HALF], F32, name="planes10", tag="planes10_then_codes01", align_bytes=MX_ALIGN)
-        rounded00 = held.tile([P, PACK * HALF], BF16, name="rounded00", align_bytes=MX_ALIGN)
-        rounded01 = held.tile([P, PACK * HALF], BF16, name="rounded01", align_bytes=MX_ALIGN)
-        rounded11 = held.tile([P, PACK * HALF], BF16, name="rounded11", align_bytes=MX_ALIGN)
-
-        gather(planes00, 0, 0, 0, 0, C)
-        gather(planes00, 0, 0, 0, C, HALF)
-        gather(planes01, 0, 0, 1)
+        nc.vector.tensor_copy(planes[0][:, 0:T], dy[0, 0][:].indirect(offsets[:]))
+        for e in range(E):
+            by_run = planes[0][:, e * C : (e + 1) * C].rearrange("m (p i) -> m i p", i=RUN)
+            turned = psum.tile([P, C], F32, name="bank")
+            for i in range(RUN):
+                nc.tensor.transpose(turned[:, i * P : (i + 1) * P], by_run[:, i, :], identity[:])
+            gated = staged.tile([P, C], F32, name="gated")
+            for i in range(RUN):
+                nc.scalar.activation(
+                    gated[:, i * P : (i + 1) * P],
+                    turned[:, i * P : (i + 1) * P],
+                    mybir.ActivationFunctionType.Copy,
+                    scale=gate_cols[:, e, i : i + 1],
+                )
+            back = psum.tile([P, C], F32, name="bank")
+            for i in range(RUN):
+                nc.tensor.transpose(back[:, i * P : (i + 1) * P], gated[:, i * P : (i + 1) * P], identity[:])
+            nc.scalar.copy(
+                planes[0][:, e * C : (e + 1) * C].rearrange("m (p i) -> m p i", i=RUN),
+                back[:].rearrange("m (i p) -> m p i", i=RUN),
+            )
         for t in range(1, PACK):
-            gather(planes01, 0, t, 1)
-            gather(planes00, 0, t, 0)
-        interleave(planes01, rounded01[:])
-        interleave(planes00, rounded00[:])
+            gather(0, t, 0, E)
+        for e in range(E):
+            interleave(0, e)
+        rounded[1] = held.tile([P, PACK * T], BF16, name="rounded1", tag="planes0_then_rounded1", align_bytes=MX_ALIGN)
+        gather(1, 1, 0, E)
+        gather(1, 2, 0, E)
+        gather(1, 0, 0, 2)
+        quantise(0, 0, 2)
+        gather(1, 3, 0, 2)
+        gather(1, 3, 2, E)
+        interleave(1, 0)
+        quantise(0, 2, 4)
+        quantise(1, 0, 1)
+        gather(1, 0, 2, E)
+        interleave(1, 1)
+        quantise(1, 1, 2)
 
-        for t in range(PACK):
-            gather(planes10, 1, t, 0)
+        dx = held.tile([P, 2 * T], F32, name="dx", tag="dy00_then_dx")
 
-        last = held.tile([P, (PACK + 1) * HALF], F32, name="last", tag="gates0_then_last", align_bytes=MX_ALIGN)
-        planes11 = last[:, HALF : (PACK + 1) * HALF].rearrange("p (t c) -> p t c", t=PACK)
-        rounded10 = last[:, 0 : 2 * HALF].bitcast(BF16)
-        interleave(planes10, rounded10)
+        def dx_of(kt, lo, hi):
+            if kt == KT - 1 and hi <= 2:
+                return planes[1][:, C + T + HALF + lo * C : C + T + HALF + hi * C]
+            if kt == 0 and hi <= 1:
+                return planes[1][:, 15 * C : 16 * C]
+            if kt == 1 and hi <= 2:
+                return planes[1][:, (16 + lo) * C : (16 + hi) * C]
+            return dx[:, kt * HALF + lo * C : kt * HALF + hi * C]
 
-        quantise(rounded00[:], 0, 0, 0, C)
-        quantise(rounded00[:], 0, 0, C, HALF)
-        for t in range(1, PACK):
-            gather(planes11, 1, t, 1)
-        quantise(rounded10, 1, 0, 0, C)
-        quantise(rounded10, 1, 0, C, HALF)
-        codes[0, 1] = held.tile([P, HALF], U32, name="codes01", tag="planes10_then_codes01", align_bytes=MX_ALIGN)
-        quantise(rounded01[:], 0, 1)
-        gather(planes11, 1, 0, 1)
+        product(0, 0, dx_of(0, 0, 1))
+        product(0, 1, dx_of(1, 0, 1))
+        product(1, 1, dx_of(1, 1, 2))
+        interleave(1, 2)
+        interleave(1, 3)
+        product(0, 2, dx_of(2, 0, 1))
+        product(1, 2, dx_of(2, 1, 2))
+        product(1, 0, dx_of(0, 1, 2))
 
-        dx00 = products(0, 0, new_dx(0, 0))
-        interleave(planes11, rounded11[:], (0,))
-        dx01 = products(0, 1, new_dx(0, 1))
-        interleave(planes11, rounded11[:], (1,))
-        dx02 = products(0, 2, planes11[:, 0, :])
-
-        scatter(dx00, 0, 0)
-        scatter(dx01, 0, 1)
-        quantise(rounded11[:], 1, 1)
-        dx1 = [products(1, kt, new_dx(1, kt)) for kt in range(KT)]
-        scatter(dx02, 0, 2)
+        scatter(dx_of(0, 0, 1), 0, 0, 1)
+        scatter(dx_of(1, 0, 2), 1, 0, 2)
+        quantise(1, 2, 4)
+        for kt in range(KT):
+            for e in (2, 3):
+                product(e, kt, dx_of(kt, e, e + 1))
+        scatter(dx_of(2, 0, 2), 2, 0, 2)
 
         for kt in range(KT):
-            scatter(dx1[kt], 1, kt)
+            lo = 2 if kt else 1
+            scatter(dx_of(kt, lo, E), kt, lo, E)
             rows = slice(kt * P, (kt + 1) * P)
             nc.sync.dma_start(out[rows, 0 : T // 2], outs[kt][:, 0 : T // 2])
             nc.scalar.dma_start(out[rows, T // 2 : T], outs[kt][:, T // 2 : T])

@@ -24,7 +24,7 @@ KT = K // P
 GROUPS = E * PASSES
 HALF = 2 * C
 PER_COLUMN = 16
-RUN = C // P
+RUN = T // P
 LINE = 4
 QUADRANTS = 4
 MX_ALIGN = 64
@@ -35,7 +35,6 @@ def tile_moe_bdx_lin_none_kernel(tc, dyT, w_words, w_scales, gate, offs, out):
     nc = tc.nc
     with ExitStack() as ctx:
         held = ctx.enter_context(tc.tile_pool(name="held", bufs=1))
-        staged = ctx.enter_context(tc.tile_pool(name="staged", bufs=2))
         psum = ctx.enter_context(tc.psum_pool(name="psum", bufs=8))
 
         offsets = held.tile([P, T // PER_COLUMN], U16, name="offsets")
@@ -62,24 +61,25 @@ def tile_moe_bdx_lin_none_kernel(tc, dyT, w_words, w_scales, gate, offs, out):
         for at in whole:
             nc.vector.memset(dy[at][:, T : T + SPARE], 0.0)
 
-        gate_cols = held.tile([P, E, 2 * RUN], F32, name="gate_cols")
-        gate_row = gate[0, :].rearrange("(e p i) -> p e i", e=E, p=P, i=RUN)
+        gate_cols = held.tile([P, RUN], F32, name="gate_cols")
         nc.sync.dma_start(dy[0, 0][:, 0:T], dy_rows[0, 0])
         nc.sync.dma_start(offsets[:], offs)
-        nc.sync.dma_start(gate_cols[:, :, 0:RUN], gate_row)
+        nc.scalar.dma_start(gate_cols[:], gate[0, :].rearrange("(p i) -> p i", i=RUN))
 
         identity = held.tile([P, P], F32, name="identity")
         make_identity(nc, identity[:])
-        for e in range(E):
-            spread = psum.tile([P, C], F32, name="bank")
-            for i in range(RUN):
-                nc.tensor.transpose(
-                    spread[:, i * P : (i + 1) * P], gate_cols[:, e, i : i + 1].to_broadcast([P, P]), identity[:]
+
+        def unturn(dst, src):
+            for g in range(RUN // LINE):
+                bank = psum.tile([P, C], F32, name="bank")
+                for i in range(LINE):
+                    nc.tensor.transpose(bank[:, i * P : (i + 1) * P], src(LINE * g + i), identity[:])
+                nc.scalar.copy(
+                    dst.rearrange("m (p g i) -> m g p i", g=RUN // LINE, i=LINE)[:, g, :, :],
+                    bank[:].rearrange("m (i p) -> m p i", i=LINE),
                 )
-            nc.scalar.copy(
-                gates[:, e * C : (e + 1) * C].rearrange("m (p i) -> m p i", i=RUN),
-                spread[:].rearrange("m (i p) -> m p i", i=RUN),
-            )
+
+        unturn(gates[:], lambda i: gate_cols[:, i : i + 1].to_broadcast([P, P]))
 
         for a, t in whole + [(1, 0), (1, 3)]:
             nc.sync.dma_start(dy[a, t][:, 0:T], dy_rows[a, t])
@@ -152,26 +152,20 @@ def tile_moe_bdx_lin_none_kernel(tc, dyT, w_words, w_scales, gate, offs, out):
             nc.vector.tensor_copy(outs[kt][:].indirect(listed(lo, hi)), dx)
 
         nc.vector.tensor_copy(planes[0][:, 0:T], dy[0, 0][:].indirect(offsets[:]))
-        for e in range(E):
-            by_run = planes[0][:, e * C : (e + 1) * C].rearrange("m (p i) -> m i p", i=RUN)
+        by_run = planes[0][:, 0:T].rearrange("m (p i) -> m i p", i=RUN)
+        gated = held.tile([P, T], F32, name="gated")
+        for g in range(RUN // LINE):
             turned = psum.tile([P, C], F32, name="bank")
-            for i in range(RUN):
-                nc.tensor.transpose(turned[:, i * P : (i + 1) * P], by_run[:, i, :], identity[:])
-            gated = staged.tile([P, C], F32, name="gated")
-            for i in range(RUN):
+            for i in range(LINE):
+                nc.tensor.transpose(turned[:, i * P : (i + 1) * P], by_run[:, LINE * g + i, :], identity[:])
+            for i in range(LINE * g, LINE * (g + 1)):
                 nc.scalar.activation(
                     gated[:, i * P : (i + 1) * P],
-                    turned[:, i * P : (i + 1) * P],
+                    turned[:, (i % LINE) * P : (i % LINE + 1) * P],
                     mybir.ActivationFunctionType.Copy,
-                    scale=gate_cols[:, e, i : i + 1],
+                    scale=gate_cols[:, i : i + 1],
                 )
-            back = psum.tile([P, C], F32, name="bank")
-            for i in range(RUN):
-                nc.tensor.transpose(back[:, i * P : (i + 1) * P], gated[:, i * P : (i + 1) * P], identity[:])
-            nc.scalar.copy(
-                planes[0][:, e * C : (e + 1) * C].rearrange("m (p i) -> m p i", i=RUN),
-                back[:].rearrange("m (i p) -> m p i", i=RUN),
-            )
+        unturn(planes[0][:, 0:T], lambda i: gated[:, i * P : (i + 1) * P])
         for t in range(1, PACK):
             gather(0, t, 0, E)
         for e in range(E):

@@ -16,6 +16,7 @@ U8 = mybir.dt.uint8
 FP8X4 = mybir.dt.float8_e5m2_x4
 FP4X4 = mybir.dt.float4_e2m1fn_x4
 MULT = mybir.AluOpType.mult
+ADD = mybir.AluOpType.add
 
 P = 128
 PACK = 4
@@ -24,11 +25,15 @@ KT = K // P
 GROUPS = E * PASSES
 HALF = 2 * C
 PER_COLUMN = 16
-RUN = T // P
+RUN = HALF // P
 LINE = 4
 QUADRANTS = 4
 MX_ALIGN = 64
-SPARE = 8
+SHORT_SCATTER = 64
+SHORT_GATHER = 128
+STEPS = KT * HALF // SHORT_SCATTER
+FILL = 3 * SHORT_GATHER
+LEAD = 2
 
 
 def tile_moe_bdx_lin_none_kernel(tc, dyT, w_words, w_scales, gate, offs, out):
@@ -38,51 +43,32 @@ def tile_moe_bdx_lin_none_kernel(tc, dyT, w_words, w_scales, gate, offs, out):
         psum = ctx.enter_context(tc.psum_pool(name="psum", bufs=8))
 
         offsets = held.tile([P, T // PER_COLUMN], U16, name="offsets")
-        gates = held.tile([P, T], F32, name="gates")
-        whole = [(0, 1), (0, 2), (0, 3), (1, 1), (1, 2)]
-        dy = {
-            (a, t): held.tile([P, T + SPARE if (a, t) in whole else T], F32, name=f"dy{a}{t}")
-            for a in range(PASSES)
-            for t in range(PACK)
-            if a or t
-        }
-        dy[0, 0] = held.tile([P, 2 * T], F32, name="dy00", tag="dy00_then_dx")
+        dy = {(a, t): held.tile([P, T], F32, name=f"dy{a}{t}") for a in range(PASSES) for t in range(PACK)}
         words = held.tile([P, GROUPS * 2 * K], U8, name="words", align_bytes=MX_ALIGN)
         word_scales = held.tile([P, GROUPS * K], U8, name="word_scales", align_bytes=MX_ALIGN)
         outs = [held.tile([P, T], F32, name=f"outs{kt}") for kt in range(KT)]
-        codes = [held.tile([P, T], U32, name=f"codes{a}", align_bytes=MX_ALIGN) for a in range(PASSES)]
+        zeros = held.tile([P, SHORT_SCATTER], F32, name="zeros")
+        gates = [
+            held.tile([P, HALF], F32, name="gates0", tag="gates0_then_codes", align_bytes=MX_ALIGN),
+            held.tile([P, HALF], F32, name="gates1"),
+        ]
+        gate_cols = held.tile([P, 2 * RUN], F32, name="gate_cols")
+        identity = held.tile([P, P], F32, name="identity")
         code_scales = [held.tile([P, T], U8, name=f"code_scales{a}", align_bytes=MX_ALIGN) for a in range(PASSES)]
-        rounded = {0: held.tile([P, PACK * T], BF16, name="rounded0", align_bytes=MX_ALIGN)}
+        rounded = [held.tile([P, PACK * T], BF16, name=f"rounded{a}", align_bytes=MX_ALIGN) for a in range(PASSES)]
 
         dy_rows = dyT.rearrange("(a p t) c -> a t p c", a=PASSES, p=P, t=PACK)
+        landing = [(0, 0), (0, 1), (0, 2), (0, 3), (1, 1), (1, 2), (1, 3), (1, 0)]
 
         nc.vector.memset(word_scales[:].bitcast(I32), 0)
-        nc.vector.memset(dy[0, 0][:, T : 2 * T], 0.0)
-        for at in whole:
-            nc.vector.memset(dy[at][:, T : T + SPARE], 0.0)
-
-        gate_cols = held.tile([P, RUN], F32, name="gate_cols")
-        nc.sync.dma_start(dy[0, 0][:, 0:T], dy_rows[0, 0])
+        nc.vector.memset(zeros[:], 0.0)
+        nc.sync.dma_start(
+            gate_cols[:].rearrange("p (h i) -> p h i", h=2), gate[0, :].rearrange("(h p i) -> p h i", h=2, i=RUN)
+        )
+        nc.sync.dma_start(dy[landing[0]][:], dy_rows[landing[0]])
         nc.sync.dma_start(offsets[:], offs)
-        nc.scalar.dma_start(gate_cols[:], gate[0, :].rearrange("(p i) -> p i", i=RUN))
-
-        identity = held.tile([P, P], F32, name="identity")
-        make_identity(nc, identity[:])
-
-        def unturn(dst, src):
-            for g in range(RUN // LINE):
-                bank = psum.tile([P, C], F32, name="bank")
-                for i in range(LINE):
-                    nc.tensor.transpose(bank[:, i * P : (i + 1) * P], src(LINE * g + i), identity[:])
-                nc.scalar.copy(
-                    dst.rearrange("m (p g i) -> m g p i", g=RUN // LINE, i=LINE)[:, g, :, :],
-                    bank[:].rearrange("m (i p) -> m p i", i=LINE),
-                )
-
-        unturn(gates[:], lambda i: gate_cols[:, i : i + 1].to_broadcast([P, P]))
-
-        for a, t in whole + [(1, 0), (1, 3)]:
-            nc.sync.dma_start(dy[a, t][:, 0:T], dy_rows[a, t])
+        for at in landing[1:]:
+            nc.sync.dma_start(dy[at][:], dy_rows[at])
         nc.sync.dma_start(
             words[:].bitcast(I32).rearrange("p (g b) -> p g b", g=GROUPS),
             w_words.bitcast(I32).rearrange("e a p b -> p (e a) b"),
@@ -93,47 +79,45 @@ def tile_moe_bdx_lin_none_kernel(tc, dyT, w_words, w_scales, gate, offs, out):
                 w_scales.bitcast(I32).rearrange("e a f k -> f (e a) k")[4 * q : 4 * q + 4, :, :],
             )
 
-        def listed(lo, hi):
-            return offsets[:, lo * C // PER_COLUMN : hi * C // PER_COLUMN]
+        make_identity(nc, identity[:])
+        for h in range(2):
+            for g in range(RUN // LINE):
+                bank = psum.tile([P, C], F32, name="bank")
+                for i in range(LINE):
+                    col = h * RUN + g * LINE + i
+                    nc.tensor.transpose(
+                        bank[:, i * P : (i + 1) * P], gate_cols[:, col : col + 1].to_broadcast([P, P]), identity[:]
+                    )
+                nc.scalar.copy(
+                    gates[h][:].rearrange("m (p g i) -> m g p i", g=RUN // LINE, i=LINE)[:, g, :, :],
+                    bank[:].rearrange("m (i p) -> m p i", i=LINE),
+                )
 
-        starts = {
-            (0, 0): (0, T, 2 * T, 3 * T),
-            (0, 1): (0, T, 2 * T, 3 * T),
-            (1, 0): (C, C + T, C + 2 * T, C + 3 * T),
-            (1, 1): (-HALF, C + T, C + 2 * T, 4 * T),
-        }
-        planes = [
-            held.tile([P, PACK * T], F32, name="planes0", tag="planes0_then_rounded1", align_bytes=MX_ALIGN),
-            held.tile([P, 22 * C], F32, name="planes1"),
-        ]
+        def listed(lo, n):
+            return offsets[:, lo // PER_COLUMN : (lo + n) // PER_COLUMN]
 
-        def gather(a, t, lo, hi):
-            at = starts[a, lo // 2][t]
+        def gather(dst, a, t, lo, n):
+            h = lo // HALF
             nc.vector.tensor_tensor(
-                planes[a][:, at + lo * C : at + hi * C],
-                dy[a, t][:].indirect(listed(lo, hi)),
-                gates[:, lo * C : hi * C],
-                MULT,
+                dst, dy[a, t][:].indirect(listed(lo, n)), gates[h][:, lo - h * HALF : lo - h * HALF + n], MULT
             )
 
-        def interleave(a, e):
-            at = starts[a, e // 2]
-            first, single, pair = at[0] // C + e, (at[1] - at[0]) // C, (at[2] - at[0]) // C
-            pairs = planes[a][:, 0 : 2 * pair * C].rearrange("p (u b s) -> p u b s", u=2, s=C)
-            src = pairs[:, :, first : first + single + 1 : single, :]
+        def interleave(src, a, lo, n):
             nc.scalar.copy(
-                rounded[a][:, PACK * e * C : PACK * (e + 1) * C].rearrange("p (c i u v) -> p c u v i", i=LINE, u=2, v=2),
-                src.rearrange("p u v (c i) -> p c u v i", i=LINE),
+                rounded[a][:, PACK * lo : PACK * (lo + n)].rearrange("p (c i t) -> p c t i", i=LINE, t=PACK),
+                src.rearrange("p t (c i) -> p c t i", i=LINE),
             )
+
+        codes = {}
 
         def quantise(a, lo, hi):
             nc.vector.quantize_mx(
-                out=codes[a][:, lo * C : hi * C].bitcast(FP8X4),
+                out=codes[a, lo // 2][:, (lo % 2) * C : (lo % 2 + hi - lo) * C].bitcast(FP8X4),
                 scales=code_scales[a][:, lo * C : hi * C],
                 in_=rounded[a][:, PACK * lo * C : PACK * hi * C],
             )
 
-        def product(e, kt, dx):
+        def product(e, kt):
             bank = psum.tile([P, C], F32, name="bank")
             for a in range(PASSES):
                 w0 = (e * PASSES + a) * K + P * kt
@@ -141,80 +125,112 @@ def tile_moe_bdx_lin_none_kernel(tc, dyT, w_words, w_scales, gate, offs, out):
                     out=bank[:],
                     lhsT=words[:, 2 * w0 : 2 * (w0 + P)].bitcast(FP4X4),
                     lhsT_scale=word_scales[:, w0 : w0 + P],
-                    rhs=codes[a][:, e * C : (e + 1) * C].bitcast(FP8X4),
+                    rhs=codes[a, e // 2][:, (e % 2) * C : (e % 2 + 1) * C].bitcast(FP8X4),
                     rhs_scale=code_scales[a][:, e * C : (e + 1) * C],
                     start=(a == 0),
                     stop=(a == PASSES - 1),
                 )
-            nc.scalar.copy(dx, bank[:])
+            return bank
 
-        def scatter(dx, kt, lo, hi):
-            nc.vector.tensor_copy(outs[kt][:].indirect(listed(lo, hi)), dx)
+        def by_plane(ap):
+            return ap.rearrange("p (t s) -> p t s", t=PACK)
 
-        nc.vector.tensor_copy(planes[0][:, 0:T], dy[0, 0][:].indirect(offsets[:]))
-        by_run = planes[0][:, 0:T].rearrange("m (p i) -> m i p", i=RUN)
-        gated = held.tile([P, T], F32, name="gated")
-        for g in range(RUN // LINE):
-            turned = psum.tile([P, C], F32, name="bank")
-            for i in range(LINE):
-                nc.tensor.transpose(turned[:, i * P : (i + 1) * P], by_run[:, LINE * g + i, :], identity[:])
-            for i in range(LINE * g, LINE * (g + 1)):
-                nc.scalar.activation(
-                    gated[:, i * P : (i + 1) * P],
-                    turned[:, (i % LINE) * P : (i % LINE + 1) * P],
-                    mybir.ActivationFunctionType.Copy,
-                    scale=gate_cols[:, i : i + 1],
-                )
-        unturn(planes[0][:, 0:T], lambda i: gated[:, i * P : (i + 1) * P])
-        for t in range(1, PACK):
-            gather(0, t, 0, E)
-        for e in range(E):
-            interleave(0, e)
-        rounded[1] = held.tile([P, PACK * T], BF16, name="rounded1", tag="planes0_then_rounded1", align_bytes=MX_ALIGN)
-        gather(1, 1, 0, E)
-        gather(1, 2, 0, E)
-        gather(1, 0, 0, 2)
+        first0 = held.tile([P, PACK * HALF], F32, name="first0")
+        first1 = [
+            held.tile([P, PACK * C], F32, name="first10", tag="first10_then_fill"),
+            held.tile([P, PACK * C], F32, name="first11"),
+        ]
+        woven = held.tile([P, C + STEPS * SHORT_GATHER], F32, name="woven")
+        for t in range(PACK):
+            gather(first0[:, t * HALF : (t + 1) * HALF], 0, t, 0, HALF)
+        for e in range(2):
+            interleave(by_plane(first0[:])[:, :, e * C : (e + 1) * C], 0, e * C, C)
+        for t in [at[1] for at in landing[PACK:]]:
+            for e in range(2):
+                gather(first1[e][:, t * C : (t + 1) * C], 1, t, e * C, C)
+        gather(woven[:, 0:C], 1, 0, 2 * C, C)
+        interleave(by_plane(first1[0][:]), 1, 0, C)
+
+        codes[0, 0] = held.tile([P, HALF], U32, name="codes00", tag="gates0_then_codes", align_bytes=MX_ALIGN)
+        for at in [(1, 0), (0, 1), (1, 1)]:
+            codes[at] = held.tile([P, HALF], U32, name=f"codes{at[0]}{at[1]}", align_bytes=MX_ALIGN)
         quantise(0, 0, 2)
-        gather(1, 3, 0, 2)
-        gather(1, 3, 2, E)
-        interleave(1, 0)
-        quantise(0, 2, 4)
         quantise(1, 0, 1)
-        gather(1, 0, 2, E)
-        interleave(1, 1)
-        quantise(1, 1, 2)
+        fill = held.tile([P, PACK * FILL], F32, name="fill", tag="first10_then_fill")
+        for t in range(PACK):
+            gather(fill[:, t * FILL : (t + 1) * FILL], 0, t, 2 * C, FILL)
 
-        dx = held.tile([P, 2 * T], F32, name="dx", tag="dy00_then_dx")
+        def first_products(e):
+            span = KT * C // SHORT_SCATTER * SHORT_GATHER
+            pieces = woven[:, C + e * span : C + (e + 1) * span].rearrange("p (g k c) -> p g k c", k=KT, c=SHORT_GATHER)
+            for kt in range(KT):
+                bank = product(e, kt)
+                nc.scalar.copy(pieces[:, :, kt, 0:SHORT_SCATTER], bank[:].rearrange("p (g c) -> p g c", c=SHORT_SCATTER))
 
-        def dx_of(kt, lo, hi):
-            if kt == KT - 1 and hi <= 2:
-                return planes[1][:, C + T + HALF + lo * C : C + T + HALF + hi * C]
-            if kt == 0 and hi <= 1:
-                return planes[1][:, 15 * C : 16 * C]
-            if kt == 1 and hi <= 2:
-                return planes[1][:, (16 + lo) * C : (16 + hi) * C]
-            return dx[:, kt * HALF + lo * C : kt * HALF + hi * C]
+        first_products(0)
+        for lo in range(0, C, P):
+            interleave(by_plane(first1[1][:])[:, :, lo : lo + P], 1, C + lo, P)
+        interleave(by_plane(fill[:]), 0, 2 * C, FILL)
 
-        product(0, 0, dx_of(0, 0, 1))
-        product(0, 1, dx_of(1, 0, 1))
-        product(1, 1, dx_of(1, 1, 2))
-        interleave(1, 2)
-        interleave(1, 3)
-        product(0, 2, dx_of(2, 0, 1))
-        product(1, 2, dx_of(2, 1, 2))
-        product(1, 0, dx_of(0, 1, 2))
+        rest = (
+            [(1, t, 2 * C + lo) for t in range(1, PACK) for lo in range(0, C, SHORT_GATHER)]
+            + [(0, t, 2 * C + FILL) for t in range(PACK)]
+            + [(a, t, 3 * C + lo) for a in range(PASSES) for t in range(PACK) for lo in range(0, C, SHORT_GATHER)]
+        )
+        block = PACK * C
+        last = held.tile([P, 5 * C], F32, name="last")
 
-        scatter(dx_of(0, 0, 1), 0, 0, 1)
-        scatter(dx_of(1, 0, 2), 1, 0, 2)
-        quantise(1, 2, 4)
+        def woven_scatter(j):
+            at = C + j * SHORT_GATHER
+            nc.vector.tensor_tensor(
+                outs[j % KT][:].indirect(listed(j // KT * SHORT_SCATTER, SHORT_SCATTER)),
+                woven[:, at : at + SHORT_SCATTER],
+                zeros[:],
+                ADD,
+            )
+
+        def woven_gather(j):
+            at = C + j * SHORT_GATHER
+            gather(woven[:, at : at + SHORT_GATHER], *rest[j], SHORT_GATHER)
+
+        for j in range(STEPS + LEAD):
+            if j < STEPS:
+                woven_scatter(j)
+            if j >= LEAD:
+                woven_gather(j - LEAD)
+            done = j - LEAD + 1
+            if done == 4:
+                quantise(1, 1, 2)
+                first_products(1)
+            if done == 12:
+                interleave(by_plane(woven[:, 0:block]), 1, 2 * C, C)
+            if done == 16:
+                interleave(by_plane(woven[:, block : block + C]), 0, 2 * C + FILL, C - FILL)
+            if done == 24:
+                quantise(1, 2, 3)
+            if done == 28:
+                quantise(0, 2, 3)
+                for kt in range(2):
+                    nc.scalar.copy(last[:, kt * C : (kt + 1) * C], product(2, kt)[:])
+            if done == 32:
+                interleave(by_plane(woven[:, block + C : 2 * block + C]), 0, 3 * C, C)
+            if done == 42:
+                quantise(0, 3, 4)
+        interleave(by_plane(woven[:, 2 * block + C : 3 * block + C]), 1, 3 * C, C)
+
+        def scatter(src, kt, e):
+            nc.vector.tensor_copy(outs[kt][:].indirect(listed(e * C, C)), src)
+
+        late = woven[:, 2 * block + C : 2 * block + 2 * C]
+        nc.scalar.copy(late, product(2, 2)[:])
+        scatter(last[:, 0:C], 0, 2)
+        scatter(last[:, C : 2 * C], 1, 2)
+        quantise(1, 3, 4)
         for kt in range(KT):
-            for e in (2, 3):
-                product(e, kt, dx_of(kt, e, e + 1))
-        scatter(dx_of(2, 0, 2), 2, 0, 2)
-
+            nc.scalar.copy(last[:, (2 + kt) * C : (3 + kt) * C], product(3, kt)[:])
+        scatter(late, 2, 2)
         for kt in range(KT):
-            lo = 2 if kt else 1
-            scatter(dx_of(kt, lo, E), kt, lo, E)
+            scatter(last[:, (2 + kt) * C : (3 + kt) * C], kt, 3)
             rows = slice(kt * P, (kt + 1) * P)
             nc.sync.dma_start(out[rows, 0 : T // 2], outs[kt][:, 0 : T // 2])
             nc.scalar.dma_start(out[rows, T // 2 : T], outs[kt][:, T // 2 : T])

@@ -29,10 +29,10 @@ RUN = HALF // P
 LINE = 4
 QUADRANTS = 4
 MX_ALIGN = 64
-SHORT_SCATTER = 64
-SHORT_GATHER = 128
-STEPS = KT * HALF // SHORT_SCATTER
-FILL = 3 * SHORT_GATHER
+SHORT = 64
+REGION = 128
+UNITS = (128, 96, 96, 96, 96)
+LATE = 128
 LEAD = 2
 
 
@@ -47,18 +47,15 @@ def tile_moe_bdx_lin_none_kernel(tc, dyT, w_words, w_scales, gate, offs, out):
         words = held.tile([P, GROUPS * 2 * K], U8, name="words", align_bytes=MX_ALIGN)
         word_scales = held.tile([P, GROUPS * K], U8, name="word_scales", align_bytes=MX_ALIGN)
         outs = [held.tile([P, T], F32, name=f"outs{kt}") for kt in range(KT)]
-        zeros = held.tile([P, SHORT_SCATTER], F32, name="zeros")
-        gates = [
-            held.tile([P, HALF], F32, name="gates0", tag="gates0_then_codes", align_bytes=MX_ALIGN),
-            held.tile([P, HALF], F32, name="gates1"),
-        ]
-        gate_cols = held.tile([P, 2 * RUN], F32, name="gate_cols")
+        zeros = held.tile([P, LATE], F32, name="zeros")
+        gates = [held.tile([P, C], F32, name=f"gates{e}", tag=f"gates{e}", align_bytes=MX_ALIGN) for e in range(E)]
+        gate_cols = held.tile([P, E * LINE], F32, name="gate_cols")
         identity = held.tile([P, P], F32, name="identity")
         code_scales = [held.tile([P, T], U8, name=f"code_scales{a}", align_bytes=MX_ALIGN) for a in range(PASSES)]
         rounded = [held.tile([P, PACK * T], BF16, name=f"rounded{a}", align_bytes=MX_ALIGN) for a in range(PASSES)]
 
         dy_rows = dyT.rearrange("(a p t) c -> a t p c", a=PASSES, p=P, t=PACK)
-        landing = [(0, 0), (0, 1), (0, 2), (0, 3), (1, 1), (1, 2), (1, 3), (1, 0)]
+        landing = [(a, t) for a in range(PASSES) for t in range(PACK)]
 
         nc.vector.memset(word_scales[:].bitcast(I32), 0)
         nc.vector.memset(zeros[:], 0.0)
@@ -88,33 +85,33 @@ def tile_moe_bdx_lin_none_kernel(tc, dyT, w_words, w_scales, gate, offs, out):
                     nc.tensor.transpose(
                         bank[:, i * P : (i + 1) * P], gate_cols[:, col : col + 1].to_broadcast([P, P]), identity[:]
                     )
-                nc.scalar.copy(
-                    gates[h][:].rearrange("m (p g i) -> m g p i", g=RUN // LINE, i=LINE)[:, g, :, :],
-                    bank[:].rearrange("m (i p) -> m p i", i=LINE),
-                )
+                for half in range(2):
+                    nc.scalar.copy(
+                        gates[2 * h + half][:].rearrange("m (p g i) -> m g p i", g=RUN // LINE, i=LINE)[:, g, :, :],
+                        bank[:].rearrange("m (i p) -> m p i", i=LINE)[:, half * P // 2 : (half + 1) * P // 2, :],
+                    )
 
         def listed(lo, n):
             return offsets[:, lo // PER_COLUMN : (lo + n) // PER_COLUMN]
 
-        def gather(dst, a, t, lo, n):
-            h = lo // HALF
-            nc.vector.tensor_tensor(
-                dst, dy[a, t][:].indirect(listed(lo, n)), gates[h][:, lo - h * HALF : lo - h * HALF + n], MULT
-            )
+        def gather(dst, a, t, e, lo, n):
+            nc.vector.tensor_tensor(dst, dy[a, t][:].indirect(listed(e * C + lo, n)), gates[e][:, lo : lo + n], MULT)
 
-        def interleave(src, a, lo, n):
+        def interleave(src, a, e, lo, n):
+            at = PACK * (e * C + lo)
             nc.scalar.copy(
-                rounded[a][:, PACK * lo : PACK * (lo + n)].rearrange("p (c i t) -> p c t i", i=LINE, t=PACK),
+                rounded[a][:, at : at + PACK * n].rearrange("p (c i t) -> p c t i", i=LINE, t=PACK),
                 src.rearrange("p t (c i) -> p c t i", i=LINE),
             )
 
         codes = {}
 
-        def quantise(a, lo, hi):
+        def quantise(a, e, lo=0, n=C):
+            at = e * C + lo
             nc.vector.quantize_mx(
-                out=codes[a, lo // 2][:, (lo % 2) * C : (lo % 2 + hi - lo) * C].bitcast(FP8X4),
-                scales=code_scales[a][:, lo * C : hi * C],
-                in_=rounded[a][:, PACK * lo * C : PACK * hi * C],
+                out=codes[a, e][:, lo : lo + n].bitcast(FP8X4),
+                scales=code_scales[a][:, at : at + n],
+                in_=rounded[a][:, PACK * at : PACK * (at + n)],
             )
 
         def product(e, kt):
@@ -125,7 +122,7 @@ def tile_moe_bdx_lin_none_kernel(tc, dyT, w_words, w_scales, gate, offs, out):
                     out=bank[:],
                     lhsT=words[:, 2 * w0 : 2 * (w0 + P)].bitcast(FP4X4),
                     lhsT_scale=word_scales[:, w0 : w0 + P],
-                    rhs=codes[a, e // 2][:, (e % 2) * C : (e % 2 + 1) * C].bitcast(FP8X4),
+                    rhs=codes[a, e][:].bitcast(FP8X4),
                     rhs_scale=code_scales[a][:, e * C : (e + 1) * C],
                     start=(a == 0),
                     stop=(a == PASSES - 1),
@@ -135,102 +132,83 @@ def tile_moe_bdx_lin_none_kernel(tc, dyT, w_words, w_scales, gate, offs, out):
         def by_plane(ap):
             return ap.rearrange("p (t s) -> p t s", t=PACK)
 
-        first0 = held.tile([P, PACK * HALF], F32, name="first0")
-        first1 = [
-            held.tile([P, PACK * C], F32, name="first10", tag="first10_then_fill"),
-            held.tile([P, PACK * C], F32, name="first11"),
-        ]
-        woven = held.tile([P, C + STEPS * SHORT_GATHER], F32, name="woven")
-        for t in range(PACK):
-            gather(first0[:, t * HALF : (t + 1) * HALF], 0, t, 0, HALF)
-        for e in range(2):
-            interleave(by_plane(first0[:])[:, :, e * C : (e + 1) * C], 0, e * C, C)
-        for t in [at[1] for at in landing[PACK:]]:
+        first = {(a, e): held.tile([P, PACK * C], F32, name=f"first{a}{e}", tag=f"first{a}{e}") for a in range(PASSES) for e in range(2)}
+        for a, t in landing[:-1]:
             for e in range(2):
-                gather(first1[e][:, t * C : (t + 1) * C], 1, t, e * C, C)
-        gather(woven[:, 0:C], 1, 0, 2 * C, C)
-        interleave(by_plane(first1[0][:]), 1, 0, C)
+                gather(first[a, e][:, t * C : (t + 1) * C], a, t, e, 0, C)
+            if (a, t) == (0, PACK - 1):
+                for e in range(2):
+                    interleave(by_plane(first[0, e][:]), 0, e, 0, C)
+        top = (PACK - 1) * C
+        for lo in (0, C // 2):
+            gather(first[1, 0][:, top + lo : top + lo + C // 2], 1, PACK - 1, 0, lo, C // 2)
+            interleave(by_plane(first[1, 0][:])[:, :, lo : lo + C // 2], 1, 0, lo, C // 2)
+        gather(first[1, 1][:, top : top + C], 1, PACK - 1, 1, 0, C)
 
-        codes[0, 0] = held.tile([P, HALF], U32, name="codes00", tag="gates0_then_codes", align_bytes=MX_ALIGN)
-        for at in [(1, 0), (0, 1), (1, 1)]:
-            codes[at] = held.tile([P, HALF], U32, name=f"codes{at[0]}{at[1]}", align_bytes=MX_ALIGN)
-        quantise(0, 0, 2)
-        quantise(1, 0, 1)
-        fill = held.tile([P, PACK * FILL], F32, name="fill", tag="first10_then_fill")
+        for a in range(PASSES):
+            for e in range(E):
+                tag = f"gates{e}" if a == 0 and e < 2 else f"codes{a}{e}"
+                codes[a, e] = held.tile([P, C], U32, name=f"codes{a}{e}", tag=tag, align_bytes=MX_ALIGN)
+        quantise(0, 0)
+        quantise(0, 1)
+        for lo in (0, C // 2):
+            quantise(1, 0, lo, C // 2)
+        fill = held.tile([P, PACK * C], F32, name="fill", tag="first10")
         for t in range(PACK):
-            gather(fill[:, t * FILL : (t + 1) * FILL], 0, t, 2 * C, FILL)
+            gather(fill[:, t * C : (t + 1) * C], 0, t, 2, 0, C)
 
-        def first_products(e):
-            span = KT * C // SHORT_SCATTER * SHORT_GATHER
-            pieces = woven[:, C + e * span : C + (e + 1) * span].rearrange("p (g k c) -> p g k c", k=KT, c=SHORT_GATHER)
+        scatters = KT * (3 * C - LATE) // SHORT
+        woven = held.tile([P, scatters * REGION], F32, name="woven")
+        banks = {}
+
+        def products(e, n):
+            first_step = KT * e * C // SHORT
+            regions = woven[:, first_step * REGION : (first_step + KT * n // SHORT) * REGION]
+            pieces = regions.rearrange("p (g k c) -> p g k c", k=KT, c=REGION)
             for kt in range(KT):
-                bank = product(e, kt)
-                nc.scalar.copy(pieces[:, :, kt, 0:SHORT_SCATTER], bank[:].rearrange("p (g c) -> p g c", c=SHORT_SCATTER))
+                banks[e, kt] = product(e, kt)
+                nc.scalar.copy(pieces[:, :, kt, 0:SHORT], banks[e, kt][:, 0:n].rearrange("p (g c) -> p g c", c=SHORT))
 
-        first_products(0)
+        products(0, C)
         for lo in range(0, C, P):
-            interleave(by_plane(first1[1][:])[:, :, lo : lo + P], 1, C + lo, P)
-        interleave(by_plane(fill[:]), 0, 2 * C, FILL)
+            interleave(by_plane(first[1, 1][:])[:, :, lo : lo + P], 1, 1, lo, P)
+        interleave(by_plane(fill[:]), 0, 2, 0, C)
 
-        rest = (
-            [(1, t, 2 * C + lo) for t in range(1, PACK) for lo in range(0, C, SHORT_GATHER)]
-            + [(0, t, 2 * C + FILL) for t in range(PACK)]
-            + [(a, t, 3 * C + lo) for a in range(PASSES) for t in range(PACK) for lo in range(0, C, SHORT_GATHER)]
-        )
-        block = PACK * C
-        last = held.tile([P, 5 * C], F32, name="last")
+        units = [(a, e, sum(UNITS[:u]), UNITS[u]) for a, e in [(1, 2), (0, 3), (1, 3)] for u in range(len(UNITS))]
+        gathers = PACK * len(units)
 
-        def woven_scatter(j):
-            at = C + j * SHORT_GATHER
-            nc.vector.tensor_tensor(
-                outs[j % KT][:].indirect(listed(j // KT * SHORT_SCATTER, SHORT_SCATTER)),
-                woven[:, at : at + SHORT_SCATTER],
-                zeros[:],
-                ADD,
-            )
+        def short_scatter(kt, lo, n, src):
+            nc.vector.tensor_tensor(outs[kt][:].indirect(listed(lo, n)), src, zeros[:, 0:n], ADD)
 
-        def woven_gather(j):
-            at = C + j * SHORT_GATHER
-            gather(woven[:, at : at + SHORT_GATHER], *rest[j], SHORT_GATHER)
+        after = {
+            4: lambda: (quantise(1, 1), products(1, C)),
+            10: lambda: quantise(0, 2),
+            24: lambda: (quantise(1, 2), products(2, C - LATE)),
+            44: lambda: quantise(0, 3),
+            56: lambda: quantise(1, 3, 0, C // 2),
+        }
+        for j in range(scatters):
+            short_scatter(j % KT, j // KT * SHORT, SHORT, woven[:, j * REGION : j * REGION + SHORT])
+            i = j - LEAD
+            if 0 <= i < gathers:
+                a, e, lo, n = units[i // PACK]
+                gather(woven[:, i * REGION : i * REGION + n], a, i % PACK, e, lo, n)
+                if i % PACK == PACK - 1:
+                    unit = woven[:, (i + 1 - PACK) * REGION : (i + 1) * REGION]
+                    interleave(by_plane(unit)[:, :, 0:n], a, e, lo, n)
+                if i + 1 in after:
+                    after[i + 1]()
 
-        for j in range(STEPS + LEAD):
-            if j < STEPS:
-                woven_scatter(j)
-            if j >= LEAD:
-                woven_gather(j - LEAD)
-            done = j - LEAD + 1
-            if done == 4:
-                quantise(1, 1, 2)
-                first_products(1)
-            if done == 12:
-                interleave(by_plane(woven[:, 0:block]), 1, 2 * C, C)
-            if done == 16:
-                interleave(by_plane(woven[:, block : block + C]), 0, 2 * C + FILL, C - FILL)
-            if done == 24:
-                quantise(1, 2, 3)
-            if done == 28:
-                quantise(0, 2, 3)
-                for kt in range(2):
-                    nc.scalar.copy(last[:, kt * C : (kt + 1) * C], product(2, kt)[:])
-            if done == 32:
-                interleave(by_plane(woven[:, block + C : 2 * block + C]), 0, 3 * C, C)
-            if done == 42:
-                quantise(0, 3, 4)
-        interleave(by_plane(woven[:, 2 * block + C : 3 * block + C]), 1, 3 * C, C)
-
-        def scatter(src, kt, e):
-            nc.vector.tensor_copy(outs[kt][:].indirect(listed(e * C, C)), src)
-
-        late = woven[:, 2 * block + C : 2 * block + 2 * C]
-        nc.scalar.copy(late, product(2, 2)[:])
-        scatter(last[:, 0:C], 0, 2)
-        scatter(last[:, C : 2 * C], 1, 2)
-        quantise(1, 3, 4)
+        late = woven[:, (gathers - PACK) * REGION : gathers * REGION]
         for kt in range(KT):
-            nc.scalar.copy(last[:, (2 + kt) * C : (3 + kt) * C], product(3, kt)[:])
-        scatter(late, 2, 2)
+            nc.scalar.copy(late[:, kt * REGION : kt * REGION + LATE], banks[2, kt][:, C - LATE : C])
+        quantise(1, 3, C // 2, C // 2)
         for kt in range(KT):
-            scatter(last[:, (2 + kt) * C : (3 + kt) * C], kt, 3)
+            nc.scalar.copy(woven[:, kt * C : (kt + 1) * C], product(3, kt)[:])
+        for kt in range(KT):
+            short_scatter(kt, 3 * C - LATE, LATE, late[:, kt * REGION : kt * REGION + LATE])
+        for kt in range(KT):
+            nc.vector.tensor_copy(outs[kt][:].indirect(listed(3 * C, C)), woven[:, kt * C : (kt + 1) * C])
             rows = slice(kt * P, (kt + 1) * P)
             nc.sync.dma_start(out[rows, 0 : T // 2], outs[kt][:, 0 : T // 2])
             nc.scalar.dma_start(out[rows, T // 2 : T], outs[kt][:, T // 2 : T])

@@ -29,9 +29,9 @@ RUN = HALF // P
 LINE = 4
 QUADRANTS = 4
 MX_ALIGN = 64
-SHORT = 64
-REGION = 128
-UNITS = (128, 96, 96, 96, 96)
+SHORT = 128
+REGION = 256
+FILL = 256
 LATE = 128
 LEAD = 2
 
@@ -153,9 +153,9 @@ def tile_moe_bdx_lin_none_kernel(tc, dyT, w_words, w_scales, gate, offs, out):
         quantise(0, 1)
         for lo in (0, C // 2):
             quantise(1, 0, lo, C // 2)
-        fill = held.tile([P, PACK * C], F32, name="fill", tag="first10")
+        fill = held.tile([P, PACK * FILL], F32, name="fill", tag="first10")
         for t in range(PACK):
-            gather(fill[:, t * C : (t + 1) * C], 0, t, 2, 0, C)
+            gather(fill[:, t * FILL : (t + 1) * FILL], 0, t, 2, 0, FILL)
 
         scatters = KT * (3 * C - LATE) // SHORT
         woven = held.tile([P, scatters * REGION], F32, name="woven")
@@ -172,20 +172,20 @@ def tile_moe_bdx_lin_none_kernel(tc, dyT, w_words, w_scales, gate, offs, out):
         products(0, C)
         for lo in range(0, C, P):
             interleave(by_plane(first[1, 1][:])[:, :, lo : lo + P], 1, 1, lo, P)
-        interleave(by_plane(fill[:]), 0, 2, 0, C)
+        interleave(by_plane(fill[:]), 0, 2, 0, FILL)
 
-        units = [(a, e, sum(UNITS[:u]), UNITS[u]) for a, e in [(1, 2), (0, 3), (1, 3)] for u in range(len(UNITS))]
+        units = [(0, 2, FILL, REGION)] + [(a, e, lo, REGION) for a, e in [(1, 2), (0, 3), (1, 3)] for lo in (0, REGION)]
         gathers = PACK * len(units)
 
         def short_scatter(kt, lo, n, src):
             nc.vector.tensor_tensor(outs[kt][:].indirect(listed(lo, n)), src, zeros[:, 0:n], ADD)
 
         after = {
-            4: lambda: (quantise(1, 1), products(1, C)),
-            10: lambda: quantise(0, 2),
-            24: lambda: (quantise(1, 2), products(2, C - LATE)),
-            44: lambda: quantise(0, 3),
-            56: lambda: quantise(1, 3, 0, C // 2),
+            2: lambda: (quantise(1, 1), products(1, C)),
+            6: lambda: quantise(0, 2),
+            14: lambda: (quantise(1, 2), products(2, C - LATE)),
+            22: lambda: quantise(0, 3),
+            26: lambda: quantise(1, 3, 0, C // 2),
         }
         for j in range(scatters):
             short_scatter(j % KT, j // KT * SHORT, SHORT, woven[:, j * REGION : j * REGION + SHORT])

@@ -29,11 +29,17 @@ RUN = HALF // P
 LINE = 4
 QUADRANTS = 4
 MX_ALIGN = 64
-SHORT = 128
-REGION = 256
-FILL = 256
-LATE = 128
+SHORT = 64
+REGION = 192
+FILL = 192
+UNITS = (
+    (0, 2, FILL, (160, 160)),
+    (0, 3, 0, (192, 160, 160)),
+    (1, 2, 0, (192, 160, 160)),
+    (1, 3, 0, (192, 160, 160)),
+)
 LEAD = 2
+PIECE = C // 2
 
 
 def tile_moe_bdx_lin_none_kernel(tc, dyT, w_words, w_scales, gate, offs, out):
@@ -47,12 +53,14 @@ def tile_moe_bdx_lin_none_kernel(tc, dyT, w_words, w_scales, gate, offs, out):
         words = held.tile([P, GROUPS * 2 * K], U8, name="words", align_bytes=MX_ALIGN)
         word_scales = held.tile([P, GROUPS * K], U8, name="word_scales", align_bytes=MX_ALIGN)
         outs = [held.tile([P, T], F32, name=f"outs{kt}") for kt in range(KT)]
-        zeros = held.tile([P, LATE], F32, name="zeros")
-        gates = [held.tile([P, C], F32, name=f"gates{e}", tag=f"gates{e}", align_bytes=MX_ALIGN) for e in range(E)]
-        gate_cols = held.tile([P, E * LINE], F32, name="gate_cols")
+        zeros = held.tile([P, SHORT], F32, name="zeros")
+        early_gates = held.tile([P, HALF], F32, name="early_gates", tag="gates_then_codes", align_bytes=MX_ALIGN)
+        late_gates = held.tile([P, T - C], F32, name="late_gates")
+        gate_cols = held.tile([P, 2 * RUN], F32, name="gate_cols")
         identity = held.tile([P, P], F32, name="identity")
         code_scales = [held.tile([P, T], U8, name=f"code_scales{a}", align_bytes=MX_ALIGN) for a in range(PASSES)]
         rounded = [held.tile([P, PACK * T], BF16, name=f"rounded{a}", align_bytes=MX_ALIGN) for a in range(PASSES)]
+        piece = held.tile([P, PACK * PIECE], BF16, name="piece", tag="piece_then_fill", align_bytes=MX_ALIGN)
 
         dy_rows = dyT.rearrange("(a p t) c -> a t p c", a=PASSES, p=P, t=PACK)
         landing = [(a, t) for a in range(PASSES) for t in range(PACK)]
@@ -76,7 +84,11 @@ def tile_moe_bdx_lin_none_kernel(tc, dyT, w_words, w_scales, gate, offs, out):
                 w_scales.bitcast(I32).rearrange("e a f k -> f (e a) k")[4 * q : 4 * q + 4, :, :],
             )
 
+        def by_run(ap, g):
+            return ap.rearrange("m (p g i) -> m g p i", g=RUN // LINE, i=LINE)[:, g, :, :]
+
         make_identity(nc, identity[:])
+        turned = {}
         for h in range(2):
             for g in range(RUN // LINE):
                 bank = psum.tile([P, C], F32, name="bank")
@@ -85,33 +97,37 @@ def tile_moe_bdx_lin_none_kernel(tc, dyT, w_words, w_scales, gate, offs, out):
                     nc.tensor.transpose(
                         bank[:, i * P : (i + 1) * P], gate_cols[:, col : col + 1].to_broadcast([P, P]), identity[:]
                     )
-                for half in range(2):
-                    nc.scalar.copy(
-                        gates[2 * h + half][:].rearrange("m (p g i) -> m g p i", g=RUN // LINE, i=LINE)[:, g, :, :],
-                        bank[:].rearrange("m (i p) -> m p i", i=LINE)[:, half * P // 2 : (half + 1) * P // 2, :],
-                    )
+                turned[h, g] = bank[:].rearrange("m (i p) -> m p i", i=LINE)
+        for g in range(RUN // LINE):
+            nc.scalar.copy(by_run(early_gates[:], g), turned[0, g])
+        for g in range(RUN // LINE):
+            nc.scalar.copy(by_run(late_gates[:, 0:C], g), turned[0, g][:, P // 2 : P, :])
+            nc.scalar.copy(by_run(late_gates[:, C : C + HALF], g), turned[1, g])
 
         def listed(lo, n):
             return offsets[:, lo // PER_COLUMN : (lo + n) // PER_COLUMN]
 
-        def gather(dst, a, t, e, lo, n):
-            nc.vector.tensor_tensor(dst, dy[a, t][:].indirect(listed(e * C + lo, n)), gates[e][:, lo : lo + n], MULT)
+        def gather(dst, a, t, lo, n, gates):
+            nc.vector.tensor_tensor(dst, dy[a, t][:].indirect(listed(lo, n)), gates, MULT)
 
-        def interleave(src, a, e, lo, n):
-            at = PACK * (e * C + lo)
+        def late_gather(dst, a, t, lo, n):
+            gather(dst, a, t, lo, n, late_gates[:, lo - C : lo - C + n])
+
+        def interleave(dst, src):
             nc.scalar.copy(
-                rounded[a][:, at : at + PACK * n].rearrange("p (c i t) -> p c t i", i=LINE, t=PACK),
-                src.rearrange("p t (c i) -> p c t i", i=LINE),
+                dst.rearrange("p (c i t) -> p c t i", i=LINE, t=PACK), src.rearrange("p t (c i) -> p c t i", i=LINE)
             )
+
+        def slots(a, lo, n):
+            return rounded[a][:, PACK * lo : PACK * (lo + n)]
 
         codes = {}
 
-        def quantise(a, e, lo=0, n=C):
-            at = e * C + lo
+        def quantise(a, lo, n, src):
             nc.vector.quantize_mx(
-                out=codes[a, e][:, lo : lo + n].bitcast(FP8X4),
-                scales=code_scales[a][:, at : at + n],
-                in_=rounded[a][:, PACK * at : PACK * (at + n)],
+                out=codes[a, lo // HALF][:, lo % HALF : lo % HALF + n].bitcast(FP8X4),
+                scales=code_scales[a][:, lo : lo + n],
+                in_=src,
             )
 
         def product(e, kt):
@@ -122,7 +138,7 @@ def tile_moe_bdx_lin_none_kernel(tc, dyT, w_words, w_scales, gate, offs, out):
                     out=bank[:],
                     lhsT=words[:, 2 * w0 : 2 * (w0 + P)].bitcast(FP4X4),
                     lhsT_scale=word_scales[:, w0 : w0 + P],
-                    rhs=codes[a, e][:].bitcast(FP8X4),
+                    rhs=codes[a, e // 2][:, (e % 2) * C : (e % 2 + 1) * C].bitcast(FP8X4),
                     rhs_scale=code_scales[a][:, e * C : (e + 1) * C],
                     start=(a == 0),
                     stop=(a == PASSES - 1),
@@ -132,83 +148,94 @@ def tile_moe_bdx_lin_none_kernel(tc, dyT, w_words, w_scales, gate, offs, out):
         def by_plane(ap):
             return ap.rearrange("p (t s) -> p t s", t=PACK)
 
-        first = {(a, e): held.tile([P, PACK * C], F32, name=f"first{a}{e}", tag=f"first{a}{e}") for a in range(PASSES) for e in range(2)}
+        first = [held.tile([P, PACK * HALF], F32, name=f"first{a}") for a in range(PASSES)]
         for a, t in landing[:-1]:
-            for e in range(2):
-                gather(first[a, e][:, t * C : (t + 1) * C], a, t, e, 0, C)
+            gather(first[a][:, t * HALF : (t + 1) * HALF], a, t, 0, HALF, early_gates[:])
             if (a, t) == (0, PACK - 1):
-                for e in range(2):
-                    interleave(by_plane(first[0, e][:]), 0, e, 0, C)
-        top = (PACK - 1) * C
-        for lo in (0, C // 2):
-            gather(first[1, 0][:, top + lo : top + lo + C // 2], 1, PACK - 1, 0, lo, C // 2)
-            interleave(by_plane(first[1, 0][:])[:, :, lo : lo + C // 2], 1, 0, lo, C // 2)
-        gather(first[1, 1][:, top : top + C], 1, PACK - 1, 1, 0, C)
+                for lo in (0, C):
+                    interleave(slots(0, lo, C), by_plane(first[0][:])[:, :, lo : lo + C])
+        top = (PACK - 1) * HALF
+        for lo in (0, PIECE):
+            gather(first[1][:, top + lo : top + lo + PIECE], 1, PACK - 1, lo, PIECE, early_gates[:, lo : lo + PIECE])
+            interleave(slots(1, lo, PIECE) if lo else piece[:], by_plane(first[1][:])[:, :, lo : lo + PIECE])
+        late_gather(first[1][:, top + C : top + HALF], 1, PACK - 1, C, C)
 
         for a in range(PASSES):
-            for e in range(E):
-                tag = f"gates{e}" if a == 0 and e < 2 else f"codes{a}{e}"
-                codes[a, e] = held.tile([P, C], U32, name=f"codes{a}{e}", tag=tag, align_bytes=MX_ALIGN)
-        quantise(0, 0)
-        quantise(0, 1)
-        for lo in (0, C // 2):
-            quantise(1, 0, lo, C // 2)
-        fill = held.tile([P, PACK * FILL], F32, name="fill", tag="first10")
+            for h in range(2):
+                tag = "gates_then_codes" if (a, h) == (0, 0) else f"codes{a}{h}"
+                codes[a, h] = held.tile([P, HALF], U32, name=f"codes{a}{h}", tag=tag, align_bytes=MX_ALIGN)
+        quantise(0, 0, HALF, slots(0, 0, HALF))
+        quantise(1, 0, PIECE, piece[:])
+        quantise(1, PIECE, PIECE, slots(1, PIECE, PIECE))
+        fill = held.tile([P, PACK * FILL], F32, name="fill", tag="piece_then_fill", align_bytes=MX_ALIGN)
         for t in range(PACK):
-            gather(fill[:, t * FILL : (t + 1) * FILL], 0, t, 2, 0, FILL)
+            late_gather(fill[:, t * FILL : (t + 1) * FILL], 0, t, HALF, FILL)
 
-        scatters = KT * (3 * C - LATE) // SHORT
-        woven = held.tile([P, scatters * REGION], F32, name="woven")
-        banks = {}
+        steps = KT * HALF // SHORT
+        woven = held.tile([P, steps * REGION], F32, name="woven")
 
-        def products(e, n):
-            first_step = KT * e * C // SHORT
-            regions = woven[:, first_step * REGION : (first_step + KT * n // SHORT) * REGION]
-            pieces = regions.rearrange("p (g k c) -> p g k c", k=KT, c=REGION)
+        def products(e):
+            span = KT * C // SHORT * REGION
+            pieces = woven[:, e * span : (e + 1) * span].rearrange("p (g k c) -> p g k c", k=KT, c=REGION)
             for kt in range(KT):
-                banks[e, kt] = product(e, kt)
-                nc.scalar.copy(pieces[:, :, kt, 0:SHORT], banks[e, kt][:, 0:n].rearrange("p (g c) -> p g c", c=SHORT))
+                nc.scalar.copy(pieces[:, :, kt, 0:SHORT], product(e, kt)[:].rearrange("p (g c) -> p g c", c=SHORT))
 
-        products(0, C)
-        for lo in range(0, C, P):
-            interleave(by_plane(first[1, 1][:])[:, :, lo : lo + P], 1, 1, lo, P)
-        interleave(by_plane(fill[:]), 0, 2, 0, FILL)
+        products(0)
+        for lo in range(C, HALF, P):
+            interleave(slots(1, lo, P), by_plane(first[1][:])[:, :, lo : lo + P])
+        interleave(slots(0, HALF, FILL), by_plane(fill[:]))
 
-        units = [(0, 2, FILL, REGION)] + [(a, e, lo, REGION) for a, e in [(1, 2), (0, 3), (1, 3)] for lo in (0, REGION)]
+        units = [(a, e * C + lo + sum(ns[:u]), ns[u]) for a, e, lo, ns in UNITS for u in range(len(ns))]
         gathers = PACK * len(units)
+        both = first[0][:, 0:HALF]
+        single = {(e, kt): first[0][:, HALF + (2 * kt + e - 2) * C : HALF + (2 * kt + e - 1) * C] for e in (2, 3) for kt in range(2)}
+        banks = []
 
-        def short_scatter(kt, lo, n, src):
-            nc.vector.tensor_tensor(outs[kt][:].indirect(listed(lo, n)), src, zeros[:, 0:n], ADD)
+        def third_products():
+            quantise(1, HALF, C, slots(1, HALF, C))
+            banks.extend(product(2, kt) for kt in range(KT))
+            nc.scalar.copy(single[2, 0], banks[0][:])
+            nc.scalar.copy(both[:, 0:C], banks[2][:])
 
         after = {
-            2: lambda: (quantise(1, 1), products(1, C)),
-            6: lambda: quantise(0, 2),
-            14: lambda: (quantise(1, 2), products(2, C - LATE)),
-            22: lambda: quantise(0, 3),
-            26: lambda: quantise(1, 3, 0, C // 2),
+            4: lambda: (quantise(1, C, C, slots(1, C, C)), products(1)),
+            24: lambda: quantise(0, HALF, HALF, slots(0, HALF, HALF)),
+            36: third_products,
         }
-        for j in range(scatters):
-            short_scatter(j % KT, j // KT * SHORT, SHORT, woven[:, j * REGION : j * REGION + SHORT])
+        for j in range(steps):
+            nc.vector.tensor_tensor(
+                outs[j % KT][:].indirect(listed(j // KT * SHORT, SHORT)),
+                woven[:, j * REGION : j * REGION + SHORT],
+                zeros[:],
+                ADD,
+            )
             i = j - LEAD
             if 0 <= i < gathers:
-                a, e, lo, n = units[i // PACK]
-                gather(woven[:, i * REGION : i * REGION + n], a, i % PACK, e, lo, n)
+                a, lo, n = units[i // PACK]
+                late_gather(woven[:, i * REGION : i * REGION + n], a, i % PACK, lo, n)
                 if i % PACK == PACK - 1:
                     unit = woven[:, (i + 1 - PACK) * REGION : (i + 1) * REGION]
-                    interleave(by_plane(unit)[:, :, 0:n], a, e, lo, n)
+                    interleave(slots(a, lo, n), by_plane(unit)[:, :, 0:n])
                 if i + 1 in after:
                     after[i + 1]()
 
-        late = woven[:, (gathers - PACK) * REGION : gathers * REGION]
-        for kt in range(KT):
-            nc.scalar.copy(late[:, kt * REGION : kt * REGION + LATE], banks[2, kt][:, C - LATE : C])
-        quantise(1, 3, C // 2, C // 2)
-        for kt in range(KT):
-            nc.scalar.copy(woven[:, kt * C : (kt + 1) * C], product(3, kt)[:])
-        for kt in range(KT):
-            short_scatter(kt, 3 * C - LATE, LATE, late[:, kt * REGION : kt * REGION + LATE])
-        for kt in range(KT):
-            nc.vector.tensor_copy(outs[kt][:].indirect(listed(3 * C, C)), woven[:, kt * C : (kt + 1) * C])
+        def scatter(kt, lo, n, src):
+            nc.vector.tensor_copy(outs[kt][:].indirect(listed(lo, n)), src)
+
+        def store(kt):
             rows = slice(kt * P, (kt + 1) * P)
             nc.sync.dma_start(out[rows, 0 : T // 2], outs[kt][:, 0 : T // 2])
             nc.scalar.dma_start(out[rows, T // 2 : T], outs[kt][:, T // 2 : T])
+
+        late = woven[:, (gathers - PACK) * REGION : (gathers - PACK) * REGION + C]
+        nc.scalar.copy(late, banks[1][:])
+        scatter(0, HALF, C, single[2, 0])
+        quantise(1, 3 * C, C, slots(1, 3 * C, C))
+        for kt, dst in enumerate([single[3, 0], single[3, 1], both[:, C:HALF]]):
+            nc.scalar.copy(dst, product(3, kt)[:])
+        scatter(1, HALF, C, late)
+        for kt in range(2):
+            scatter(kt, 3 * C, C, single[3, kt])
+            store(kt)
+        scatter(2, HALF, HALF, both)
+        store(2)

@@ -31,15 +31,11 @@ QUADRANTS = 4
 MX_ALIGN = 64
 SHORT = 64
 REGION = 192
-FILL = 192
-UNITS = (
-    (0, 2, FILL, (160, 160)),
-    (0, 3, 0, (192, 160, 160)),
-    (1, 2, 0, (192, 160, 160)),
-    (1, 3, 0, (192, 160, 160)),
-)
+EARLY = 736
+FIRST = 128
+FILL = 160
 LEAD = 2
-PIECE = C // 2
+UNITS = 2 * [(1, 160)] + [(0, 192), (0, 160)] + 3 * [(1, 160)] + [(0, 192), (0, 160), (0, 160), (1, 192), (1, 160), (1, 160)]
 
 
 def tile_moe_bdx_lin_none_kernel(tc, dyT, w_words, w_scales, gate, offs, out):
@@ -50,23 +46,47 @@ def tile_moe_bdx_lin_none_kernel(tc, dyT, w_words, w_scales, gate, offs, out):
 
         offsets = held.tile([P, T // PER_COLUMN], U16, name="offsets")
         dy = {(a, t): held.tile([P, T], F32, name=f"dy{a}{t}") for a in range(PASSES) for t in range(PACK)}
-        words = held.tile([P, GROUPS * 2 * K], U8, name="words", align_bytes=MX_ALIGN)
-        word_scales = held.tile([P, GROUPS * K], U8, name="word_scales", align_bytes=MX_ALIGN)
+        words = [
+            held.tile([P, groups * 2 * K], U8, name=f"words{groups}", align_bytes=MX_ALIGN)
+            for groups in (PASSES, GROUPS - PASSES)
+        ]
+        word_scales = [
+            held.tile([P, groups * K], U8, name=f"word_scales{groups}", align_bytes=MX_ALIGN)
+            for groups in (PASSES, GROUPS - PASSES)
+        ]
         outs = [held.tile([P, T], F32, name=f"outs{kt}") for kt in range(KT)]
         zeros = held.tile([P, SHORT], F32, name="zeros")
         early_gates = held.tile([P, HALF], F32, name="early_gates", tag="gates_then_codes", align_bytes=MX_ALIGN)
-        late_gates = held.tile([P, T - C], F32, name="late_gates")
+        late_gates = held.tile([P, T], F32, name="late_gates")
         gate_cols = held.tile([P, 2 * RUN], F32, name="gate_cols")
         identity = held.tile([P, P], F32, name="identity")
         code_scales = [held.tile([P, T], U8, name=f"code_scales{a}", align_bytes=MX_ALIGN) for a in range(PASSES)]
-        rounded = [held.tile([P, PACK * T], BF16, name=f"rounded{a}", align_bytes=MX_ALIGN) for a in range(PASSES)]
-        piece = held.tile([P, PACK * PIECE], BF16, name="piece", tag="piece_then_fill", align_bytes=MX_ALIGN)
+        rounded = {
+            (a, e): held.tile([P, PACK * C], BF16, name=f"rounded{a}{e}", tag=f"rounded{a}{e}", align_bytes=MX_ALIGN)
+            for a in range(PASSES)
+            for e in range(E)
+            if (a, e) != (0, 2)
+        }
+        steps = PACK * len(UNITS) + LEAD
+        woven = held.tile([P, steps * REGION], F32, name="woven")
+        regions = woven[:].rearrange("p (g k c) -> p g k c", k=KT, c=REGION)
+        first_steps = KT * FIRST // SHORT
+        codes = {
+            (a, e): held.tile([P, C], U32, name=f"codes{a}{e}", align_bytes=MX_ALIGN)
+            for a in range(PASSES)
+            for e in range(E)
+            if a or e > 1
+        }
 
         dy_rows = dyT.rearrange("(a p t) c -> a t p c", a=PASSES, p=P, t=PACK)
         landing = [(a, t) for a in range(PASSES) for t in range(PACK)]
 
-        nc.vector.memset(word_scales[:].bitcast(I32), 0)
+        for plane in word_scales:
+            nc.vector.memset(plane[:].bitcast(I32), 0)
         nc.vector.memset(zeros[:], 0.0)
+        nc.vector.memset(regions[:, 0 : FIRST // SHORT, :, 0:SHORT], 0.0)
+        nc.vector.memset(codes[1, 0][:, FIRST:C], 0)
+        nc.vector.memset(code_scales[1][:, FIRST:C].bitcast(I32), 0)
         nc.sync.dma_start(
             gate_cols[:].rearrange("p (h i) -> p h i", h=2), gate[0, :].rearrange("(h p i) -> p h i", h=2, i=RUN)
         )
@@ -74,15 +94,15 @@ def tile_moe_bdx_lin_none_kernel(tc, dyT, w_words, w_scales, gate, offs, out):
         nc.sync.dma_start(offsets[:], offs)
         for at in landing[1:]:
             nc.sync.dma_start(dy[at][:], dy_rows[at])
-        nc.sync.dma_start(
-            words[:].bitcast(I32).rearrange("p (g b) -> p g b", g=GROUPS),
-            w_words.bitcast(I32).rearrange("e a p b -> p (e a) b"),
-        )
-        for q in range(QUADRANTS):
-            nc.sync.dma_start(
-                word_scales[32 * q : 32 * q + 4, :].bitcast(I32).rearrange("p (g k) -> p g k", g=GROUPS),
-                w_scales.bitcast(I32).rearrange("e a f k -> f (e a) k")[4 * q : 4 * q + 4, :, :],
-            )
+        word_rows = w_words.bitcast(I32).rearrange("e a p b -> p (e a) b")
+        scale_rows = w_scales.bitcast(I32).rearrange("e a f k -> f (e a) k")
+        for part, (lo, hi) in enumerate([(0, PASSES), (PASSES, GROUPS)]):
+            nc.sync.dma_start(words[part][:].bitcast(I32).rearrange("p (g b) -> p g b", g=hi - lo), word_rows[:, lo:hi, :])
+            for q in range(QUADRANTS):
+                nc.sync.dma_start(
+                    word_scales[part][32 * q : 32 * q + 4, :].bitcast(I32).rearrange("p (g k) -> p g k", g=hi - lo),
+                    scale_rows[4 * q : 4 * q + 4, lo:hi, :],
+                )
 
         def by_run(ap, g):
             return ap.rearrange("m (p g i) -> m g p i", g=RUN // LINE, i=LINE)[:, g, :, :]
@@ -99,46 +119,42 @@ def tile_moe_bdx_lin_none_kernel(tc, dyT, w_words, w_scales, gate, offs, out):
                     )
                 turned[h, g] = bank[:].rearrange("m (i p) -> m p i", i=LINE)
         for g in range(RUN // LINE):
-            nc.scalar.copy(by_run(early_gates[:], g), turned[0, g])
-        for g in range(RUN // LINE):
-            nc.scalar.copy(by_run(late_gates[:, 0:C], g), turned[0, g][:, P // 2 : P, :])
-            nc.scalar.copy(by_run(late_gates[:, C : C + HALF], g), turned[1, g])
+            nc.scalar.copy(by_run(early_gates[:, 0:HALF], g), turned[0, g])
+        for h in range(2):
+            for g in range(RUN // LINE):
+                nc.scalar.copy(by_run(late_gates[:, h * HALF : (h + 1) * HALF], g), turned[h, g])
 
         def listed(lo, n):
             return offsets[:, lo // PER_COLUMN : (lo + n) // PER_COLUMN]
 
         def gather(dst, a, t, lo, n, gates):
-            nc.vector.tensor_tensor(dst, dy[a, t][:].indirect(listed(lo, n)), gates, MULT)
+            nc.vector.tensor_tensor(dst, dy[a, t][:].indirect(listed(lo, n)), gates[:, lo : lo + n], MULT)
 
-        def late_gather(dst, a, t, lo, n):
-            gather(dst, a, t, lo, n, late_gates[:, lo - C : lo - C + n])
+        def interleave(a, lo, n, src):
+            cut = min(n, C - lo % C)
+            for at, m, part in [(lo, cut, src[:, :, 0:cut]), (lo + cut, n - cut, src[:, :, cut:n])][: 1 + (cut < n)]:
+                dst = rounded[a, at // C][:, PACK * (at % C) : PACK * (at % C + m)]
+                nc.scalar.copy(
+                    dst.rearrange("p (c i t) -> p c t i", i=LINE, t=PACK), part.rearrange("p t (c i) -> p c t i", i=LINE)
+                )
 
-        def interleave(dst, src):
-            nc.scalar.copy(
-                dst.rearrange("p (c i t) -> p c t i", i=LINE, t=PACK), src.rearrange("p t (c i) -> p c t i", i=LINE)
-            )
-
-        def slots(a, lo, n):
-            return rounded[a][:, PACK * lo : PACK * (lo + n)]
-
-        codes = {}
-
-        def quantise(a, lo, n, src):
+        def quantise(a, lo, n):
             nc.vector.quantize_mx(
-                out=codes[a, lo // HALF][:, lo % HALF : lo % HALF + n].bitcast(FP8X4),
+                out=codes[a, lo // C][:, lo % C : lo % C + n].bitcast(FP8X4),
                 scales=code_scales[a][:, lo : lo + n],
-                in_=src,
+                in_=rounded[a, lo // C][:, PACK * (lo % C) : PACK * (lo % C + n)],
             )
 
         def product(e, kt):
             bank = psum.tile([P, C], F32, name="bank")
             for a in range(PASSES):
-                w0 = (e * PASSES + a) * K + P * kt
+                part = min(e, 1)
+                w0 = ((e - part) * PASSES + a) * K + P * kt
                 nc.tensor.matmul_mx(
                     out=bank[:],
-                    lhsT=words[:, 2 * w0 : 2 * (w0 + P)].bitcast(FP4X4),
-                    lhsT_scale=word_scales[:, w0 : w0 + P],
-                    rhs=codes[a, e // 2][:, (e % 2) * C : (e % 2 + 1) * C].bitcast(FP8X4),
+                    lhsT=words[part][:, 2 * w0 : 2 * (w0 + P)].bitcast(FP4X4),
+                    lhsT_scale=word_scales[part][:, w0 : w0 + P],
+                    rhs=codes[a, e][:].bitcast(FP8X4),
                     rhs_scale=code_scales[a][:, e * C : (e + 1) * C],
                     start=(a == 0),
                     stop=(a == PASSES - 1),
@@ -148,74 +164,106 @@ def tile_moe_bdx_lin_none_kernel(tc, dyT, w_words, w_scales, gate, offs, out):
         def by_plane(ap):
             return ap.rearrange("p (t s) -> p t s", t=PACK)
 
-        first = [held.tile([P, PACK * HALF], F32, name=f"first{a}") for a in range(PASSES)]
-        for a, t in landing[:-1]:
-            gather(first[a][:, t * HALF : (t + 1) * HALF], a, t, 0, HALF, early_gates[:])
-            if (a, t) == (0, PACK - 1):
-                for lo in (0, C):
-                    interleave(slots(0, lo, C), by_plane(first[0][:])[:, :, lo : lo + C])
-        top = (PACK - 1) * HALF
-        for lo in (0, PIECE):
-            gather(first[1][:, top + lo : top + lo + PIECE], 1, PACK - 1, lo, PIECE, early_gates[:, lo : lo + PIECE])
-            interleave(slots(1, lo, PIECE) if lo else piece[:], by_plane(first[1][:])[:, :, lo : lo + PIECE])
-        late_gather(first[1][:, top + C : top + HALF], 1, PACK - 1, C, C)
-
-        for a in range(PASSES):
-            for h in range(2):
-                tag = "gates_then_codes" if (a, h) == (0, 0) else f"codes{a}{h}"
-                codes[a, h] = held.tile([P, HALF], U32, name=f"codes{a}{h}", tag=tag, align_bytes=MX_ALIGN)
-        quantise(0, 0, HALF, slots(0, 0, HALF))
-        quantise(1, 0, PIECE, piece[:])
-        quantise(1, PIECE, PIECE, slots(1, PIECE, PIECE))
-        fill = held.tile([P, PACK * FILL], F32, name="fill", tag="piece_then_fill", align_bytes=MX_ALIGN)
+        narrow = EARLY - FIRST
+        gap = KT * FIRST
+        early0 = held.tile([P, PACK * HALF], F32, name="early0")
+        second = KT * C // SHORT * REGION
+        early1 = by_plane(woven[:, second : second + PACK * (narrow + gap)])
+        first = held.tile([P, PACK * FIRST], F32, name="first", tag="first_then_fill", align_bytes=MX_ALIGN)
         for t in range(PACK):
-            late_gather(fill[:, t * FILL : (t + 1) * FILL], 0, t, HALF, FILL)
-
-        steps = KT * HALF // SHORT
-        woven = held.tile([P, steps * REGION], F32, name="woven")
+            gather(early0[:, t * HALF : (t + 1) * HALF], 0, t, 0, HALF, early_gates)
+        for lo in (0, C):
+            interleave(0, lo, C, by_plane(early0[:])[:, :, lo : lo + C])
+        for t in range(PACK):
+            gather(first[:, t * FIRST : (t + 1) * FIRST], 1, t, 0, FIRST, early_gates if t < 3 else late_gates)
+            gather(early1[:, t, 0:narrow], 1, t, FIRST, narrow, early_gates if t < 2 else late_gates)
+            if t == 2:
+                codes[0, 0] = held.tile([P, C], U32, name="codes00", tag="gates_then_codes", align_bytes=MX_ALIGN)
+                quantise(0, 0, C)
+        interleave(1, 0, FIRST, by_plane(first[:]))
+        quantise(1, 0, FIRST)
+        fill = held.tile([P, PACK * FILL], F32, name="fill", tag="first_then_fill", align_bytes=MX_ALIGN)
+        for t in range(PACK):
+            gather(fill[:, t * FILL : (t + 1) * FILL], 0, t, HALF, FILL, late_gates)
 
         def products(e):
-            span = KT * C // SHORT * REGION
-            pieces = woven[:, e * span : (e + 1) * span].rearrange("p (g k c) -> p g k c", k=KT, c=REGION)
+            return [product(e, kt) for kt in range(KT)]
+
+        def spread(banks, e, lo, hi):
             for kt in range(KT):
-                nc.scalar.copy(pieces[:, :, kt, 0:SHORT], product(e, kt)[:].rearrange("p (g c) -> p g c", c=SHORT))
+                nc.scalar.copy(
+                    regions[:, (e * C + lo) // SHORT : (e * C + hi) // SHORT, kt, 0:SHORT],
+                    banks[kt][:, lo:hi].rearrange("p (g c) -> p g c", c=SHORT),
+                )
 
-        products(0)
-        for lo in range(C, HALF, P):
-            interleave(slots(1, lo, P), by_plane(first[1][:])[:, :, lo : lo + P])
-        interleave(slots(0, HALF, FILL), by_plane(fill[:]))
+        def first_source(j):
+            return early1[:, 0, narrow + j * SHORT : narrow + (j + 1) * SHORT]
 
-        units = [(a, e * C + lo + sum(ns[:u]), ns[u]) for a, e, lo, ns in UNITS for u in range(len(ns))]
-        gathers = PACK * len(units)
-        both = first[0][:, 0:HALF]
-        single = {(e, kt): first[0][:, HALF + (2 * kt + e - 2) * C : HALF + (2 * kt + e - 1) * C] for e in (2, 3) for kt in range(2)}
-        banks = []
+        def first_copy(j):
+            nc.scalar.copy(first_source(j), banks[j % KT][:, j // KT * SHORT : (j // KT + 1) * SHORT])
+
+        def piece(lo, n):
+            interleave(1, lo, n, early1[:, :, lo - FIRST : lo - FIRST + n])
+
+        banks = products(0)
+        piece(P, P)
+        first_copy(0)
+        piece(2 * P, P)
+        first_copy(1)
+        first_copy(2)
+        piece(3 * P, P)
+        for j in range(KT, first_steps):
+            first_copy(j)
+        piece(C, EARLY - C)
+
+        units, at = [], [HALF + FILL, EARLY]
+        for a, n in UNITS:
+            units.append((a, at[a], n))
+            at[a] = at[a] + n
+        woven_slots = steps // KT * SHORT
+        left = 3 * C - woven_slots
+        both = early0[:, 0 : left + C]
+        single = [early0[:, HALF + i * C : HALF + (i + 1) * C] for i in range(3)]
+        third = []
+
+        def rest_of_first():
+            quantise(1, FIRST, FIRST)
+            quantise(1, 2 * FIRST, C - 2 * FIRST)
+            spread(products(0), 0, FIRST, C)
+            rounded[0, 2] = held.tile([P, PACK * C], BF16, name="rounded02", tag="rounded10", align_bytes=MX_ALIGN)
+            interleave(0, HALF, FILL, by_plane(fill[:]))
+            codes[0, 1] = held.tile([P, C], U32, name="codes01", tag="first_then_fill", align_bytes=MX_ALIGN)
 
         def third_products():
-            quantise(1, HALF, C, slots(1, HALF, C))
-            banks.extend(product(2, kt) for kt in range(KT))
-            nc.scalar.copy(single[2, 0], banks[0][:])
-            nc.scalar.copy(both[:, 0:C], banks[2][:])
+            quantise(0, HALF, C)
+            quantise(1, HALF, C)
+            third.extend(products(2))
+            spread(third, 2, 0, C - left)
+            nc.scalar.copy(single[2][:, 0:left], third[0][:, C - left : C])
+            nc.scalar.copy(both[:, 0:left], third[2][:, C - left : C])
 
         after = {
-            4: lambda: (quantise(1, C, C, slots(1, C, C)), products(1)),
-            24: lambda: quantise(0, HALF, HALF, slots(0, HALF, HALF)),
-            36: third_products,
+            1: rest_of_first,
+            8: lambda: quantise(0, C, C),
+            11: lambda: (quantise(1, C, C), spread(products(1), 1, 0, C)),
+            32: third_products,
+            44: lambda: quantise(0, 3 * C, C),
         }
         for j in range(steps):
+            held_back = woven[:, j * REGION : j * REGION + SHORT]
             nc.vector.tensor_tensor(
                 outs[j % KT][:].indirect(listed(j // KT * SHORT, SHORT)),
-                woven[:, j * REGION : j * REGION + SHORT],
-                zeros[:],
+                first_source(j) if j < first_steps else held_back,
+                held_back if j < first_steps else zeros[:],
                 ADD,
             )
             i = j - LEAD
-            if 0 <= i < gathers:
+            if i >= 0:
                 a, lo, n = units[i // PACK]
-                late_gather(woven[:, i * REGION : i * REGION + n], a, i % PACK, lo, n)
+                gather(woven[:, i * REGION : i * REGION + n], a, i % PACK, lo, n, late_gates)
                 if i % PACK == PACK - 1:
                     unit = woven[:, (i + 1 - PACK) * REGION : (i + 1) * REGION]
-                    interleave(slots(a, lo, n), by_plane(unit)[:, :, 0:n])
+                    interleave(a, lo, n, by_plane(unit)[:, :, 0:n])
                 if i + 1 in after:
                     after[i + 1]()
 
@@ -227,15 +275,16 @@ def tile_moe_bdx_lin_none_kernel(tc, dyT, w_words, w_scales, gate, offs, out):
             nc.sync.dma_start(out[rows, 0 : T // 2], outs[kt][:, 0 : T // 2])
             nc.scalar.dma_start(out[rows, T // 2 : T], outs[kt][:, T // 2 : T])
 
-        late = woven[:, (gathers - PACK) * REGION : (gathers - PACK) * REGION + C]
-        nc.scalar.copy(late, banks[1][:])
-        scatter(0, HALF, C, single[2, 0])
-        quantise(1, 3 * C, C, slots(1, 3 * C, C))
-        for kt, dst in enumerate([single[3, 0], single[3, 1], both[:, C:HALF]]):
+        last_unit = (steps - LEAD - PACK) * REGION
+        late = woven[:, last_unit : last_unit + left]
+        nc.scalar.copy(late, third[1][:, C - left : C])
+        scatter(0, woven_slots, left, single[2][:, 0:left])
+        quantise(1, 3 * C, C)
+        for kt, dst in enumerate([single[0], single[1], both[:, left : left + C]]):
             nc.scalar.copy(dst, product(3, kt)[:])
-        scatter(1, HALF, C, late)
+        scatter(1, woven_slots, left, late)
         for kt in range(2):
-            scatter(kt, 3 * C, C, single[3, kt])
+            scatter(kt, 3 * C, C, single[kt])
             store(kt)
-        scatter(2, HALF, HALF, both)
+        scatter(2, woven_slots, left + C, both)
         store(2)

@@ -31,18 +31,21 @@ QUADRANTS = 4
 MX_ALIGN = 64
 SHORT = 64
 REGION = 192
-EARLY = 736
+EARLY = 672
 FIRST = 128
 FILL = 160
 LEAD = 2
-UNITS = 2 * [(1, 160)] + [(0, 192), (0, 160)] + 3 * [(1, 160)] + [(0, 192), (0, 160), (0, 160), (1, 192), (1, 160), (1, 160)]
+UNITS = 2 * [(1, 192)] + [(0, 192), (0, 160)] + 3 * [(1, 160)] + [(0, 192), (0, 160), (0, 160), (1, 192), (1, 160), (1, 160)]
 
 
 def tile_moe_bdx_lin_none_kernel(tc, dyT, w_words, w_scales, gate, offs, out):
     nc = tc.nc
     with ExitStack() as ctx:
         held = ctx.enter_context(tc.tile_pool(name="held", bufs=1))
-        psum = ctx.enter_context(tc.psum_pool(name="psum", bufs=8))
+        psum = ctx.enter_context(tc.psum_pool(name="psum", bufs=1))
+
+        def by_plane(ap):
+            return ap.rearrange("p (t s) -> p t s", t=PACK)
 
         offsets = held.tile([P, T // PER_COLUMN], U16, name="offsets")
         dy = {(a, t): held.tile([P, T], F32, name=f"dy{a}{t}") for a in range(PASSES) for t in range(PACK)}
@@ -65,14 +68,22 @@ def tile_moe_bdx_lin_none_kernel(tc, dyT, w_words, w_scales, gate, offs, out):
             (a, e): held.tile([P, PACK * C], BF16, name=f"rounded{a}{e}", tag=f"rounded{a}{e}", align_bytes=MX_ALIGN)
             for a in range(PASSES)
             for e in range(E)
-            if (a, e) != (0, 2)
+            if a or e == 3
         }
-        steps = PACK * len(UNITS) + LEAD
-        woven = held.tile([P, steps * REGION], F32, name="woven")
-        regions = woven[:].rearrange("p (g k c) -> p g k c", k=KT, c=REGION)
+        early_rounded = held.tile([P, PACK * HALF], BF16, name="early_rounded", align_bytes=MX_ALIGN)
+        for e in range(2):
+            rounded[0, e] = early_rounded[:, PACK * e * C : PACK * (e + 1) * C]
         first_steps = KT * FIRST // SHORT
+        steps = first_steps + PACK * len(UNITS) - (PACK - 1) + LEAD
+        narrow = EARLY - FIRST
+        row = narrow + KT * FIRST
+        front = (PACK - 1) * row + P
+        planes = held.tile([P, front + (steps - first_steps) * REGION], F32, name="planes")
+        early1 = by_plane(planes[:, 0 : PACK * row])
+        woven = planes[:, front:]
+        regions = woven.rearrange("p (g k c) -> p g k c", k=KT, c=REGION)
         codes = {
-            (a, e): held.tile([P, C], U32, name=f"codes{a}{e}", align_bytes=MX_ALIGN)
+            (a, e): held.tile([P, C], U32, name=f"codes{a}{e}", tag=f"codes{a}{e}", align_bytes=MX_ALIGN)
             for a in range(PASSES)
             for e in range(E)
             if a or e > 1
@@ -84,34 +95,50 @@ def tile_moe_bdx_lin_none_kernel(tc, dyT, w_words, w_scales, gate, offs, out):
         for plane in word_scales:
             nc.vector.memset(plane[:].bitcast(I32), 0)
         nc.vector.memset(zeros[:], 0.0)
-        nc.vector.memset(regions[:, 0 : FIRST // SHORT, :, 0:SHORT], 0.0)
-        nc.vector.memset(codes[1, 0][:, FIRST:C], 0)
-        nc.vector.memset(code_scales[1][:, FIRST:C].bitcast(I32), 0)
-        nc.sync.dma_start(
+        padded_codes = held.tile([P, C], U32, name="padded_codes", align_bytes=MX_ALIGN)
+        padded_scales = held.tile([P, C], U8, name="padded_scales", align_bytes=MX_ALIGN)
+        nc.vector.memset(padded_codes[:, FIRST:C], 0)
+        nc.vector.memset(padded_scales[:, FIRST:C].bitcast(I32), 0)
+        nc.scalar.dma_start(
             gate_cols[:].rearrange("p (h i) -> p h i", h=2), gate[0, :].rearrange("(h p i) -> p h i", h=2, i=RUN)
         )
         nc.sync.dma_start(dy[landing[0]][:], dy_rows[landing[0]])
         nc.sync.dma_start(offsets[:], offs)
-        for at in landing[1:]:
-            nc.sync.dma_start(dy[at][:], dy_rows[at])
         word_rows = w_words.bitcast(I32).rearrange("e a p b -> p (e a) b")
         scale_rows = w_scales.bitcast(I32).rearrange("e a f k -> f (e a) k")
-        for part, (lo, hi) in enumerate([(0, PASSES), (PASSES, GROUPS)]):
+        parts = [(0, PASSES), (PASSES, GROUPS)]
+
+        def load_words(part):
+            lo, hi = parts[part]
             nc.sync.dma_start(words[part][:].bitcast(I32).rearrange("p (g b) -> p g b", g=hi - lo), word_rows[:, lo:hi, :])
+
+        def load_scales(part):
+            lo, hi = parts[part]
             for q in range(QUADRANTS):
                 nc.sync.dma_start(
                     word_scales[part][32 * q : 32 * q + 4, :].bitcast(I32).rearrange("p (g k) -> p g k", g=hi - lo),
                     scale_rows[4 * q : 4 * q + 4, lo:hi, :],
                 )
 
+        for at in landing[1:-1]:
+            nc.sync.dma_start(dy[at][:], dy_rows[at])
+        load_scales(0)
+        nc.sync.dma_start(dy[landing[-1]][:], dy_rows[landing[-1]])
+        load_words(0)
+        load_words(1)
+        load_scales(1)
+
         def by_run(ap, g):
             return ap.rearrange("m (p g i) -> m g p i", g=RUN // LINE, i=LINE)[:, g, :, :]
+
+        def bank_tile(b):
+            return psum.tile([P, C], F32, name="bank", tag=f"bank{b}")
 
         make_identity(nc, identity[:])
         turned = {}
         for h in range(2):
             for g in range(RUN // LINE):
-                bank = psum.tile([P, C], F32, name="bank")
+                bank = bank_tile(2 * h + g)
                 for i in range(LINE):
                     col = h * RUN + g * LINE + i
                     nc.tensor.transpose(
@@ -145,8 +172,8 @@ def tile_moe_bdx_lin_none_kernel(tc, dyT, w_words, w_scales, gate, offs, out):
                 in_=rounded[a, lo // C][:, PACK * (lo % C) : PACK * (lo % C + n)],
             )
 
-        def product(e, kt):
-            bank = psum.tile([P, C], F32, name="bank")
+        def product(e, kt, banks, padded=False):
+            bank = bank_tile(KT * banks + kt)
             for a in range(PASSES):
                 part = min(e, 1)
                 w0 = ((e - part) * PASSES + a) * K + P * kt
@@ -154,45 +181,68 @@ def tile_moe_bdx_lin_none_kernel(tc, dyT, w_words, w_scales, gate, offs, out):
                     out=bank[:],
                     lhsT=words[part][:, 2 * w0 : 2 * (w0 + P)].bitcast(FP4X4),
                     lhsT_scale=word_scales[part][:, w0 : w0 + P],
-                    rhs=codes[a, e][:].bitcast(FP8X4),
-                    rhs_scale=code_scales[a][:, e * C : (e + 1) * C],
+                    rhs=(padded_codes[:] if padded and a else codes[a, e][:, 0:C]).bitcast(FP8X4),
+                    rhs_scale=padded_scales[:] if padded and a else code_scales[a][:, e * C : (e + 1) * C],
                     start=(a == 0),
                     stop=(a == PASSES - 1),
                 )
             return bank
 
-        def by_plane(ap):
-            return ap.rearrange("p (t s) -> p t s", t=PACK)
-
-        narrow = EARLY - FIRST
-        gap = KT * FIRST
         early0 = held.tile([P, PACK * HALF], F32, name="early0")
-        second = KT * C // SHORT * REGION
-        early1 = by_plane(woven[:, second : second + PACK * (narrow + gap)])
         first = held.tile([P, PACK * FIRST], F32, name="first", tag="first_then_fill", align_bytes=MX_ALIGN)
-        for t in range(PACK):
+        nc.vector.tensor_copy(early0[:, 0:HALF], dy[0, 0][:].indirect(listed(0, HALF)))
+        runs = early0[:, 0:HALF].rearrange("m (p i) -> m i p", i=RUN)
+        gated = held.tile([P, HALF], F32, name="gated")
+        for g in range(RUN // LINE):
+            bank = bank_tile(4 + g)
+            for i in range(LINE):
+                nc.tensor.transpose(bank[:, i * P : (i + 1) * P], runs[:, LINE * g + i, :], identity[:])
+            for i in range(LINE):
+                col = LINE * g + i
+                nc.scalar.activation(
+                    gated[:, col * P : (col + 1) * P],
+                    bank[:, i * P : (i + 1) * P],
+                    mybir.ActivationFunctionType.Copy,
+                    scale=gate_cols[:, col : col + 1],
+                )
+        for g in range(RUN // LINE):
+            bank = bank_tile(6 + g)
+            for i in range(LINE):
+                col = LINE * g + i
+                nc.tensor.transpose(bank[:, i * P : (i + 1) * P], gated[:, col * P : (col + 1) * P], identity[:])
+            nc.scalar.copy(by_run(early0[:, 0:HALF], g), bank[:].rearrange("m (i p) -> m p i", i=LINE))
+        for t in range(1, PACK - 1):
             gather(early0[:, t * HALF : (t + 1) * HALF], 0, t, 0, HALF, early_gates)
         for lo in (0, C):
+            gather(by_plane(early0[:])[:, PACK - 1, lo : lo + C], 0, PACK - 1, lo, C, early_gates)
             interleave(0, lo, C, by_plane(early0[:])[:, :, lo : lo + C])
         for t in range(PACK):
             gather(first[:, t * FIRST : (t + 1) * FIRST], 1, t, 0, FIRST, early_gates if t < 3 else late_gates)
             gather(early1[:, t, 0:narrow], 1, t, FIRST, narrow, early_gates if t < 2 else late_gates)
             if t == 2:
-                codes[0, 0] = held.tile([P, C], U32, name="codes00", tag="gates_then_codes", align_bytes=MX_ALIGN)
-                quantise(0, 0, C)
+                early_codes = held.tile([P, HALF], U32, name="early_codes", tag="gates_then_codes", align_bytes=MX_ALIGN)
+                nc.vector.quantize_mx(
+                    out=early_codes[:].bitcast(FP8X4), scales=code_scales[0][:, 0:HALF], in_=early_rounded[:]
+                )
+                for e in range(2):
+                    codes[0, e] = early_codes[:, e * C : (e + 1) * C]
         interleave(1, 0, FIRST, by_plane(first[:]))
-        quantise(1, 0, FIRST)
+        nc.vector.quantize_mx(
+            out=padded_codes[:, 0:FIRST].bitcast(FP8X4),
+            scales=padded_scales[:, 0:FIRST],
+            in_=rounded[1, 0][:, 0 : PACK * FIRST],
+        )
         fill = held.tile([P, PACK * FILL], F32, name="fill", tag="first_then_fill", align_bytes=MX_ALIGN)
         for t in range(PACK):
             gather(fill[:, t * FILL : (t + 1) * FILL], 0, t, HALF, FILL, late_gates)
 
-        def products(e):
-            return [product(e, kt) for kt in range(KT)]
+        def products(e, banks):
+            return [product(e, kt, banks) for kt in range(KT)]
 
         def spread(banks, e, lo, hi):
             for kt in range(KT):
                 nc.scalar.copy(
-                    regions[:, (e * C + lo) // SHORT : (e * C + hi) // SHORT, kt, 0:SHORT],
+                    regions[:, (e * C + lo - FIRST) // SHORT : (e * C + hi - FIRST) // SHORT, kt, 0:SHORT],
                     banks[kt][:, lo:hi].rearrange("p (g c) -> p g c", c=SHORT),
                 )
 
@@ -205,7 +255,7 @@ def tile_moe_bdx_lin_none_kernel(tc, dyT, w_words, w_scales, gate, offs, out):
         def piece(lo, n):
             interleave(1, lo, n, early1[:, :, lo - FIRST : lo - FIRST + n])
 
-        banks = products(0)
+        banks = [product(0, kt, 0, padded=True) for kt in range(KT)]
         piece(P, P)
         first_copy(0)
         piece(2 * P, P)
@@ -227,43 +277,49 @@ def tile_moe_bdx_lin_none_kernel(tc, dyT, w_words, w_scales, gate, offs, out):
         third = []
 
         def rest_of_first():
-            quantise(1, FIRST, FIRST)
-            quantise(1, 2 * FIRST, C - 2 * FIRST)
-            spread(products(0), 0, FIRST, C)
-            rounded[0, 2] = held.tile([P, PACK * C], BF16, name="rounded02", tag="rounded10", align_bytes=MX_ALIGN)
+            quantise(1, 0, C)
+            spread(products(0, 1), 0, FIRST, C)
+            rounded[0, 2] = held.tile([P, PACK * C], BF16, name="rounded02", tag="codes10", align_bytes=MX_ALIGN)
             interleave(0, HALF, FILL, by_plane(fill[:]))
-            codes[0, 1] = held.tile([P, C], U32, name="codes01", tag="first_then_fill", align_bytes=MX_ALIGN)
 
         def third_products():
             quantise(0, HALF, C)
             quantise(1, HALF, C)
-            third.extend(products(2))
+            third.extend(products(2, 0))
             spread(third, 2, 0, C - left)
             nc.scalar.copy(single[2][:, 0:left], third[0][:, C - left : C])
             nc.scalar.copy(both[:, 0:left], third[2][:, C - left : C])
 
         after = {
             1: rest_of_first,
-            8: lambda: quantise(0, C, C),
-            11: lambda: (quantise(1, C, C), spread(products(1), 1, 0, C)),
+            11: lambda: (quantise(1, C, C), spread(products(1, 1), 1, 0, C)),
             32: third_products,
             44: lambda: quantise(0, 3 * C, C),
         }
+        def region(j, count=1):
+            return woven[:, (j - first_steps) * REGION : (j - first_steps + count) * REGION]
+
+        def unit_planes(u):
+            if u == 0:
+                return early1[:, :, P : P + REGION]
+            return by_plane(region(first_steps + PACK * u - (PACK - 1), PACK))
+
+        follows = {LEAD + i: i for i in range(PACK - 1)}
+        follows.update({first_steps + LEAD + i: PACK - 1 + i for i in range(steps - first_steps - LEAD)})
         for j in range(steps):
-            held_back = woven[:, j * REGION : j * REGION + SHORT]
             nc.vector.tensor_tensor(
                 outs[j % KT][:].indirect(listed(j // KT * SHORT, SHORT)),
-                first_source(j) if j < first_steps else held_back,
-                held_back if j < first_steps else zeros[:],
+                first_source(j) if j < first_steps else region(j)[:, 0:SHORT],
+                zeros[:],
                 ADD,
             )
-            i = j - LEAD
-            if i >= 0:
+            if j in follows:
+                i = follows[j]
                 a, lo, n = units[i // PACK]
-                gather(woven[:, i * REGION : i * REGION + n], a, i % PACK, lo, n, late_gates)
+                unit = unit_planes(i // PACK)[:, :, 0:n]
+                gather(unit[:, i % PACK, :], a, i % PACK, lo, n, late_gates)
                 if i % PACK == PACK - 1:
-                    unit = woven[:, (i + 1 - PACK) * REGION : (i + 1) * REGION]
-                    interleave(a, lo, n, by_plane(unit)[:, :, 0:n])
+                    interleave(a, lo, n, unit)
                 if i + 1 in after:
                     after[i + 1]()
 
@@ -275,13 +331,12 @@ def tile_moe_bdx_lin_none_kernel(tc, dyT, w_words, w_scales, gate, offs, out):
             nc.sync.dma_start(out[rows, 0 : T // 2], outs[kt][:, 0 : T // 2])
             nc.scalar.dma_start(out[rows, T // 2 : T], outs[kt][:, T // 2 : T])
 
-        last_unit = (steps - LEAD - PACK) * REGION
-        late = woven[:, last_unit : last_unit + left]
+        late = region(steps - LEAD - PACK, PACK)[:, 0:left]
         nc.scalar.copy(late, third[1][:, C - left : C])
         scatter(0, woven_slots, left, single[2][:, 0:left])
         quantise(1, 3 * C, C)
         for kt, dst in enumerate([single[0], single[1], both[:, left : left + C]]):
-            nc.scalar.copy(dst, product(3, kt)[:])
+            nc.scalar.copy(dst, product(3, kt, 1)[:])
         scatter(1, woven_slots, left, late)
         for kt in range(2):
             scatter(kt, 3 * C, C, single[kt])

@@ -60,6 +60,7 @@ def tile_moe_bdx_lin_none_kernel(tc, dyT, w_words, w_scales, gate, offs, out):
         outs = [held.tile([P, T], F32, name=f"outs{kt}") for kt in range(KT)]
         zeros = held.tile([P, SHORT], F32, name="zeros")
         early_gates = held.tile([P, HALF], F32, name="early_gates", tag="gates_then_codes", align_bytes=MX_ALIGN)
+        first_gates = held.tile([P, FIRST], F32, name="first_gates", tag="first_gates_then_codes", align_bytes=MX_ALIGN)
         late_gates = held.tile([P, T], F32, name="late_gates")
         gate_cols = held.tile([P, 2 * RUN], F32, name="gate_cols")
         identity = held.tile([P, P], F32, name="identity")
@@ -68,11 +69,8 @@ def tile_moe_bdx_lin_none_kernel(tc, dyT, w_words, w_scales, gate, offs, out):
             (a, e): held.tile([P, PACK * C], BF16, name=f"rounded{a}{e}", tag=f"rounded{a}{e}", align_bytes=MX_ALIGN)
             for a in range(PASSES)
             for e in range(E)
-            if a or e == 3
+            if (a, e) != (0, 2)
         }
-        early_rounded = held.tile([P, PACK * HALF], BF16, name="early_rounded", align_bytes=MX_ALIGN)
-        for e in range(2):
-            rounded[0, e] = early_rounded[:, PACK * e * C : PACK * (e + 1) * C]
         first_steps = KT * FIRST // SHORT
         steps = first_steps + PACK * len(UNITS) - (PACK - 1) + LEAD
         narrow = EARLY - FIRST
@@ -99,6 +97,8 @@ def tile_moe_bdx_lin_none_kernel(tc, dyT, w_words, w_scales, gate, offs, out):
         padded_scales = held.tile([P, C], U8, name="padded_scales", align_bytes=MX_ALIGN)
         nc.vector.memset(padded_codes[:, FIRST:C], 0)
         nc.vector.memset(padded_scales[:, FIRST:C].bitcast(I32), 0)
+        nc.vector.memset(codes[1, 0][:, 0:FIRST], 0)
+        nc.vector.memset(code_scales[1][:, 0:FIRST].bitcast(I32), 0)
         nc.scalar.dma_start(
             gate_cols[:].rearrange("p (h i) -> p h i", h=2), gate[0, :].rearrange("(h p i) -> p h i", h=2, i=RUN)
         )
@@ -147,6 +147,8 @@ def tile_moe_bdx_lin_none_kernel(tc, dyT, w_words, w_scales, gate, offs, out):
                 turned[h, g] = bank[:].rearrange("m (i p) -> m p i", i=LINE)
         for g in range(RUN // LINE):
             nc.scalar.copy(by_run(early_gates[:, 0:HALF], g), turned[0, g])
+        for g in range(RUN // LINE):
+            nc.scalar.copy(by_run(first_gates[:], g), turned[0, g][:, 0 : FIRST // RUN, :])
         for h in range(2):
             for g in range(RUN // LINE):
                 nc.scalar.copy(by_run(late_gates[:, h * HALF : (h + 1) * HALF], g), turned[h, g])
@@ -217,15 +219,12 @@ def tile_moe_bdx_lin_none_kernel(tc, dyT, w_words, w_scales, gate, offs, out):
             gather(by_plane(early0[:])[:, PACK - 1, lo : lo + C], 0, PACK - 1, lo, C, early_gates)
             interleave(0, lo, C, by_plane(early0[:])[:, :, lo : lo + C])
         for t in range(PACK):
-            gather(first[:, t * FIRST : (t + 1) * FIRST], 1, t, 0, FIRST, early_gates if t < 3 else late_gates)
-            gather(early1[:, t, 0:narrow], 1, t, FIRST, narrow, early_gates if t < 2 else late_gates)
-            if t == 2:
-                early_codes = held.tile([P, HALF], U32, name="early_codes", tag="gates_then_codes", align_bytes=MX_ALIGN)
-                nc.vector.quantize_mx(
-                    out=early_codes[:].bitcast(FP8X4), scales=code_scales[0][:, 0:HALF], in_=early_rounded[:]
-                )
-                for e in range(2):
-                    codes[0, e] = early_codes[:, e * C : (e + 1) * C]
+            gather(first[:, t * FIRST : (t + 1) * FIRST], 1, t, 0, FIRST, [early_gates, early_gates, first_gates, late_gates][t])
+            gather(early1[:, t, 0:narrow], 1, t, FIRST, narrow, late_gates if t else early_gates)
+            if t in (1, 2):
+                tag = ["gates_then_codes", "first_gates_then_codes"][t - 1]
+                codes[0, t - 1] = held.tile([P, C], U32, name=f"codes0{t - 1}", tag=tag, align_bytes=MX_ALIGN)
+                quantise(0, (t - 1) * C, C)
         interleave(1, 0, FIRST, by_plane(first[:]))
         nc.vector.quantize_mx(
             out=padded_codes[:, 0:FIRST].bitcast(FP8X4),
@@ -277,7 +276,8 @@ def tile_moe_bdx_lin_none_kernel(tc, dyT, w_words, w_scales, gate, offs, out):
         third = []
 
         def rest_of_first():
-            quantise(1, 0, C)
+            quantise(1, FIRST, FIRST)
+            quantise(1, 2 * FIRST, C - 2 * FIRST)
             spread(products(0, 1), 0, FIRST, C)
             rounded[0, 2] = held.tile([P, PACK * C], BF16, name="rounded02", tag="codes10", align_bytes=MX_ALIGN)
             interleave(0, HALF, FILL, by_plane(fill[:]))

@@ -25,17 +25,25 @@ KT = K // P
 GROUPS = E * PASSES
 HALF = 2 * C
 PER_COLUMN = 16
+GRAIN = 2 * PER_COLUMN
 RUN = HALF // P
 LINE = 4
 QUADRANTS = 4
 MX_ALIGN = 64
+
 SHORT = 64
 REGION = 192
-EARLY = 672
+EARLY = 704
 FIRST = 128
 FILL = 160
 LEAD = 2
-UNITS = 2 * [(1, 192)] + [(0, 192), (0, 160)] + 3 * [(1, 160)] + [(0, 192), (0, 160), (0, 160), (1, 192), (1, 160), (1, 160)]
+
+
+def cut(lo, hi):
+    count = -(-(hi - lo) // REGION)
+    grains, more = divmod((hi - lo) // GRAIN, count)
+    sizes = [GRAIN * (grains + (i < more)) for i in range(count)]
+    return [(lo + sum(sizes[:i]), sizes[i]) for i in range(count)]
 
 
 def tile_moe_bdx_lin_none_kernel(tc, dyT, w_words, w_scales, gate, offs, out):
@@ -47,16 +55,19 @@ def tile_moe_bdx_lin_none_kernel(tc, dyT, w_words, w_scales, gate, offs, out):
         def by_plane(ap):
             return ap.rearrange("p (t s) -> p t s", t=PACK)
 
+        one, two = EARLY + 2 * REGION, EARLY + 5 * REGION
+        stretches = [(1, EARLY, one), (0, HALF + FILL, 3 * C), (1, one, two), (0, 3 * C, T), (1, two, T)]
+        units = [(a, lo, n) for a, begin, end in stretches for lo, n in cut(begin, end)]
+        gathered = [PACK * sum(len(cut(begin, end)) for a, begin, end in stretches[: i + 1]) for i in range(len(stretches))]
+        first_steps = KT * FIRST // SHORT
+        owned = PACK * len(units) - (PACK - 1)
+        steps = -(-(first_steps + owned + LEAD) // KT) * KT
+
         offsets = held.tile([P, T // PER_COLUMN], U16, name="offsets")
         dy = {(a, t): held.tile([P, T], F32, name=f"dy{a}{t}") for a in range(PASSES) for t in range(PACK)}
-        words = [
-            held.tile([P, groups * 2 * K], U8, name=f"words{groups}", align_bytes=MX_ALIGN)
-            for groups in (PASSES, GROUPS - PASSES)
-        ]
-        word_scales = [
-            held.tile([P, groups * K], U8, name=f"word_scales{groups}", align_bytes=MX_ALIGN)
-            for groups in (PASSES, GROUPS - PASSES)
-        ]
+        parts = [(0, PASSES), (PASSES, GROUPS)]
+        words = [held.tile([P, (hi - lo) * 2 * K], U8, name=f"words{lo}", align_bytes=MX_ALIGN) for lo, hi in parts]
+        word_scales = [held.tile([P, (hi - lo) * K], U8, name=f"word_scales{lo}", align_bytes=MX_ALIGN) for lo, hi in parts]
         outs = [held.tile([P, T], F32, name=f"outs{kt}") for kt in range(KT)]
         zeros = held.tile([P, SHORT], F32, name="zeros")
         early_gates = held.tile([P, HALF], F32, name="early_gates", tag="gates_then_codes", align_bytes=MX_ALIGN)
@@ -66,13 +77,11 @@ def tile_moe_bdx_lin_none_kernel(tc, dyT, w_words, w_scales, gate, offs, out):
         identity = held.tile([P, P], F32, name="identity")
         code_scales = [held.tile([P, T], U8, name=f"code_scales{a}", align_bytes=MX_ALIGN) for a in range(PASSES)]
         rounded = {
-            (a, e): held.tile([P, PACK * C], BF16, name=f"rounded{a}{e}", tag=f"rounded{a}{e}", align_bytes=MX_ALIGN)
+            (a, e): held.tile([P, PACK * C], BF16, name=f"rounded{a}{e}", align_bytes=MX_ALIGN)
             for a in range(PASSES)
             for e in range(E)
             if (a, e) != (0, 2)
         }
-        first_steps = KT * FIRST // SHORT
-        steps = first_steps + PACK * len(UNITS) - (PACK - 1) + LEAD
         narrow = EARLY - FIRST
         row = narrow + KT * FIRST
         front = (PACK - 1) * row + P
@@ -93,12 +102,13 @@ def tile_moe_bdx_lin_none_kernel(tc, dyT, w_words, w_scales, gate, offs, out):
         for plane in word_scales:
             nc.vector.memset(plane[:].bitcast(I32), 0)
         nc.vector.memset(zeros[:], 0.0)
-        padded_codes = held.tile([P, C], U32, name="padded_codes", align_bytes=MX_ALIGN)
-        padded_scales = held.tile([P, C], U8, name="padded_scales", align_bytes=MX_ALIGN)
-        nc.vector.memset(padded_codes[:, FIRST:C], 0)
-        nc.vector.memset(padded_scales[:, FIRST:C].bitcast(I32), 0)
+        first_codes = held.tile([P, C], U32, name="first_codes", align_bytes=MX_ALIGN)
+        first_scales = held.tile([P, C], U8, name="first_scales", align_bytes=MX_ALIGN)
+        nc.vector.memset(first_codes[:, FIRST:C], 0)
+        nc.vector.memset(first_scales[:, FIRST:C].bitcast(I32), 0)
         nc.vector.memset(codes[1, 0][:, 0:FIRST], 0)
         nc.vector.memset(code_scales[1][:, 0:FIRST].bitcast(I32), 0)
+
         nc.scalar.dma_start(
             gate_cols[:].rearrange("p (h i) -> p h i", h=2), gate[0, :].rearrange("(h p i) -> p h i", h=2, i=RUN)
         )
@@ -106,7 +116,6 @@ def tile_moe_bdx_lin_none_kernel(tc, dyT, w_words, w_scales, gate, offs, out):
         nc.sync.dma_start(offsets[:], offs)
         word_rows = w_words.bitcast(I32).rearrange("e a p b -> p (e a) b")
         scale_rows = w_scales.bitcast(I32).rearrange("e a f k -> f (e a) k")
-        parts = [(0, PASSES), (PASSES, GROUPS)]
 
         def load_words(part):
             lo, hi = parts[part]
@@ -146,7 +155,7 @@ def tile_moe_bdx_lin_none_kernel(tc, dyT, w_words, w_scales, gate, offs, out):
                     )
                 turned[h, g] = bank[:].rearrange("m (i p) -> m p i", i=LINE)
         for g in range(RUN // LINE):
-            nc.scalar.copy(by_run(early_gates[:, 0:HALF], g), turned[0, g])
+            nc.scalar.copy(by_run(early_gates[:], g), turned[0, g])
         for g in range(RUN // LINE):
             nc.scalar.copy(by_run(first_gates[:], g), turned[0, g][:, 0 : FIRST // RUN, :])
         for h in range(2):
@@ -160,31 +169,36 @@ def tile_moe_bdx_lin_none_kernel(tc, dyT, w_words, w_scales, gate, offs, out):
             nc.vector.tensor_tensor(dst, dy[a, t][:].indirect(listed(lo, n)), gates[:, lo : lo + n], MULT)
 
         def interleave(a, lo, n, src):
-            cut = min(n, C - lo % C)
-            for at, m, part in [(lo, cut, src[:, :, 0:cut]), (lo + cut, n - cut, src[:, :, cut:n])][: 1 + (cut < n)]:
-                dst = rounded[a, at // C][:, PACK * (at % C) : PACK * (at % C + m)]
+            here = min(n, C - lo % C)
+            for begin, end in [(0, here), (here, n)] if here < n else [(0, n)]:
+                e, c = divmod(lo + begin, C)
                 nc.scalar.copy(
-                    dst.rearrange("p (c i t) -> p c t i", i=LINE, t=PACK), part.rearrange("p t (c i) -> p c t i", i=LINE)
+                    rounded[a, e][:, PACK * c : PACK * (c + end - begin)].rearrange("p (c i t) -> p c t i", i=LINE, t=PACK),
+                    src[:, :, begin:end].rearrange("p t (c i) -> p c t i", i=LINE),
                 )
 
         def quantise(a, lo, n):
+            e, c = divmod(lo, C)
             nc.vector.quantize_mx(
-                out=codes[a, lo // C][:, lo % C : lo % C + n].bitcast(FP8X4),
+                out=codes[a, e][:, c : c + n].bitcast(FP8X4),
                 scales=code_scales[a][:, lo : lo + n],
-                in_=rounded[a, lo // C][:, PACK * (lo % C) : PACK * (lo % C + n)],
+                in_=rounded[a, e][:, PACK * c : PACK * (c + n)],
             )
 
-        def product(e, kt, banks, padded=False):
-            bank = bank_tile(KT * banks + kt)
-            for a in range(PASSES):
-                part = min(e, 1)
-                w0 = ((e - part) * PASSES + a) * K + P * kt
+        def operands(e):
+            return [(codes[a, e][:], code_scales[a][:, e * C : (e + 1) * C]) for a in range(PASSES)]
+
+        def product(e, kt, bank_set, moving):
+            bank = bank_tile(KT * bank_set + kt)
+            part = min(e, 1)
+            for a, (moving_codes, moving_scales) in enumerate(moving):
+                w0 = (e * PASSES + a - parts[part][0]) * K + P * kt
                 nc.tensor.matmul_mx(
                     out=bank[:],
                     lhsT=words[part][:, 2 * w0 : 2 * (w0 + P)].bitcast(FP4X4),
                     lhsT_scale=word_scales[part][:, w0 : w0 + P],
-                    rhs=(padded_codes[:] if padded and a else codes[a, e][:, 0:C]).bitcast(FP8X4),
-                    rhs_scale=padded_scales[:] if padded and a else code_scales[a][:, e * C : (e + 1) * C],
+                    rhs=moving_codes.bitcast(FP8X4),
+                    rhs_scale=moving_scales,
                     start=(a == 0),
                     stop=(a == PASSES - 1),
                 )
@@ -218,25 +232,27 @@ def tile_moe_bdx_lin_none_kernel(tc, dyT, w_words, w_scales, gate, offs, out):
         for lo in (0, C):
             gather(by_plane(early0[:])[:, PACK - 1, lo : lo + C], 0, PACK - 1, lo, C, early_gates)
             interleave(0, lo, C, by_plane(early0[:])[:, :, lo : lo + C])
+        gates_of_first = [early_gates, early_gates, first_gates, late_gates]
+        heirs = {1: (0, "gates_then_codes"), 2: (1, "first_gates_then_codes")}
         for t in range(PACK):
-            gather(first[:, t * FIRST : (t + 1) * FIRST], 1, t, 0, FIRST, [early_gates, early_gates, first_gates, late_gates][t])
+            gather(first[:, t * FIRST : (t + 1) * FIRST], 1, t, 0, FIRST, gates_of_first[t])
             gather(early1[:, t, 0:narrow], 1, t, FIRST, narrow, late_gates if t else early_gates)
-            if t in (1, 2):
-                tag = ["gates_then_codes", "first_gates_then_codes"][t - 1]
-                codes[0, t - 1] = held.tile([P, C], U32, name=f"codes0{t - 1}", tag=tag, align_bytes=MX_ALIGN)
-                quantise(0, (t - 1) * C, C)
+            if t in heirs:
+                e, tag = heirs[t]
+                codes[0, e] = held.tile([P, C], U32, name=f"codes0{e}", tag=tag, align_bytes=MX_ALIGN)
+                quantise(0, e * C, C)
         interleave(1, 0, FIRST, by_plane(first[:]))
         nc.vector.quantize_mx(
-            out=padded_codes[:, 0:FIRST].bitcast(FP8X4),
-            scales=padded_scales[:, 0:FIRST],
+            out=first_codes[:, 0:FIRST].bitcast(FP8X4),
+            scales=first_scales[:, 0:FIRST],
             in_=rounded[1, 0][:, 0 : PACK * FIRST],
         )
         fill = held.tile([P, PACK * FILL], F32, name="fill", tag="first_then_fill", align_bytes=MX_ALIGN)
         for t in range(PACK):
             gather(fill[:, t * FILL : (t + 1) * FILL], 0, t, HALF, FILL, late_gates)
 
-        def products(e, banks):
-            return [product(e, kt, banks) for kt in range(KT)]
+        def products(e, bank_set):
+            return [product(e, kt, bank_set, operands(e)) for kt in range(KT)]
 
         def spread(banks, e, lo, hi):
             for kt in range(KT):
@@ -249,53 +265,59 @@ def tile_moe_bdx_lin_none_kernel(tc, dyT, w_words, w_scales, gate, offs, out):
             return early1[:, 0, narrow + j * SHORT : narrow + (j + 1) * SHORT]
 
         def first_copy(j):
-            nc.scalar.copy(first_source(j), banks[j % KT][:, j // KT * SHORT : (j // KT + 1) * SHORT])
+            nc.scalar.copy(first_source(j), first_banks[j % KT][:, j // KT * SHORT : (j // KT + 1) * SHORT])
 
-        def piece(lo, n):
+        def interleave_early(lo, n):
             interleave(1, lo, n, early1[:, :, lo - FIRST : lo - FIRST + n])
 
-        banks = [product(0, kt, 0, padded=True) for kt in range(KT)]
-        piece(P, P)
+        first_operands = [operands(0)[0], (first_codes[:], first_scales[:])]
+        first_banks = [product(0, kt, 0, first_operands) for kt in range(KT)]
+        interleave_early(P, P)
         first_copy(0)
-        piece(2 * P, P)
+        interleave_early(2 * P, P)
         first_copy(1)
         first_copy(2)
-        piece(3 * P, P)
+        interleave_early(3 * P, P)
         for j in range(KT, first_steps):
             first_copy(j)
-        piece(C, EARLY - C)
+        interleave_early(C, EARLY - C)
 
-        units, at = [], [HALF + FILL, EARLY]
-        for a, n in UNITS:
-            units.append((a, at[a], n))
-            at[a] = at[a] + n
         woven_slots = steps // KT * SHORT
         left = 3 * C - woven_slots
-        both = early0[:, 0 : left + C]
-        single = [early0[:, HALF + i * C : HALF + (i + 1) * C] for i in range(3)]
-        third = []
+        last_tile = early0[:, 0 : left + C]
+        fourth = [early0[:, HALF + kt * C : HALF + (kt + 1) * C] for kt in range(2)] + [last_tile[:, left : left + C]]
+        left_of_tile0 = early0[:, 2 * HALF : 2 * HALF + left]
+        third_banks = []
 
-        def rest_of_first():
+        def rest_of_expert0():
             quantise(1, FIRST, FIRST)
             quantise(1, 2 * FIRST, C - 2 * FIRST)
             spread(products(0, 1), 0, FIRST, C)
             rounded[0, 2] = held.tile([P, PACK * C], BF16, name="rounded02", tag="codes10", align_bytes=MX_ALIGN)
             interleave(0, HALF, FILL, by_plane(fill[:]))
 
-        def third_products():
+        def expert1():
+            quantise(1, C, C)
+            spread(products(1, 1), 1, 0, C)
+
+        def expert2():
             quantise(0, HALF, C)
             quantise(1, HALF, C)
-            third.extend(products(2, 0))
-            spread(third, 2, 0, C - left)
-            nc.scalar.copy(single[2][:, 0:left], third[0][:, C - left : C])
-            nc.scalar.copy(both[:, 0:left], third[2][:, C - left : C])
+            third_banks.extend(products(2, 0))
+            spread(third_banks, 2, 0, C - left)
+            nc.scalar.copy(left_of_tile0, third_banks[0][:, C - left : C])
+            nc.scalar.copy(last_tile[:, 0:left], third_banks[2][:, C - left : C])
+
+        def pass0_of_expert3():
+            quantise(0, 3 * C, C)
 
         after = {
-            1: rest_of_first,
-            11: lambda: (quantise(1, C, C), spread(products(1, 1), 1, 0, C)),
-            32: third_products,
-            44: lambda: quantise(0, 3 * C, C),
+            1: rest_of_expert0,
+            gathered[0] + PACK - 1: expert1,
+            gathered[2] + PACK: expert2,
+            gathered[3] + PACK: pass0_of_expert3,
         }
+
         def region(j, count=1):
             return woven[:, (j - first_steps) * REGION : (j - first_steps + count) * REGION]
 
@@ -305,7 +327,7 @@ def tile_moe_bdx_lin_none_kernel(tc, dyT, w_words, w_scales, gate, offs, out):
             return by_plane(region(first_steps + PACK * u - (PACK - 1), PACK))
 
         follows = {LEAD + i: i for i in range(PACK - 1)}
-        follows.update({first_steps + LEAD + i: PACK - 1 + i for i in range(steps - first_steps - LEAD)})
+        follows.update({first_steps + LEAD + i: PACK - 1 + i for i in range(owned)})
         for j in range(steps):
             nc.vector.tensor_tensor(
                 outs[j % KT][:].indirect(listed(j // KT * SHORT, SHORT)),
@@ -314,14 +336,14 @@ def tile_moe_bdx_lin_none_kernel(tc, dyT, w_words, w_scales, gate, offs, out):
                 ADD,
             )
             if j in follows:
-                i = follows[j]
-                a, lo, n = units[i // PACK]
-                unit = unit_planes(i // PACK)[:, :, 0:n]
-                gather(unit[:, i % PACK, :], a, i % PACK, lo, n, late_gates)
-                if i % PACK == PACK - 1:
+                u, t = divmod(follows[j], PACK)
+                a, lo, n = units[u]
+                unit = unit_planes(u)[:, :, 0:n]
+                gather(unit[:, t, :], a, t, lo, n, late_gates)
+                if t == PACK - 1:
                     interleave(a, lo, n, unit)
-                if i + 1 in after:
-                    after[i + 1]()
+                if follows[j] + 1 in after:
+                    after[follows[j] + 1]()
 
         def scatter(kt, lo, n, src):
             nc.vector.tensor_copy(outs[kt][:].indirect(listed(lo, n)), src)
@@ -331,15 +353,15 @@ def tile_moe_bdx_lin_none_kernel(tc, dyT, w_words, w_scales, gate, offs, out):
             nc.sync.dma_start(out[rows, 0 : T // 2], outs[kt][:, 0 : T // 2])
             nc.scalar.dma_start(out[rows, T // 2 : T], outs[kt][:, T // 2 : T])
 
-        late = region(steps - LEAD - PACK, PACK)[:, 0:left]
-        nc.scalar.copy(late, third[1][:, C - left : C])
-        scatter(0, woven_slots, left, single[2][:, 0:left])
+        left_of_tile1 = region(first_steps + owned - PACK, PACK)[:, 0:left]
+        nc.scalar.copy(left_of_tile1, third_banks[1][:, C - left : C])
+        scatter(0, woven_slots, left, left_of_tile0)
         quantise(1, 3 * C, C)
-        for kt, dst in enumerate([single[0], single[1], both[:, left : left + C]]):
-            nc.scalar.copy(dst, product(3, kt, 1)[:])
-        scatter(1, woven_slots, left, late)
+        for kt in range(KT):
+            nc.scalar.copy(fourth[kt], product(3, kt, 1, operands(3))[:])
+        scatter(1, woven_slots, left, left_of_tile1)
         for kt in range(2):
-            scatter(kt, 3 * C, C, single[kt])
+            scatter(kt, 3 * C, C, fourth[kt])
             store(kt)
-        scatter(2, woven_slots, left + C, both)
+        scatter(2, woven_slots, left + C, last_tile)
         store(2)

@@ -17,6 +17,7 @@ FP8X4 = mybir.dt.float8_e5m2_x4
 FP4X4 = mybir.dt.float4_e2m1fn_x4
 MULT = mybir.AluOpType.mult
 ADD = mybir.AluOpType.add
+COPY = mybir.ActivationFunctionType.Copy
 
 P = 128
 PACK = 4
@@ -25,25 +26,15 @@ KT = K // P
 GROUPS = E * PASSES
 HALF = 2 * C
 PER_COLUMN = 16
-GRAIN = 2 * PER_COLUMN
-RUN = HALF // P
 LINE = 4
 QUADRANTS = 4
 MX_ALIGN = 64
 
-SHORT = 64
-REGION = 192
-EARLY = 704
-FIRST = 128
-FILL = 160
-LEAD = 2
-
-
-def cut(lo, hi):
-    count = -(-(hi - lo) // REGION)
-    grains, more = divmod((hi - lo) // GRAIN, count)
-    sizes = [GRAIN * (grains + (i < more)) for i in range(count)]
-    return [(lo + sum(sizes[:i]), sizes[i]) for i in range(count)]
+PIECE = 256
+FILL = 128
+SHIFT = 192
+OWN = HALF - SHIFT
+WIDE = 384
 
 
 def tile_moe_bdx_lin_none_kernel(tc, dyT, w_words, w_scales, gate, offs, out):
@@ -55,63 +46,48 @@ def tile_moe_bdx_lin_none_kernel(tc, dyT, w_words, w_scales, gate, offs, out):
         def by_plane(ap):
             return ap.rearrange("p (t s) -> p t s", t=PACK)
 
-        one, two = EARLY + 2 * REGION, EARLY + 5 * REGION
-        stretches = [(1, EARLY, one), (0, HALF + FILL, 3 * C), (1, one, two), (0, 3 * C, T), (1, two, T)]
-        units = [(a, lo, n) for a, begin, end in stretches for lo, n in cut(begin, end)]
-        gathered = [PACK * sum(len(cut(begin, end)) for a, begin, end in stretches[: i + 1]) for i in range(len(stretches))]
-        first_steps = KT * FIRST // SHORT
-        owned = PACK * len(units) - (PACK - 1)
-        steps = -(-(first_steps + owned + LEAD) // KT) * KT
-
         offsets = held.tile([P, T // PER_COLUMN], U16, name="offsets")
         dy = {(a, t): held.tile([P, T], F32, name=f"dy{a}{t}") for a in range(PASSES) for t in range(PACK)}
         parts = [(0, PASSES), (PASSES, GROUPS)]
         words = [held.tile([P, (hi - lo) * 2 * K], U8, name=f"words{lo}", align_bytes=MX_ALIGN) for lo, hi in parts]
         word_scales = [held.tile([P, (hi - lo) * K], U8, name=f"word_scales{lo}", align_bytes=MX_ALIGN) for lo, hi in parts]
         outs = [held.tile([P, T], F32, name=f"outs{kt}") for kt in range(KT)]
-        zeros = held.tile([P, SHORT], F32, name="zeros")
-        early_gates = held.tile([P, HALF], F32, name="early_gates", tag="gates_then_codes", align_bytes=MX_ALIGN)
-        first_gates = held.tile([P, FIRST], F32, name="first_gates", tag="first_gates_then_codes", align_bytes=MX_ALIGN)
-        late_gates = held.tile([P, T], F32, name="late_gates")
-        gate_cols = held.tile([P, 2 * RUN], F32, name="gate_cols")
+        dx = [held.tile([P, T], F32, name=f"dx{kt}") for kt in range(KT)]
+        last = held.tile([P, 2 * C], F32, name="last")
+        gates = held.tile([P, HALF], F32, name="gates")
+        gate_cols = [held.tile([P, 2 * LINE], F32, name=f"gate_cols{h}") for h in range(2)]
         identity = held.tile([P, P], F32, name="identity")
-        code_scales = [held.tile([P, T], U8, name=f"code_scales{a}", align_bytes=MX_ALIGN) for a in range(PASSES)]
+        code_scales = {(a, e): held.tile([P, C], U8, name=f"code_scales{a}{e}", align_bytes=MX_ALIGN) for a in range(PASSES) for e in range(E)}
+        codes = {(a, e): held.tile([P, C], U32, name=f"codes{a}{e}", align_bytes=MX_ALIGN) for a in range(PASSES) for e in range(E)}
         rounded = {
-            (a, e): held.tile([P, PACK * C], BF16, name=f"rounded{a}{e}", align_bytes=MX_ALIGN)
-            for a in range(PASSES)
-            for e in range(E)
-            if (a, e) != (0, 2)
+            at: held.tile([P, PACK * C], BF16, name=f"rounded{at[0]}{at[1]}", align_bytes=MX_ALIGN)
+            for at in [(0, 0), (0, 1), (1, 0), (1, 1), (1, 2), (1, 3)]
         }
-        narrow = EARLY - FIRST
-        row = narrow + KT * FIRST
-        front = (PACK - 1) * row + P
-        planes = held.tile([P, front + (steps - first_steps) * REGION], F32, name="planes")
-        early1 = by_plane(planes[:, 0 : PACK * row])
-        woven = planes[:, front:]
-        regions = woven.rearrange("p (g k c) -> p g k c", k=KT, c=REGION)
-        codes = {
-            (a, e): held.tile([P, C], U32, name=f"codes{a}{e}", tag=f"codes{a}{e}", align_bytes=MX_ALIGN)
-            for a in range(PASSES)
-            for e in range(E)
-            if a or e > 1
+        rounded[0, 2] = rounded[1, 0]
+        rounded[0, 3] = rounded[1, 1]
+        gated0 = held.tile([P, PACK * OWN], F32, name="gated0")
+        gated1 = held.tile([P, (PACK + 1) * C], F32, name="gated1")
+        first_plain = [OWN, HALF]
+        plain = [held.tile([P, PACK * (T - first_plain[a])], F32, name=f"plain{a}") for a in range(PASSES)]
+        planes = {
+            (0, 0): by_plane(gated0[:])[:, :, 0:C],
+            (0, 1): by_plane(gated0[:])[:, :, C:OWN],
+            (1, 0): by_plane(gated1[:, 0 : PACK * C]),
+            (1, 1): by_plane(gated1[:, C : (PACK + 1) * C]),
         }
+        planes.update({(a, e): by_plane(plain[a][:])[:, :, e * C - first_plain[a] : (e + 1) * C - first_plain[a]] for a in range(PASSES) for e in (2, 3)})
 
         dy_rows = dyT.rearrange("(a p t) c -> a t p c", a=PASSES, p=P, t=PACK)
         landing = [(a, t) for a in range(PASSES) for t in range(PACK)]
 
+        warm = held.tile([P, 2], F32, name="warm")
+        nc.vector.memset(warm[:, 0:1], 0.0)
+        nc.scalar.activation(warm[:, 1:2], warm[:, 0:1], COPY)
         for plane in word_scales:
             nc.vector.memset(plane[:].bitcast(I32), 0)
-        nc.vector.memset(zeros[:], 0.0)
-        first_codes = held.tile([P, C], U32, name="first_codes", align_bytes=MX_ALIGN)
-        first_scales = held.tile([P, C], U8, name="first_scales", align_bytes=MX_ALIGN)
-        nc.vector.memset(first_codes[:, FIRST:C], 0)
-        nc.vector.memset(first_scales[:, FIRST:C].bitcast(I32), 0)
-        nc.vector.memset(codes[1, 0][:, 0:FIRST], 0)
-        nc.vector.memset(code_scales[1][:, 0:FIRST].bitcast(I32), 0)
 
-        nc.scalar.dma_start(
-            gate_cols[:].rearrange("p (h i) -> p h i", h=2), gate[0, :].rearrange("(h p i) -> p h i", h=2, i=RUN)
-        )
+        gate_rows = gate[0, :].rearrange("(h e p i) -> h p e i", h=2, e=2, i=LINE)
+        nc.sync.dma_start(gate_cols[0][:].rearrange("p (e i) -> p e i", e=2), gate_rows[0])
         nc.sync.dma_start(dy[landing[0]][:], dy_rows[landing[0]])
         nc.sync.dma_start(offsets[:], offs)
         word_rows = w_words.bitcast(I32).rearrange("e a p b -> p (e a) b")
@@ -129,7 +105,10 @@ def tile_moe_bdx_lin_none_kernel(tc, dyT, w_words, w_scales, gate, offs, out):
                     scale_rows[4 * q : 4 * q + 4, lo:hi, :],
                 )
 
-        for at in landing[1:-1]:
+        for at in landing[1:3]:
+            nc.sync.dma_start(dy[at][:], dy_rows[at])
+        nc.sync.dma_start(gate_cols[1][:].rearrange("p (e i) -> p e i", e=2), gate_rows[1])
+        for at in landing[3:-1]:
             nc.sync.dma_start(dy[at][:], dy_rows[at])
         load_scales(0)
         nc.sync.dma_start(dy[landing[-1]][:], dy_rows[landing[-1]])
@@ -137,231 +116,148 @@ def tile_moe_bdx_lin_none_kernel(tc, dyT, w_words, w_scales, gate, offs, out):
         load_words(1)
         load_scales(1)
 
-        def by_run(ap, g):
-            return ap.rearrange("m (p g i) -> m g p i", g=RUN // LINE, i=LINE)[:, g, :, :]
-
         def bank_tile(b):
             return psum.tile([P, C], F32, name="bank", tag=f"bank{b}")
 
         make_identity(nc, identity[:])
-        turned = {}
-        for h in range(2):
-            for g in range(RUN // LINE):
-                bank = bank_tile(2 * h + g)
-                for i in range(LINE):
-                    col = h * RUN + g * LINE + i
-                    nc.tensor.transpose(
-                        bank[:, i * P : (i + 1) * P], gate_cols[:, col : col + 1].to_broadcast([P, P]), identity[:]
-                    )
-                turned[h, g] = bank[:].rearrange("m (i p) -> m p i", i=LINE)
-        for g in range(RUN // LINE):
-            nc.scalar.copy(by_run(early_gates[:], g), turned[0, g])
-        for g in range(RUN // LINE):
-            nc.scalar.copy(by_run(first_gates[:], g), turned[0, g][:, 0 : FIRST // RUN, :])
-        for h in range(2):
-            for g in range(RUN // LINE):
-                nc.scalar.copy(by_run(late_gates[:, h * HALF : (h + 1) * HALF], g), turned[h, g])
+        gate_banks = {}
+        for e in range(E):
+            bank = bank_tile([0, 1, 6, 7][e])
+            for i in range(LINE):
+                col = e % 2 * LINE + i
+                nc.tensor.transpose(bank[:, i * P : (i + 1) * P], gate_cols[e // 2][:, col : col + 1].to_broadcast([P, P]), identity[:])
+            gate_banks[e] = bank[:].rearrange("m (i c) -> m c i", i=LINE)
+        for e in range(2):
+            nc.vector.tensor_copy(gates[:, e * C : (e + 1) * C].rearrange("m (c i) -> m c i", i=LINE), gate_banks[e])
 
         def listed(lo, n):
             return offsets[:, lo // PER_COLUMN : (lo + n) // PER_COLUMN]
 
-        def gather(dst, a, t, lo, n, gates):
-            nc.vector.tensor_tensor(dst, dy[a, t][:].indirect(listed(lo, n)), gates[:, lo : lo + n], MULT)
+        def window(a, t, lo, n):
+            return dy[a, t][:].indirect(listed(lo, n))
 
-        def interleave(a, lo, n, src):
-            here = min(n, C - lo % C)
-            for begin, end in [(0, here), (here, n)] if here < n else [(0, n)]:
-                e, c = divmod(lo + begin, C)
-                nc.scalar.copy(
-                    rounded[a, e][:, PACK * c : PACK * (c + end - begin)].rearrange("p (c i t) -> p c t i", i=LINE, t=PACK),
-                    src[:, :, begin:end].rearrange("p t (c i) -> p c t i", i=LINE),
-                )
+        def gated_gather(dst, a, t, lo, n):
+            nc.vector.tensor_tensor(dst, window(a, t, lo, n), gates[:, lo : lo + n], MULT)
 
-        def quantise(a, lo, n):
-            e, c = divmod(lo, C)
-            nc.vector.quantize_mx(
-                out=codes[a, e][:, c : c + n].bitcast(FP8X4),
-                scales=code_scales[a][:, lo : lo + n],
-                in_=rounded[a, e][:, PACK * c : PACK * (c + n)],
-            )
+        def walk_out(a, e, lo, n):
+            return rounded[a, e][:, PACK * lo : PACK * (lo + n)].rearrange("p (c i t) -> p c t i", i=LINE, t=PACK)
 
-        def operands(e):
-            return [(codes[a, e][:], code_scales[a][:, e * C : (e + 1) * C]) for a in range(PASSES)]
+        def walk_in(a, e, lo, n):
+            return planes[a, e][:, :, lo : lo + n].rearrange("p t (c i) -> p c t i", i=LINE)
 
-        def product(e, kt, bank_set, moving):
-            bank = bank_tile(KT * bank_set + kt)
+        def interleave(a, e, n=C):
+            nc.vector.tensor_copy(walk_out(a, e, 0, n), walk_in(a, e, 0, n))
+
+        def gate_and_interleave(a, e, lo, n):
+            spread = gate_banks[e][:, lo // LINE : (lo + n) // LINE, :].unsqueeze(2).to_broadcast([P, n // LINE, PACK, LINE])
+            nc.vector.tensor_tensor(walk_out(a, e, lo, n), walk_in(a, e, lo, n), spread, MULT)
+
+        def quantise(a, e):
+            nc.vector.quantize_mx(out=codes[a, e][:].bitcast(FP8X4), scales=code_scales[a, e][:], in_=rounded[a, e][:])
+
+        banks = {}
+
+        def products(e):
             part = min(e, 1)
-            for a, (moving_codes, moving_scales) in enumerate(moving):
-                w0 = (e * PASSES + a - parts[part][0]) * K + P * kt
-                nc.tensor.matmul_mx(
-                    out=bank[:],
-                    lhsT=words[part][:, 2 * w0 : 2 * (w0 + P)].bitcast(FP4X4),
-                    lhsT_scale=word_scales[part][:, w0 : w0 + P],
-                    rhs=moving_codes.bitcast(FP8X4),
-                    rhs_scale=moving_scales,
-                    start=(a == 0),
-                    stop=(a == PASSES - 1),
-                )
-            return bank
-
-        early0 = held.tile([P, PACK * HALF], F32, name="early0")
-        first = held.tile([P, PACK * FIRST], F32, name="first", tag="first_then_fill", align_bytes=MX_ALIGN)
-        nc.vector.tensor_copy(early0[:, 0:HALF], dy[0, 0][:].indirect(listed(0, HALF)))
-        runs = early0[:, 0:HALF].rearrange("m (p i) -> m i p", i=RUN)
-        gated = held.tile([P, HALF], F32, name="gated")
-        for g in range(RUN // LINE):
-            bank = bank_tile(4 + g)
-            for i in range(LINE):
-                nc.tensor.transpose(bank[:, i * P : (i + 1) * P], runs[:, LINE * g + i, :], identity[:])
-            for i in range(LINE):
-                col = LINE * g + i
-                nc.scalar.activation(
-                    gated[:, col * P : (col + 1) * P],
-                    bank[:, i * P : (i + 1) * P],
-                    mybir.ActivationFunctionType.Copy,
-                    scale=gate_cols[:, col : col + 1],
-                )
-        for g in range(RUN // LINE):
-            bank = bank_tile(6 + g)
-            for i in range(LINE):
-                col = LINE * g + i
-                nc.tensor.transpose(bank[:, i * P : (i + 1) * P], gated[:, col * P : (col + 1) * P], identity[:])
-            nc.scalar.copy(by_run(early0[:, 0:HALF], g), bank[:].rearrange("m (i p) -> m p i", i=LINE))
-        for t in range(1, PACK - 1):
-            gather(early0[:, t * HALF : (t + 1) * HALF], 0, t, 0, HALF, early_gates)
-        for lo in (0, C):
-            gather(by_plane(early0[:])[:, PACK - 1, lo : lo + C], 0, PACK - 1, lo, C, early_gates)
-            interleave(0, lo, C, by_plane(early0[:])[:, :, lo : lo + C])
-        gates_of_first = [early_gates, early_gates, first_gates, late_gates]
-        heirs = {1: (0, "gates_then_codes"), 2: (1, "first_gates_then_codes")}
-        for t in range(PACK):
-            gather(first[:, t * FIRST : (t + 1) * FIRST], 1, t, 0, FIRST, gates_of_first[t])
-            gather(early1[:, t, 0:narrow], 1, t, FIRST, narrow, late_gates if t else early_gates)
-            if t in heirs:
-                e, tag = heirs[t]
-                codes[0, e] = held.tile([P, C], U32, name=f"codes0{e}", tag=tag, align_bytes=MX_ALIGN)
-                quantise(0, e * C, C)
-        interleave(1, 0, FIRST, by_plane(first[:]))
-        nc.vector.quantize_mx(
-            out=first_codes[:, 0:FIRST].bitcast(FP8X4),
-            scales=first_scales[:, 0:FIRST],
-            in_=rounded[1, 0][:, 0 : PACK * FIRST],
-        )
-        fill = held.tile([P, PACK * FILL], F32, name="fill", tag="first_then_fill", align_bytes=MX_ALIGN)
-        for t in range(PACK):
-            gather(fill[:, t * FILL : (t + 1) * FILL], 0, t, HALF, FILL, late_gates)
-
-        def products(e, bank_set):
-            return [product(e, kt, bank_set, operands(e)) for kt in range(KT)]
-
-        def spread(banks, e, lo, hi):
             for kt in range(KT):
-                nc.scalar.copy(
-                    regions[:, (e * C + lo - FIRST) // SHORT : (e * C + hi - FIRST) // SHORT, kt, 0:SHORT],
-                    banks[kt][:, lo:hi].rearrange("p (g c) -> p g c", c=SHORT),
-                )
+                banks[e, kt] = bank_tile(KT * (e % 2) + kt)
+                for a in range(PASSES):
+                    w0 = (e * PASSES + a - parts[part][0]) * K + P * kt
+                    nc.tensor.matmul_mx(
+                        out=banks[e, kt][:],
+                        lhsT=words[part][:, 2 * w0 : 2 * (w0 + P)].bitcast(FP4X4),
+                        lhsT_scale=word_scales[part][:, w0 : w0 + P],
+                        rhs=codes[a, e][:].bitcast(FP8X4),
+                        rhs_scale=code_scales[a, e][:],
+                        start=(a == 0),
+                        stop=(a == PASSES - 1),
+                    )
 
-        def first_source(j):
-            return early1[:, 0, narrow + j * SHORT : narrow + (j + 1) * SHORT]
+        def scalar_share(e):
+            for kt in (1, 2, 0):
+                nc.scalar.copy(dx[kt][:, e * C : (e + 1) * C], banks[e, kt][:])
+            for lo in range(e * C, (e + 1) * C, PIECE):
+                for kt in (1, 2):
+                    nc.scalar.activation(outs[kt][:].indirect(listed(lo, PIECE)), dx[kt][:, lo : lo + PIECE], COPY)
 
-        def first_copy(j):
-            nc.scalar.copy(first_source(j), first_banks[j % KT][:, j // KT * SHORT : (j // KT + 1) * SHORT])
+        def scalar_scatter(kt, lo, n, src):
+            nc.scalar.activation(outs[kt][:].indirect(listed(lo, n)), src, COPY)
 
-        def interleave_early(lo, n):
-            interleave(1, lo, n, early1[:, :, lo - FIRST : lo - FIRST + n])
+        def third_share():
+            lo = 2 * C
+            nc.scalar.copy(dx[1][:, lo : lo + C], banks[2, 1][:])
+            nc.scalar.copy(dx[2][:, lo : lo + PIECE], banks[2, 2][:, 0:PIECE])
+            scalar_scatter(1, lo, PIECE, dx[1][:, lo : lo + PIECE])
+            scalar_scatter(2, lo, PIECE, dx[2][:, lo : lo + PIECE])
+            scalar_scatter(1, lo + PIECE, PIECE, dx[1][:, lo + PIECE : lo + C])
 
-        first_operands = [operands(0)[0], (first_codes[:], first_scales[:])]
-        first_banks = [product(0, kt, 0, first_operands) for kt in range(KT)]
-        interleave_early(P, P)
-        first_copy(0)
-        interleave_early(2 * P, P)
-        first_copy(1)
-        first_copy(2)
-        interleave_early(3 * P, P)
-        for j in range(KT, first_steps):
-            first_copy(j)
-        interleave_early(C, EARLY - C)
+        def last_share():
+            lo = 3 * C
+            nc.scalar.copy(last[:, 0:C], banks[3, 1][:])
+            nc.scalar.copy(last[:, C : 2 * C], banks[3, 2][:])
+            scalar_scatter(1, lo + PIECE, PIECE, last[:, PIECE:C])
+            nc.scalar.copy(last[:, PIECE:C], banks[2, 2][:, PIECE:C])
+            scalar_scatter(1, lo, PIECE, last[:, 0:PIECE])
+            for i in range(2):
+                scalar_scatter(2, lo - PIECE + i * WIDE, WIDE, last[:, PIECE + i * WIDE : PIECE + (i + 1) * WIDE])
 
-        woven_slots = steps // KT * SHORT
-        left = 3 * C - woven_slots
-        last_tile = early0[:, 0 : left + C]
-        fourth = [early0[:, HALF + kt * C : HALF + (kt + 1) * C] for kt in range(2)] + [last_tile[:, left : left + C]]
-        left_of_tile0 = early0[:, 2 * HALF : 2 * HALF + left]
-        third_banks = []
+        def vector_copy(e):
+            nc.vector.tensor_copy(dx[0][:, e * C : (e + 1) * C], banks[e, 0][:])
 
-        def rest_of_expert0():
-            quantise(1, FIRST, FIRST)
-            quantise(1, 2 * FIRST, C - 2 * FIRST)
-            spread(products(0, 1), 0, FIRST, C)
-            rounded[0, 2] = held.tile([P, PACK * C], BF16, name="rounded02", tag="codes10", align_bytes=MX_ALIGN)
-            interleave(0, HALF, FILL, by_plane(fill[:]))
-
-        def expert1():
-            quantise(1, C, C)
-            spread(products(1, 1), 1, 0, C)
-
-        def expert2():
-            quantise(0, HALF, C)
-            quantise(1, HALF, C)
-            third_banks.extend(products(2, 0))
-            spread(third_banks, 2, 0, C - left)
-            nc.scalar.copy(left_of_tile0, third_banks[0][:, C - left : C])
-            nc.scalar.copy(last_tile[:, 0:left], third_banks[2][:, C - left : C])
-
-        def pass0_of_expert3():
-            quantise(0, 3 * C, C)
-
-        after = {
-            1: rest_of_expert0,
-            gathered[0] + PACK - 1: expert1,
-            gathered[2] + PACK: expert2,
-            gathered[3] + PACK: pass0_of_expert3,
-        }
-
-        def region(j, count=1):
-            return woven[:, (j - first_steps) * REGION : (j - first_steps + count) * REGION]
-
-        def unit_planes(u):
-            if u == 0:
-                return early1[:, :, P : P + REGION]
-            return by_plane(region(first_steps + PACK * u - (PACK - 1), PACK))
-
-        follows = {LEAD + i: i for i in range(PACK - 1)}
-        follows.update({first_steps + LEAD + i: PACK - 1 + i for i in range(owned)})
-        for j in range(steps):
-            nc.vector.tensor_tensor(
-                outs[j % KT][:].indirect(listed(j // KT * SHORT, SHORT)),
-                first_source(j) if j < first_steps else region(j)[:, 0:SHORT],
-                zeros[:],
-                ADD,
-            )
-            if j in follows:
-                u, t = divmod(follows[j], PACK)
-                a, lo, n = units[u]
-                unit = unit_planes(u)[:, :, 0:n]
-                gather(unit[:, t, :], a, t, lo, n, late_gates)
-                if t == PACK - 1:
-                    interleave(a, lo, n, unit)
-                if follows[j] + 1 in after:
-                    after[follows[j] + 1]()
-
-        def scatter(kt, lo, n, src):
-            nc.vector.tensor_copy(outs[kt][:].indirect(listed(lo, n)), src)
-
-        def store(kt):
-            rows = slice(kt * P, (kt + 1) * P)
-            nc.sync.dma_start(out[rows, 0 : T // 2], outs[kt][:, 0 : T // 2])
-            nc.scalar.dma_start(out[rows, T // 2 : T], outs[kt][:, T // 2 : T])
-
-        left_of_tile1 = region(first_steps + owned - PACK, PACK)[:, 0:left]
-        nc.scalar.copy(left_of_tile1, third_banks[1][:, C - left : C])
-        scatter(0, woven_slots, left, left_of_tile0)
-        quantise(1, 3 * C, C)
-        for kt in range(KT):
-            nc.scalar.copy(fourth[kt], product(3, kt, 1, operands(3))[:])
-        scatter(1, woven_slots, left, left_of_tile1)
-        for kt in range(2):
-            scatter(kt, 3 * C, C, fourth[kt])
-            store(kt)
-        scatter(2, woven_slots, left + C, last_tile)
-        store(2)
+        for a, t in landing:
+            if (a, t) == (0, PACK - 1):
+                nc.scalar.activation(by_plane(plain[a][:])[:, t, 0:SHIFT], window(a, t, OWN, SHIFT), COPY)
+                nc.scalar.activation(by_plane(plain[a][:])[:, t, SHIFT:], window(a, t, HALF, HALF), COPY)
+            else:
+                nc.scalar.activation(by_plane(plain[a][:])[:, t, :], window(a, t, first_plain[a], T - first_plain[a]), COPY)
+        for t in range(PACK - 1):
+            gated_gather(gated0[:, t * OWN : (t + 1) * OWN], 0, t, 0, OWN)
+        gated_gather(planes[0, 0][:, PACK - 1, :], 0, PACK - 1, 0, C)
+        gated_gather(planes[0, 1][:, PACK - 1, :], 0, PACK - 1, C, OWN - C)
+        interleave(0, 0)
+        interleave(0, 1, OWN - C)
+        nc.vector.tensor_tensor(
+            walk_out(0, 1, OWN - C, SHIFT),
+            by_plane(plain[0][:])[:, :, 0:SHIFT].rearrange("p t (c i) -> p c t i", i=LINE),
+            gates[:, OWN:HALF].rearrange("p (c i) -> p c i", i=LINE).unsqueeze(2).to_broadcast([P, SHIFT // LINE, PACK, LINE]),
+            MULT,
+        )
+        quantise(0, 0)
+        gated_gather(planes[1, 0][:, 0, :], 1, 0, 0, C)
+        quantise(0, 1)
+        for t in range(1, PACK):
+            gated_gather(planes[1, 0][:, t, :], 1, t, 0, C)
+        gated_gather(planes[1, 1][:, PACK - 1, 0:FILL], 1, PACK - 1, C, FILL)
+        interleave(1, 0)
+        gated_gather(planes[1, 1][:, PACK - 1, FILL : 2 * FILL], 1, PACK - 1, C + FILL, FILL)
+        quantise(1, 0)
+        products(0)
+        scalar_share(0)
+        gated_gather(planes[1, 1][:, PACK - 1, 2 * FILL : C], 1, PACK - 1, C + 2 * FILL, C - 2 * FILL)
+        for t in range(PACK - 1):
+            gated_gather(planes[1, 1][:, t, :], 1, t, C, C)
+        interleave(1, 1)
+        gate_and_interleave(0, 2, 0, C // 2)
+        quantise(1, 1)
+        products(1)
+        scalar_share(1)
+        gate_and_interleave(0, 2, C // 2, C // 2)
+        gate_and_interleave(1, 2, 0, C)
+        quantise(0, 2)
+        quantise(1, 2)
+        products(2)
+        third_share()
+        gate_and_interleave(0, 3, 0, C)
+        gate_and_interleave(1, 3, 0, C)
+        quantise(0, 3)
+        vector_copy(2)
+        quantise(1, 3)
+        products(3)
+        last_share()
+        nc.vector.tensor_copy(outs[0][:].indirect(listed(0, 3 * C // 2)), dx[0][:, 0 : 3 * C // 2])
+        vector_copy(3)
+        nc.vector.tensor_copy(outs[0][:].indirect(listed(3 * C // 2, T - 3 * C // 2)), dx[0][:, 3 * C // 2 : T])
+        nc.scalar.dma_start(out[P : 2 * P, :], outs[1][:])
+        nc.sync.dma_start(out[0:P, :], outs[0][:])
+        nc.sync.dma_start(out[2 * P : 3 * P, 0 : T // 2], outs[2][:, 0 : T // 2])
+        nc.scalar.dma_start(out[2 * P : 3 * P, T // 2 : T], outs[2][:, T // 2 : T])

@@ -30,11 +30,13 @@ LINE = 4
 QUADRANTS = 4
 MX_ALIGN = 64
 
-PIECE = 256
-FILL = 128
-SHIFT = 192
-OWN = HALF - SHIFT
-WIDE = 384
+U = 256
+PLAIN = [HALF, HALF]
+SHORT = 64
+WOVEN = [192, 192, 192, 192]
+REGION = max(WOVEN)
+ORDER = [7, 0, 1, 2, 3, 4, 5, 6]
+RING = 3
 
 
 def tile_moe_bdx_lin_none_kernel(tc, dyT, w_words, w_scales, gate, offs, out):
@@ -48,46 +50,39 @@ def tile_moe_bdx_lin_none_kernel(tc, dyT, w_words, w_scales, gate, offs, out):
 
         offsets = held.tile([P, T // PER_COLUMN], U16, name="offsets")
         dy = {(a, t): held.tile([P, T], F32, name=f"dy{a}{t}") for a in range(PASSES) for t in range(PACK)}
-        parts = [(0, PASSES), (PASSES, GROUPS)]
+        parts = [(GROUPS - PASSES, GROUPS), (0, GROUPS - PASSES)]
         words = [held.tile([P, (hi - lo) * 2 * K], U8, name=f"words{lo}", align_bytes=MX_ALIGN) for lo, hi in parts]
         word_scales = [held.tile([P, (hi - lo) * K], U8, name=f"word_scales{lo}", align_bytes=MX_ALIGN) for lo, hi in parts]
         outs = [held.tile([P, T], F32, name=f"outs{kt}") for kt in range(KT)]
-        dx = [held.tile([P, T], F32, name=f"dx{kt}") for kt in range(KT)]
-        last = held.tile([P, 2 * C], F32, name="last")
-        gates = held.tile([P, HALF], F32, name="gates")
         gate_cols = [held.tile([P, 2 * LINE], F32, name=f"gate_cols{h}") for h in range(2)]
         identity = held.tile([P, P], F32, name="identity")
-        code_scales = {(a, e): held.tile([P, C], U8, name=f"code_scales{a}{e}", align_bytes=MX_ALIGN) for a in range(PASSES) for e in range(E)}
-        codes = {(a, e): held.tile([P, C], U32, name=f"codes{a}{e}", align_bytes=MX_ALIGN) for a in range(PASSES) for e in range(E)}
-        rounded = {
-            at: held.tile([P, PACK * C], BF16, name=f"rounded{at[0]}{at[1]}", align_bytes=MX_ALIGN)
-            for at in [(0, 0), (0, 1), (1, 0), (1, 1), (1, 2), (1, 3)]
-        }
-        rounded[0, 2] = rounded[1, 0]
-        rounded[0, 3] = rounded[1, 1]
-        gated0 = held.tile([P, PACK * OWN], F32, name="gated0")
-        gated1 = held.tile([P, (PACK + 1) * C], F32, name="gated1")
-        first_plain = [OWN, HALF]
-        plain = [held.tile([P, PACK * (T - first_plain[a])], F32, name=f"plain{a}") for a in range(PASSES)]
-        planes = {
-            (0, 0): by_plane(gated0[:])[:, :, 0:C],
-            (0, 1): by_plane(gated0[:])[:, :, C:OWN],
-            (1, 0): by_plane(gated1[:, 0 : PACK * C]),
-            (1, 1): by_plane(gated1[:, C : (PACK + 1) * C]),
-        }
-        planes.update({(a, e): by_plane(plain[a][:])[:, :, e * C - first_plain[a] : (e + 1) * C - first_plain[a]] for a in range(PASSES) for e in (2, 3)})
+        zeros = held.tile([P, SHORT], F32, name="zeros")
+        code_scales = [held.tile([P, T], U8, name=f"code_scales{a}", align_bytes=MX_ALIGN) for a in range(PASSES)]
+        codes = [held.tile([P, T], U32, name=f"codes{a}", align_bytes=MX_ALIGN) for a in range(PASSES)]
+        rounded0 = held.tile([P, PACK * T], BF16, name="rounded0", align_bytes=MX_ALIGN)
+        late = held.tile([P, 2 * sum(WOVEN) + 4 * U], F32, name="late", align_bytes=MX_ALIGN)
+        rounded1 = late[:, 0 : 2 * sum(WOVEN)].bitcast(BF16)
+        tail = late[:, 2 * sum(WOVEN) - U :]
+        gated0 = held.tile([P, PACK * HALF], F32, name="gated0")
+        gates = held.tile([P, HALF], F32, name="gates")
+        first1 = held.tile([P, PACK * U], F32, name="first1")
+        plain0 = held.tile([P, PACK * PLAIN[0]], F32, name="plain0")
+        plain1 = held.tile([P, PACK * PLAIN[1]], F32, name="plain1")
+        steps = PACK * len(WOVEN) + 1
+        regions = held.tile([P, steps * REGION], F32, name="regions")
+        staged = held.tile([P, RING * 2 * U], F32, name="staged")
 
         dy_rows = dyT.rearrange("(a p t) c -> a t p c", a=PASSES, p=P, t=PACK)
         landing = [(a, t) for a in range(PASSES) for t in range(PACK)]
 
-        warm = held.tile([P, 2], F32, name="warm")
-        nc.vector.memset(warm[:, 0:1], 0.0)
-        nc.scalar.activation(warm[:, 1:2], warm[:, 0:1], COPY)
+        warm = held.tile([P, 1], F32, name="warm")
+        nc.vector.memset(zeros[:], 0.0)
+        nc.scalar.activation(warm[:], zeros[:, 0:1], COPY)
         for plane in word_scales:
             nc.vector.memset(plane[:].bitcast(I32), 0)
 
         gate_rows = gate[0, :].rearrange("(h e p i) -> h p e i", h=2, e=2, i=LINE)
-        nc.sync.dma_start(gate_cols[0][:].rearrange("p (e i) -> p e i", e=2), gate_rows[0])
+        nc.sync.dma_start(gate_cols[1][:].rearrange("p (e i) -> p e i", e=2), gate_rows[1])
         nc.sync.dma_start(dy[landing[0]][:], dy_rows[landing[0]])
         nc.sync.dma_start(offsets[:], offs)
         word_rows = w_words.bitcast(I32).rearrange("e a p b -> p (e a) b")
@@ -107,7 +102,7 @@ def tile_moe_bdx_lin_none_kernel(tc, dyT, w_words, w_scales, gate, offs, out):
 
         for at in landing[1:3]:
             nc.sync.dma_start(dy[at][:], dy_rows[at])
-        nc.sync.dma_start(gate_cols[1][:].rearrange("p (e i) -> p e i", e=2), gate_rows[1])
+        nc.sync.dma_start(gate_cols[0][:].rearrange("p (e i) -> p e i", e=2), gate_rows[0])
         for at in landing[3:-1]:
             nc.sync.dma_start(dy[at][:], dy_rows[at])
         load_scales(0)
@@ -121,14 +116,25 @@ def tile_moe_bdx_lin_none_kernel(tc, dyT, w_words, w_scales, gate, offs, out):
 
         make_identity(nc, identity[:])
         gate_banks = {}
-        for e in range(E):
-            bank = bank_tile([0, 1, 6, 7][e])
+        for e in reversed(range(E)):
+            bank = bank_tile([6, 7, 0, 1][e])
             for i in range(LINE):
                 col = e % 2 * LINE + i
                 nc.tensor.transpose(bank[:, i * P : (i + 1) * P], gate_cols[e // 2][:, col : col + 1].to_broadcast([P, P]), identity[:])
             gate_banks[e] = bank[:].rearrange("m (i c) -> m c i", i=LINE)
-        for e in range(2):
-            nc.vector.tensor_copy(gates[:, e * C : (e + 1) * C].rearrange("m (c i) -> m c i", i=LINE), gate_banks[e])
+
+        def gate_row(lo, n):
+            return gates[:, lo - PLAIN[1] : lo - PLAIN[1] + n]
+
+        def banked_gates(lo, n):
+            e, c = divmod(lo, C)
+            return gate_banks[e][:, c // LINE : (c + n) // LINE, :]
+
+        def copy_gates(lo, hi):
+            nc.vector.tensor_copy(gate_row(lo, hi - lo).rearrange("m (c i) -> m c i", i=LINE), banked_gates(lo, hi - lo))
+
+        copy_gates(3 * C, T)
+        copy_gates(HALF, 3 * C)
 
         def listed(lo, n):
             return offsets[:, lo // PER_COLUMN : (lo + n) // PER_COLUMN]
@@ -137,127 +143,189 @@ def tile_moe_bdx_lin_none_kernel(tc, dyT, w_words, w_scales, gate, offs, out):
             return dy[a, t][:].indirect(listed(lo, n))
 
         def gated_gather(dst, a, t, lo, n):
-            nc.vector.tensor_tensor(dst, window(a, t, lo, n), gates[:, lo : lo + n], MULT)
+            nc.vector.tensor_tensor(dst, window(a, t, lo, n), gate_row(lo, n), MULT)
 
-        def walk_out(a, e, lo, n):
-            return rounded[a, e][:, PACK * lo : PACK * (lo + n)].rearrange("p (c i t) -> p c t i", i=LINE, t=PACK)
+        def plain_gather(dst, a, t, lo, n):
+            nc.scalar.activation(dst, window(a, t, lo, n), COPY)
 
-        def walk_in(a, e, lo, n):
-            return planes[a, e][:, :, lo : lo + n].rearrange("p t (c i) -> p c t i", i=LINE)
+        def walk_out(tile, at, n):
+            return tile[:, PACK * at : PACK * (at + n)].rearrange("p (c i t) -> p c t i", i=LINE, t=PACK)
 
-        def interleave(a, e, n=C):
-            nc.vector.tensor_copy(walk_out(a, e, 0, n), walk_in(a, e, 0, n))
+        def walk_in(src):
+            return src.rearrange("p t (c i) -> p c t i", i=LINE)
 
-        def gate_and_interleave(a, e, lo, n):
-            spread = gate_banks[e][:, lo // LINE : (lo + n) // LINE, :].unsqueeze(2).to_broadcast([P, n // LINE, PACK, LINE])
-            nc.vector.tensor_tensor(walk_out(a, e, lo, n), walk_in(a, e, lo, n), spread, MULT)
+        def interleave(tile, at, src):
+            nc.vector.tensor_copy(walk_out(tile, at, src.shape[2]), walk_in(src))
 
-        def quantise(a, e):
-            nc.vector.quantize_mx(out=codes[a, e][:].bitcast(FP8X4), scales=code_scales[a, e][:], in_=rounded[a, e][:])
+        def gate_and_interleave(tile, at, src, lo):
+            n = src.shape[2]
+            row = banked_gates(lo, n) if lo < HALF else gate_row(lo, n).rearrange("p (c i) -> p c i", i=LINE)
+            nc.vector.tensor_tensor(walk_out(tile, at, n), walk_in(src), row.unsqueeze(2).to_broadcast([P, n // LINE, PACK, LINE]), MULT)
 
-        banks = {}
+        def quantise(a, lo, n, tile, at):
+            nc.vector.quantize_mx(
+                out=codes[a][:, lo : lo + n].bitcast(FP8X4),
+                scales=code_scales[a][:, lo : lo + n],
+                in_=tile[:, PACK * at : PACK * (at + n)],
+            )
 
-        def products(e):
-            part = min(e, 1)
-            for kt in range(KT):
-                banks[e, kt] = bank_tile(KT * (e % 2) + kt)
-                for a in range(PASSES):
-                    w0 = (e * PASSES + a - parts[part][0]) * K + P * kt
-                    nc.tensor.matmul_mx(
-                        out=banks[e, kt][:],
-                        lhsT=words[part][:, 2 * w0 : 2 * (w0 + P)].bitcast(FP4X4),
-                        lhsT_scale=word_scales[part][:, w0 : w0 + P],
-                        rhs=codes[a, e][:].bitcast(FP8X4),
-                        rhs_scale=code_scales[a, e][:],
-                        start=(a == 0),
-                        stop=(a == PASSES - 1),
-                    )
+        def product(dst, u, kt):
+            e = u * U // C
+            part = 0 if e == E - 1 else 1
+            for a in range(PASSES):
+                w0 = (e * PASSES + a - parts[part][0]) * K + P * kt
+                nc.tensor.matmul_mx(
+                    out=dst,
+                    lhsT=words[part][:, 2 * w0 : 2 * (w0 + P)].bitcast(FP4X4),
+                    lhsT_scale=word_scales[part][:, w0 : w0 + P],
+                    rhs=codes[a][:, u * U : (u + 1) * U].bitcast(FP8X4),
+                    rhs_scale=code_scales[a][:, u * U : (u + 1) * U],
+                    start=(a == 0),
+                    stop=(a == PASSES - 1),
+                )
 
-        def scalar_share(e):
-            for kt in (1, 2, 0):
-                nc.scalar.copy(dx[kt][:, e * C : (e + 1) * C], banks[e, kt][:])
-            for lo in range(e * C, (e + 1) * C, PIECE):
-                for kt in (1, 2):
-                    nc.scalar.activation(outs[kt][:].indirect(listed(lo, PIECE)), dx[kt][:, lo : lo + PIECE], COPY)
+        pair_bank, first_bank = {}, {}
+
+        def products(k):
+            pair_bank[k] = bank_tile(k % RING)
+            product(pair_bank[k][:, 0:U], ORDER[k], 1)
+            if k != 6:
+                product(pair_bank[k][:, U : 2 * U], ORDER[min(k, 6)], 2)
+            first_bank[k] = bank_tile(6 if k == 7 else RING + k % RING)
+            product(first_bank[k][:, 0:U], ORDER[k], 0)
+            if k == 7:
+                product(first_bank[k][:, U : 2 * U], ORDER[k], 2)
 
         def scalar_scatter(kt, lo, n, src):
             nc.scalar.activation(outs[kt][:].indirect(listed(lo, n)), src, COPY)
 
-        def third_share():
-            lo = 2 * C
-            nc.scalar.copy(dx[1][:, lo : lo + C], banks[2, 1][:])
-            nc.scalar.copy(dx[2][:, lo : lo + PIECE], banks[2, 2][:, 0:PIECE])
-            scalar_scatter(1, lo, PIECE, dx[1][:, lo : lo + PIECE])
-            scalar_scatter(2, lo, PIECE, dx[2][:, lo : lo + PIECE])
-            scalar_scatter(1, lo + PIECE, PIECE, dx[1][:, lo + PIECE : lo + C])
-
-        def last_share():
-            lo = 3 * C
-            nc.scalar.copy(last[:, 0:C], banks[3, 1][:])
-            nc.scalar.copy(last[:, C : 2 * C], banks[3, 2][:])
-            scalar_scatter(1, lo + PIECE, PIECE, last[:, PIECE:C])
-            nc.scalar.copy(last[:, PIECE:C], banks[2, 2][:, PIECE:C])
-            scalar_scatter(1, lo, PIECE, last[:, 0:PIECE])
+        def scalar_share(k):
+            room = staged[:, k % RING * 2 * U : (k % RING + 1) * 2 * U]
             for i in range(2):
-                scalar_scatter(2, lo - PIECE + i * WIDE, WIDE, last[:, PIECE + i * WIDE : PIECE + (i + 1) * WIDE])
+                nc.scalar.copy(room[:, i * U : (i + 1) * U], pair_bank[k][:, i * U : (i + 1) * U])
+            for i in range(2):
+                scalar_scatter(1 + i, ORDER[k] * U, U, room[:, i * U : (i + 1) * U])
 
-        def vector_copy(e):
-            nc.vector.tensor_copy(dx[0][:, e * C : (e + 1) * C], banks[e, 0][:])
+        heads = regions[:].rearrange("p (j c) -> p j c", c=REGION)
 
-        for a, t in landing:
-            if (a, t) == (0, PACK - 1):
-                nc.scalar.activation(by_plane(plain[a][:])[:, t, 0:SHIFT], window(a, t, OWN, SHIFT), COPY)
-                nc.scalar.activation(by_plane(plain[a][:])[:, t, SHIFT:], window(a, t, HALF, HALF), COPY)
-            else:
-                nc.scalar.activation(by_plane(plain[a][:])[:, t, :], window(a, t, first_plain[a], T - first_plain[a]), COPY)
+        def spread(k, count=PACK):
+            nc.vector.tensor_copy(
+                heads[:, PACK * k : PACK * k + count, 0:SHORT], first_bank[k][:, 0 : count * SHORT].rearrange("p (j c) -> p j c", c=SHORT)
+            )
+
+        starts = [PLAIN[1] + sum(WOVEN[:w]) for w in range(len(WOVEN))]
+
+        def step(j):
+            k, i = divmod(j, PACK)
+            nc.vector.tensor_tensor(outs[0][:].indirect(listed(ORDER[k] * U + i * SHORT, SHORT)), heads[:, j, 0:SHORT], zeros[:], ADD)
+            if j:
+                w, t = divmod(j - 1, PACK)
+                gated_gather(heads[:, j - 1, 0 : WOVEN[w]], 1, t, starts[w], WOVEN[w])
+
+        def woven_interleave(w):
+            interleave(rounded1, starts[w] - PLAIN[1], heads[:, PACK * w : PACK * (w + 1), 0 : WOVEN[w]])
+
+        p0, p1 = by_plane(plain0[:]), by_plane(plain1[:])
+        for a, planes in enumerate([p0, p1]):
+            for t in range(PACK - 1):
+                plain_gather(planes[:, t, :], a, t, 0, PLAIN[a])
+            for lo, hi in [(0, C), (C, PLAIN[a])]:
+                plain_gather(planes[:, PACK - 1, lo:hi], a, PACK - 1, lo, hi - lo)
+        g0, f1 = by_plane(gated0[:]), by_plane(first1[:])
+        first = T - U
         for t in range(PACK - 1):
-            gated_gather(gated0[:, t * OWN : (t + 1) * OWN], 0, t, 0, OWN)
-        gated_gather(planes[0, 0][:, PACK - 1, :], 0, PACK - 1, 0, C)
-        gated_gather(planes[0, 1][:, PACK - 1, :], 0, PACK - 1, C, OWN - C)
-        interleave(0, 0)
-        interleave(0, 1, OWN - C)
-        nc.vector.tensor_tensor(
-            walk_out(0, 1, OWN - C, SHIFT),
-            by_plane(plain[0][:])[:, :, 0:SHIFT].rearrange("p t (c i) -> p c t i", i=LINE),
-            gates[:, OWN:HALF].rearrange("p (c i) -> p c i", i=LINE).unsqueeze(2).to_broadcast([P, SHIFT // LINE, PACK, LINE]),
-            MULT,
-        )
-        quantise(0, 0)
-        gated_gather(planes[1, 0][:, 0, :], 1, 0, 0, C)
-        quantise(0, 1)
-        for t in range(1, PACK):
-            gated_gather(planes[1, 0][:, t, :], 1, t, 0, C)
-        gated_gather(planes[1, 1][:, PACK - 1, 0:FILL], 1, PACK - 1, C, FILL)
-        interleave(1, 0)
-        gated_gather(planes[1, 1][:, PACK - 1, FILL : 2 * FILL], 1, PACK - 1, C + FILL, FILL)
-        quantise(1, 0)
+            gated_gather(g0[:, t, :], 0, t, PLAIN[0], T - PLAIN[0])
+        gated_gather(g0[:, PACK - 1, C:], 0, PACK - 1, 3 * C, C)
+        gated_gather(g0[:, PACK - 1, 0:C], 0, PACK - 1, HALF, C)
+        interleave(rounded0, 3 * C, g0[:, :, C:])
+        gated_gather(f1[:, 0, :], 1, 0, first, U)
+        quantise(0, 3 * C, C, rounded0, 3 * C)
+        gate_and_interleave(rounded0, 0, p0[:, :, 0:C], 0)
+        gated_gather(f1[:, 1, :], 1, 1, first, U)
+        quantise(0, 0, C, rounded0, 0)
+        gated_gather(f1[:, 2, :], 1, 2, first, U)
+        for h in range(2):
+            gated_gather(f1[:, 3, h * P : (h + 1) * P], 1, 3, first + h * P, P)
+        room_a, room_b, room_c = 2 * U, 3 * U, 4 * U
+        astride = [room_b - P // 2, room_c - P // 2]
+        for h in range(2):
+            interleave(rounded0, astride[h], f1[:, :, h * P : (h + 1) * P])
+        for h in range(2):
+            quantise(1, first + h * P, P, rounded0, astride[h])
         products(0)
         scalar_share(0)
-        gated_gather(planes[1, 1][:, PACK - 1, 2 * FILL : C], 1, PACK - 1, C + 2 * FILL, C - 2 * FILL)
-        for t in range(PACK - 1):
-            gated_gather(planes[1, 1][:, t, :], 1, t, C, C)
-        interleave(1, 1)
-        gate_and_interleave(0, 2, 0, C // 2)
-        quantise(1, 1)
-        products(1)
+
+        def plain_unit(k, room):
+            lo = ORDER[k] * U
+            gate_and_interleave(rounded0, room, p1[:, :, lo : lo + U], lo)
+
+        def finish(k, tile, at):
+            quantise(1, ORDER[k] * U, U, tile, at)
+            products(k)
+
+        def run(lo, hi):
+            for j in range(lo, hi):
+                step(j)
+
+        def plain_pass0(room):
+            gate_and_interleave(rounded0, room, p0[:, :, room : room + U], room)
+
+        def keep(k, lo=0):
+            nc.vector.tensor_copy(tail[:, (k - 4) * U + lo : (k - 3) * U], first_bank[k][:, lo:U])
+
+        plain_unit(1, room_b)
+        spread(0)
+        finish(1, rounded0, room_b)
         scalar_share(1)
-        gate_and_interleave(0, 2, C // 2, C // 2)
-        gate_and_interleave(1, 2, 0, C)
-        quantise(0, 2)
-        quantise(1, 2)
-        products(2)
-        third_share()
-        gate_and_interleave(0, 3, 0, C)
-        gate_and_interleave(1, 3, 0, C)
-        quantise(0, 3)
-        vector_copy(2)
-        quantise(1, 3)
-        products(3)
-        last_share()
-        nc.vector.tensor_copy(outs[0][:].indirect(listed(0, 3 * C // 2)), dx[0][:, 0 : 3 * C // 2])
-        vector_copy(3)
-        nc.vector.tensor_copy(outs[0][:].indirect(listed(3 * C // 2, T - 3 * C // 2)), dx[0][:, 3 * C // 2 : T])
-        nc.scalar.dma_start(out[P : 2 * P, :], outs[1][:])
-        nc.sync.dma_start(out[0:P, :], outs[0][:])
-        nc.sync.dma_start(out[2 * P : 3 * P, 0 : T // 2], outs[2][:, 0 : T // 2])
-        nc.scalar.dma_start(out[2 * P : 3 * P, T // 2 : T], outs[2][:, T // 2 : T])
+        run(0, 4)
+        plain_unit(2, room_a)
+        spread(1)
+        finish(2, rounded0, room_a)
+        scalar_share(2)
+        run(4, 7)
+        plain_pass0(room_a)
+        plain_unit(3, room_b)
+        quantise(0, room_a, U, rounded0, room_a)
+        spread(2)
+        finish(3, rounded0, room_b)
+        scalar_share(3)
+        run(7, 8)
+        plain_pass0(room_b)
+        plain_unit(4, room_c)
+        quantise(0, room_b, U, rounded0, room_b)
+        spread(3)
+        finish(4, rounded0, room_c)
+        scalar_share(4)
+        run(8, 9)
+        interleave(rounded0, HALF, g0[:, :, 0:C])
+        woven_interleave(0)
+        woven_interleave(1)
+        quantise(0, HALF, C, rounded0, HALF)
+        spread(4, 1)
+        finish(5, rounded1, 0)
+        scalar_share(5)
+        run(9, 13)
+        woven_interleave(2)
+        keep(5)
+        finish(6, rounded1, U)
+        run(13, 17)
+        woven_interleave(3)
+        keep(6)
+        finish(7, rounded1, 2 * U)
+        lo = ORDER[4] * U + SHORT
+        keep(4, SHORT)
+        nc.vector.tensor_copy(outs[0][:].indirect(listed(lo, U)), tail[:, SHORT : SHORT + U])
+        nc.vector.tensor_copy(tail[:, 3 * U : 5 * U], first_bank[7][:])
+        nc.vector.tensor_copy(outs[0][:].indirect(listed(lo + U, 3 * U - SHORT)), tail[:, SHORT + U : 4 * U])
+        room6, room7 = staged[:, 0 : 2 * U], staged[:, 2 * U : 4 * U]
+        nc.scalar.copy(room6[:, 0:U], pair_bank[6][:, 0:U])
+        scalar_scatter(1, ORDER[6] * U, U, room6[:, 0:U])
+        for i in range(2):
+            nc.scalar.copy(room7[:, i * U : (i + 1) * U], pair_bank[7][:, i * U : (i + 1) * U])
+        scalar_scatter(1, ORDER[7] * U, U, room7[:, 0:U])
+        scalar_scatter(2, ORDER[6] * U, U, room7[:, U : 2 * U])
+        scalar_scatter(2, ORDER[7] * U, U, tail[:, 4 * U : 5 * U])
+        nc.sync.dma_start(out[P : 2 * P, :], outs[1][:])
+        nc.sync.dma_start(out[2 * P : 3 * P, :], outs[2][:])
+        nc.sync.dma_start(out[0:P, 0 : T // 2], outs[0][:, 0 : T // 2])
+        nc.scalar.dma_start(out[0:P, T // 2 : T], outs[0][:, T // 2 : T])

@@ -37,6 +37,7 @@ WOVEN = [192, 192, 192, 192]
 REGION = max(WOVEN)
 ORDER = [7, 0, 1, 2, 3, 4, 5, 6]
 RING = 3
+WIDE = 384
 
 
 def tile_moe_bdx_lin_none_kernel(tc, dyT, w_words, w_scales, gate, offs, out):
@@ -60,9 +61,10 @@ def tile_moe_bdx_lin_none_kernel(tc, dyT, w_words, w_scales, gate, offs, out):
         code_scales = [held.tile([P, T], U8, name=f"code_scales{a}", align_bytes=MX_ALIGN) for a in range(PASSES)]
         codes = [held.tile([P, T], U32, name=f"codes{a}", align_bytes=MX_ALIGN) for a in range(PASSES)]
         rounded0 = held.tile([P, PACK * T], BF16, name="rounded0", align_bytes=MX_ALIGN)
-        late = held.tile([P, 2 * sum(WOVEN) + 4 * U], F32, name="late", align_bytes=MX_ALIGN)
+        late = held.tile([P, 2 * sum(WOVEN) + 3 * U], F32, name="late", align_bytes=MX_ALIGN)
         rounded1 = late[:, 0 : 2 * sum(WOVEN)].bitcast(BF16)
-        tail = late[:, 2 * sum(WOVEN) - U :]
+        rest = late[:, 2 * sum(WOVEN) - U :]
+        last = held.tile([P, 3 * U], F32, name="last")
         gated0 = held.tile([P, PACK * HALF], F32, name="gated0")
         gates = held.tile([P, HALF], F32, name="gates")
         first1 = held.tile([P, PACK * U], F32, name="first1")
@@ -189,11 +191,21 @@ def tile_moe_bdx_lin_none_kernel(tc, dyT, w_words, w_scales, gate, offs, out):
         def products(k):
             pair_bank[k] = bank_tile(k % RING)
             product(pair_bank[k][:, 0:U], ORDER[k], 1)
-            if k != 6:
-                product(pair_bank[k][:, U : 2 * U], ORDER[min(k, 6)], 2)
-            first_bank[k] = bank_tile(6 if k == 7 else RING + k % RING)
-            product(first_bank[k][:, 0:U], ORDER[k], 0)
-            if k == 7:
+            if k < 5:
+                product(pair_bank[k][:, U : 2 * U], ORDER[k], 2)
+                first_bank[k] = bank_tile(RING + k % RING)
+                product(first_bank[k][:, 0:U], ORDER[k], 0)
+            elif k == 5:
+                product(pair_bank[k][:, U : 2 * U], ORDER[k], 0)
+            elif k == 6:
+                first_bank[k] = bank_tile(RING)
+                product(first_bank[k][:, 0:U], ORDER[k], 0)
+            else:
+                product(pair_bank[k][:, U : 2 * U], ORDER[5], 2)
+                first_bank[8] = bank_tile(7)
+                product(first_bank[8][:, 0:U], ORDER[6], 2)
+                first_bank[k] = bank_tile(6)
+                product(first_bank[k][:, 0:U], ORDER[k], 0)
                 product(first_bank[k][:, U : 2 * U], ORDER[k], 2)
 
         def scalar_scatter(kt, lo, n, src):
@@ -201,15 +213,22 @@ def tile_moe_bdx_lin_none_kernel(tc, dyT, w_words, w_scales, gate, offs, out):
 
         def scalar_share(k):
             room = staged[:, k % RING * 2 * U : (k % RING + 1) * 2 * U]
-            for i in range(2):
-                nc.scalar.copy(room[:, i * U : (i + 1) * U], pair_bank[k][:, i * U : (i + 1) * U])
+            nc.scalar.copy(room, pair_bank[k][:])
+            spread(k, PACK if k < 4 else 1)
             for i in range(2):
                 scalar_scatter(1 + i, ORDER[k] * U, U, room[:, i * U : (i + 1) * U])
 
+        def late_share(k):
+            room = staged[:, k % RING * 2 * U : k % RING * 2 * U + U]
+            nc.scalar.copy(room, pair_bank[k][:, 0:U])
+            if k == 5:
+                nc.scalar.copy(rest[:, U : 2 * U], pair_bank[k][:, U : 2 * U])
+            scalar_scatter(1, ORDER[k] * U, U, room)
+
         heads = regions[:].rearrange("p (j c) -> p j c", c=REGION)
 
-        def spread(k, count=PACK):
-            nc.vector.tensor_copy(
+        def spread(k, count):
+            nc.scalar.copy(
                 heads[:, PACK * k : PACK * k + count, 0:SHORT], first_bank[k][:, 0 : count * SHORT].rearrange("p (j c) -> p j c", c=SHORT)
             )
 
@@ -270,62 +289,57 @@ def tile_moe_bdx_lin_none_kernel(tc, dyT, w_words, w_scales, gate, offs, out):
         def plain_pass0(room):
             gate_and_interleave(rounded0, room, p0[:, :, room : room + U], room)
 
-        def keep(k, lo=0):
-            nc.vector.tensor_copy(tail[:, (k - 4) * U + lo : (k - 3) * U], first_bank[k][:, lo:U])
-
         plain_unit(1, room_b)
-        spread(0)
+        plain_unit(2, room_a)
         finish(1, rounded0, room_b)
         scalar_share(1)
-        run(0, 4)
-        plain_unit(2, room_a)
-        spread(1)
+        run(0, 2)
         finish(2, rounded0, room_a)
         scalar_share(2)
-        run(4, 7)
+        run(2, 4)
         plain_pass0(room_a)
         plain_unit(3, room_b)
         quantise(0, room_a, U, rounded0, room_a)
-        spread(2)
+        run(4, 5)
         finish(3, rounded0, room_b)
         scalar_share(3)
-        run(7, 8)
+        run(5, 8)
         plain_pass0(room_b)
         plain_unit(4, room_c)
         quantise(0, room_b, U, rounded0, room_b)
-        spread(3)
+        run(8, 9)
         finish(4, rounded0, room_c)
         scalar_share(4)
-        run(8, 9)
-        interleave(rounded0, HALF, g0[:, :, 0:C])
         woven_interleave(0)
+        interleave(rounded0, HALF, g0[:, :, 0:C])
         woven_interleave(1)
         quantise(0, HALF, C, rounded0, HALF)
-        spread(4, 1)
+        run(9, 10)
         finish(5, rounded1, 0)
-        scalar_share(5)
-        run(9, 13)
+        late_share(5)
+        run(10, 14)
         woven_interleave(2)
-        keep(5)
+        run(14, 15)
         finish(6, rounded1, U)
-        run(13, 17)
+        late_share(6)
+        run(15, 17)
         woven_interleave(3)
-        keep(6)
+        nc.vector.tensor_copy(rest[:, 2 * U : 3 * U], first_bank[6][:, 0:U])
         finish(7, rounded1, 2 * U)
         lo = ORDER[4] * U + SHORT
-        keep(4, SHORT)
-        nc.vector.tensor_copy(outs[0][:].indirect(listed(lo, U)), tail[:, SHORT : SHORT + U])
-        nc.vector.tensor_copy(tail[:, 3 * U : 5 * U], first_bank[7][:])
-        nc.vector.tensor_copy(outs[0][:].indirect(listed(lo + U, 3 * U - SHORT)), tail[:, SHORT + U : 4 * U])
-        room6, room7 = staged[:, 0 : 2 * U], staged[:, 2 * U : 4 * U]
-        nc.scalar.copy(room6[:, 0:U], pair_bank[6][:, 0:U])
-        scalar_scatter(1, ORDER[6] * U, U, room6[:, 0:U])
+        nc.vector.tensor_copy(rest[:, SHORT:U], first_bank[4][:, SHORT:U])
+        nc.vector.tensor_copy(outs[0][:].indirect(listed(lo, 2 * U - SHORT)), rest[:, SHORT : 2 * U])
+        room = staged[:, 2 * U : 3 * U]
+        nc.scalar.copy(room, pair_bank[7][:, 0:U])
+        nc.vector.tensor_copy(rest[:, 3 * U : 4 * U], first_bank[7][:, 0:U])
+        nc.vector.tensor_copy(outs[0][:].indirect(listed(ORDER[6] * U, 2 * U)), rest[:, 2 * U : 4 * U])
+        nc.scalar.copy(last[:, 0:U], pair_bank[7][:, U : 2 * U])
+        nc.scalar.copy(last[:, U : 2 * U], first_bank[8][:, 0:U])
+        scalar_scatter(1, ORDER[7] * U, U, room)
+        nc.scalar.copy(last[:, 2 * U : 3 * U], first_bank[7][:, U : 2 * U])
         for i in range(2):
-            nc.scalar.copy(room7[:, i * U : (i + 1) * U], pair_bank[7][:, i * U : (i + 1) * U])
-        scalar_scatter(1, ORDER[7] * U, U, room7[:, 0:U])
-        scalar_scatter(2, ORDER[6] * U, U, room7[:, U : 2 * U])
-        scalar_scatter(2, ORDER[7] * U, U, tail[:, 4 * U : 5 * U])
-        nc.sync.dma_start(out[P : 2 * P, :], outs[1][:])
-        nc.sync.dma_start(out[2 * P : 3 * P, :], outs[2][:])
-        nc.sync.dma_start(out[0:P, 0 : T // 2], outs[0][:, 0 : T // 2])
-        nc.scalar.dma_start(out[0:P, T // 2 : T], outs[0][:, T // 2 : T])
+            scalar_scatter(2, ORDER[5] * U + i * WIDE, WIDE, last[:, i * WIDE : (i + 1) * WIDE])
+        nc.scalar.dma_start(out[P : 2 * P, :], outs[1][:])
+        nc.sync.dma_start(out[0:P, :], outs[0][:])
+        nc.sync.dma_start(out[2 * P : 3 * P, 0 : T // 2], outs[2][:, 0 : T // 2])
+        nc.scalar.dma_start(out[2 * P : 3 * P, T // 2 : T], outs[2][:, T // 2 : T])

@@ -36,7 +36,7 @@ SHORT = 64
 WOVEN = [192, 192, 192, 192]
 REGION = max(WOVEN)
 ORDER = [7, 0, 1, 2, 3, 4, 5, 6]
-RING = 3
+SLOW = C - P
 WIDE = 384
 
 
@@ -55,6 +55,7 @@ def tile_moe_bdx_lin_none_kernel(tc, dyT, w_words, w_scales, gate, offs, out):
         words = [held.tile([P, (hi - lo) * 2 * K], U8, name=f"words{lo}", align_bytes=MX_ALIGN) for lo, hi in parts]
         word_scales = [held.tile([P, (hi - lo) * K], U8, name=f"word_scales{lo}", align_bytes=MX_ALIGN) for lo, hi in parts]
         outs = [held.tile([P, T], F32, name=f"outs{kt}") for kt in range(KT)]
+        slow_gates = held.tile([P, 3 * P], F32, name="slow_gates")
         gate_cols = [held.tile([P, 2 * LINE], F32, name=f"gate_cols{h}") for h in range(2)]
         identity = held.tile([P, P], F32, name="identity")
         zeros = held.tile([P, SHORT], F32, name="zeros")
@@ -72,7 +73,7 @@ def tile_moe_bdx_lin_none_kernel(tc, dyT, w_words, w_scales, gate, offs, out):
         plain1 = held.tile([P, PACK * PLAIN[1]], F32, name="plain1")
         steps = PACK * len(WOVEN) + 1
         regions = held.tile([P, steps * REGION], F32, name="regions")
-        staged = held.tile([P, RING * 2 * U], F32, name="staged")
+        staged = held.tile([P, 10 * U], F32, name="staged")
 
         dy_rows = dyT.rearrange("(a p t) c -> a t p c", a=PASSES, p=P, t=PACK)
         landing = [(a, t) for a in range(PASSES) for t in range(PACK)]
@@ -164,6 +165,15 @@ def tile_moe_bdx_lin_none_kernel(tc, dyT, w_words, w_scales, gate, offs, out):
             row = banked_gates(lo, n) if lo < HALF else gate_row(lo, n).rearrange("p (c i) -> p c i", i=LINE)
             nc.vector.tensor_tensor(walk_out(tile, at, n), walk_in(src), row.unsqueeze(2).to_broadcast([P, n // LINE, PACK, LINE]), MULT)
 
+        def gpsimd_share(at, src, lo):
+            n = src.shape[2]
+            nc.gpsimd.tensor_tensor(
+                rounded0[:, PACK * at : PACK * (at + n)].rearrange("p (s t) -> p s t", t=PACK),
+                src.rearrange("p t s -> p s t"),
+                slow_gates[:, lo - SLOW : lo - SLOW + n].unsqueeze(2).to_broadcast([P, n, PACK]),
+                MULT,
+            )
+
         def quantise(a, lo, n, tile, at):
             nc.vector.quantize_mx(
                 out=codes[a][:, lo : lo + n].bitcast(FP8X4),
@@ -171,7 +181,7 @@ def tile_moe_bdx_lin_none_kernel(tc, dyT, w_words, w_scales, gate, offs, out):
                 in_=tile[:, PACK * at : PACK * (at + n)],
             )
 
-        def product(dst, u, kt):
+        def product(dst, u, kt, n=U):
             e = u * U // C
             part = 0 if e == E - 1 else 1
             for a in range(PASSES):
@@ -180,25 +190,26 @@ def tile_moe_bdx_lin_none_kernel(tc, dyT, w_words, w_scales, gate, offs, out):
                     out=dst,
                     lhsT=words[part][:, 2 * w0 : 2 * (w0 + P)].bitcast(FP4X4),
                     lhsT_scale=word_scales[part][:, w0 : w0 + P],
-                    rhs=codes[a][:, u * U : (u + 1) * U].bitcast(FP8X4),
-                    rhs_scale=code_scales[a][:, u * U : (u + 1) * U],
+                    rhs=codes[a][:, u * U : u * U + n].bitcast(FP8X4),
+                    rhs_scale=code_scales[a][:, u * U : u * U + n],
                     start=(a == 0),
                     stop=(a == PASSES - 1),
                 )
 
         pair_bank, first_bank = {}, {}
 
+        wide_banks = {}
+
+        def wide_products(u, n, banks):
+            for kt, b in zip((1, 2, 0), banks):
+                wide_banks[u, kt] = bank_tile(b)
+                product(wide_banks[u, kt][:, 0:n], u, kt, n)
+
         def products(k):
-            pair_bank[k] = bank_tile(k % RING)
+            pair_bank[k] = bank_tile({5: 1, 6: 4, 7: 0}[k])
             product(pair_bank[k][:, 0:U], ORDER[k], 1)
-            if k < 5:
-                product(pair_bank[k][:, U : 2 * U], ORDER[k], 2)
-                first_bank[k] = bank_tile(RING + k % RING)
-                product(first_bank[k][:, 0:U], ORDER[k], 0)
-            elif k == 5:
-                product(pair_bank[k][:, U : 2 * U], ORDER[k], 0)
-            elif k == 6:
-                first_bank[k] = bank_tile(RING)
+            if k < 7:
+                first_bank[k] = bank_tile({5: 2, 6: 5}[k])
                 product(first_bank[k][:, 0:U], ORDER[k], 0)
             else:
                 product(pair_bank[k][:, U : 2 * U], ORDER[5], 2)
@@ -211,26 +222,23 @@ def tile_moe_bdx_lin_none_kernel(tc, dyT, w_words, w_scales, gate, offs, out):
         def scalar_scatter(kt, lo, n, src):
             nc.scalar.activation(outs[kt][:].indirect(listed(lo, n)), src, COPY)
 
-        def scalar_share(k):
-            room = staged[:, k % RING * 2 * U : (k % RING + 1) * 2 * U]
-            nc.scalar.copy(room, pair_bank[k][:])
-            spread(k, PACK if k < 4 else 1)
+        def scalar_share(u, n, room, first_step, count):
             for i in range(2):
-                scalar_scatter(1 + i, ORDER[k] * U, U, room[:, i * U : (i + 1) * U])
+                nc.scalar.copy(room[:, i * n : (i + 1) * n], wide_banks[u, 1 + i][:, 0:n])
+            nc.scalar.copy(
+                heads[:, first_step : first_step + count, 0:SHORT],
+                wide_banks[u, 0][:, 0 : count * SHORT].rearrange("p (j c) -> p j c", c=SHORT),
+            )
+            for lo in range(0, n, U):
+                for i in range(2):
+                    scalar_scatter(1 + i, u * U + lo, U, room[:, i * n + lo : i * n + lo + U])
 
         def late_share(k):
-            room = staged[:, k % RING * 2 * U : k % RING * 2 * U + U]
+            room = staged[:, (k - 5) * U : (k - 4) * U]
             nc.scalar.copy(room, pair_bank[k][:, 0:U])
-            if k == 5:
-                nc.scalar.copy(rest[:, U : 2 * U], pair_bank[k][:, U : 2 * U])
             scalar_scatter(1, ORDER[k] * U, U, room)
 
         heads = regions[:].rearrange("p (j c) -> p j c", c=REGION)
-
-        def spread(k, count):
-            nc.scalar.copy(
-                heads[:, PACK * k : PACK * k + count, 0:SHORT], first_bank[k][:, 0 : count * SHORT].rearrange("p (j c) -> p j c", c=SHORT)
-            )
 
         starts = [PLAIN[1] + sum(WOVEN[:w]) for w in range(len(WOVEN))]
 
@@ -261,22 +269,19 @@ def tile_moe_bdx_lin_none_kernel(tc, dyT, w_words, w_scales, gate, offs, out):
         quantise(0, 3 * C, C, rounded0, 3 * C)
         gate_and_interleave(rounded0, 0, p0[:, :, 0:C], 0)
         gated_gather(f1[:, 1, :], 1, 1, first, U)
+        nc.vector.tensor_copy(slow_gates[:, 0:P].rearrange("m (c i) -> m c i", i=LINE), banked_gates(SLOW, P))
         quantise(0, 0, C, rounded0, 0)
         gated_gather(f1[:, 2, :], 1, 2, first, U)
         for h in range(2):
             gated_gather(f1[:, 3, h * P : (h + 1) * P], 1, 3, first + h * P, P)
-        room_a, room_b, room_c = 2 * U, 3 * U, 4 * U
-        astride = [room_b - P // 2, room_c - P // 2]
+        room = C + P
+        astride = [room, HALF]
         for h in range(2):
             interleave(rounded0, astride[h], f1[:, :, h * P : (h + 1) * P])
         for h in range(2):
             quantise(1, first + h * P, P, rounded0, astride[h])
-        products(0)
-        scalar_share(0)
-
-        def plain_unit(k, room):
-            lo = ORDER[k] * U
-            gate_and_interleave(rounded0, room, p1[:, :, lo : lo + U], lo)
+        wide_products(ORDER[0], U, (0, 2, 3))
+        scalar_share(ORDER[0], U, staged[:, 0 : 2 * U], 0, PACK)
 
         def finish(k, tile, at):
             quantise(1, ORDER[k] * U, U, tile, at)
@@ -286,30 +291,21 @@ def tile_moe_bdx_lin_none_kernel(tc, dyT, w_words, w_scales, gate, offs, out):
             for j in range(lo, hi):
                 step(j)
 
-        def plain_pass0(room):
-            gate_and_interleave(rounded0, room, p0[:, :, room : room + U], room)
-
-        plain_unit(1, room_b)
-        plain_unit(2, room_a)
-        finish(1, rounded0, room_b)
-        scalar_share(1)
-        run(0, 2)
-        finish(2, rounded0, room_a)
-        scalar_share(2)
-        run(2, 4)
-        plain_pass0(room_a)
-        plain_unit(3, room_b)
-        quantise(0, room_a, U, rounded0, room_a)
-        run(4, 5)
-        finish(3, rounded0, room_b)
-        scalar_share(3)
-        run(5, 8)
-        plain_pass0(room_b)
-        plain_unit(4, room_c)
-        quantise(0, room_b, U, rounded0, room_b)
-        run(8, 9)
-        finish(4, rounded0, room_c)
-        scalar_share(4)
+        gpsimd_share(room + SLOW, p1[:, :, SLOW:C], SLOW)
+        gate_and_interleave(rounded0, room, p1[:, :, 0:SLOW], 0)
+        nc.vector.tensor_copy(slow_gates[:, P:].rearrange("m (c i) -> m c i", i=LINE), banked_gates(C, U))
+        run(0, 1)
+        quantise(1, 0, C, rounded0, room)
+        wide_products(0, C, (1, 4, 5))
+        scalar_share(0, C, staged[:, 2 * U : 6 * U], PACK, 2 * PACK)
+        gpsimd_share(C, p0[:, :, C : C + U], C)
+        gate_and_interleave(rounded0, HALF, p1[:, :, C:HALF], C)
+        gate_and_interleave(rounded0, C + U, p0[:, :, C + U : HALF], C + U)
+        quantise(1, C, C, rounded0, HALF)
+        quantise(0, C, C, rounded0, C)
+        wide_products(2, C, (0, 2, 3))
+        scalar_share(2, C, staged[:, 6 * U : 10 * U], 3 * PACK, steps - 3 * PACK)
+        run(1, 9)
         woven_interleave(0)
         interleave(rounded0, HALF, g0[:, :, 0:C])
         woven_interleave(1)
@@ -317,24 +313,24 @@ def tile_moe_bdx_lin_none_kernel(tc, dyT, w_words, w_scales, gate, offs, out):
         run(9, 10)
         finish(5, rounded1, 0)
         late_share(5)
-        run(10, 14)
+        run(10, 13)
         woven_interleave(2)
-        run(14, 15)
+        nc.vector.tensor_copy(rest[:, U : 2 * U], first_bank[5][:, 0:U])
         finish(6, rounded1, U)
         late_share(6)
-        run(15, 17)
+        run(13, 17)
         woven_interleave(3)
         nc.vector.tensor_copy(rest[:, 2 * U : 3 * U], first_bank[6][:, 0:U])
         finish(7, rounded1, 2 * U)
         lo = ORDER[4] * U + SHORT
-        nc.vector.tensor_copy(rest[:, SHORT:U], first_bank[4][:, SHORT:U])
+        nc.vector.tensor_copy(last[:, U : 2 * U], first_bank[8][:, 0:U])
+        nc.vector.tensor_copy(rest[:, SHORT:U], wide_banks[2, 0][:, U + SHORT : C])
         nc.vector.tensor_copy(outs[0][:].indirect(listed(lo, 2 * U - SHORT)), rest[:, SHORT : 2 * U])
         room = staged[:, 2 * U : 3 * U]
         nc.scalar.copy(room, pair_bank[7][:, 0:U])
         nc.vector.tensor_copy(rest[:, 3 * U : 4 * U], first_bank[7][:, 0:U])
         nc.vector.tensor_copy(outs[0][:].indirect(listed(ORDER[6] * U, 2 * U)), rest[:, 2 * U : 4 * U])
         nc.scalar.copy(last[:, 0:U], pair_bank[7][:, U : 2 * U])
-        nc.scalar.copy(last[:, U : 2 * U], first_bank[8][:, 0:U])
         scalar_scatter(1, ORDER[7] * U, U, room)
         nc.scalar.copy(last[:, 2 * U : 3 * U], first_bank[7][:, U : 2 * U])
         for i in range(2):

@@ -36,7 +36,7 @@ SHORT = 64
 WOVEN = [192, 192, 192, 192]
 REGION = max(WOVEN)
 ORDER = [7, 0, 1, 2, 3, 4, 5, 6]
-SLOW = C - P
+SLOW = HALF - P
 WIDE = 384
 
 
@@ -55,7 +55,7 @@ def tile_moe_bdx_lin_none_kernel(tc, dyT, w_words, w_scales, gate, offs, out):
         words = [held.tile([P, (hi - lo) * 2 * K], U8, name=f"words{lo}", align_bytes=MX_ALIGN) for lo, hi in parts]
         word_scales = [held.tile([P, (hi - lo) * K], U8, name=f"word_scales{lo}", align_bytes=MX_ALIGN) for lo, hi in parts]
         outs = [held.tile([P, T], F32, name=f"outs{kt}") for kt in range(KT)]
-        slow_gates = held.tile([P, 3 * P], F32, name="slow_gates")
+        slow_gates = held.tile([P, P], F32, name="slow_gates")
         gate_cols = [held.tile([P, 2 * LINE], F32, name=f"gate_cols{h}") for h in range(2)]
         identity = held.tile([P, P], F32, name="identity")
         zeros = held.tile([P, SHORT], F32, name="zeros")
@@ -174,6 +174,16 @@ def tile_moe_bdx_lin_none_kernel(tc, dyT, w_words, w_scales, gate, offs, out):
                 MULT,
             )
 
+        def gpsimd_interleave(at, src):
+            nc.gpsimd.tensor_scalar(
+                rounded0[:, PACK * at : PACK * (at + src.shape[2])].rearrange("p (s t) -> p s t", t=PACK),
+                src.rearrange("p t s -> p s t"),
+                1.0,
+                0.0,
+                MULT,
+                ADD,
+            )
+
         def quantise(a, lo, n, tile, at):
             nc.vector.quantize_mx(
                 out=codes[a][:, lo : lo + n].bitcast(FP8X4),
@@ -222,10 +232,10 @@ def tile_moe_bdx_lin_none_kernel(tc, dyT, w_words, w_scales, gate, offs, out):
         def scalar_scatter(kt, lo, n, src):
             nc.scalar.activation(outs[kt][:].indirect(listed(lo, n)), src, COPY)
 
-        def scalar_share(u, n, room, first_step, count):
+        def scalar_share(u, n, room, first_step, count, spread):
             for i in range(2):
                 nc.scalar.copy(room[:, i * n : (i + 1) * n], wide_banks[u, 1 + i][:, 0:n])
-            nc.scalar.copy(
+            spread(
                 heads[:, first_step : first_step + count, 0:SHORT],
                 wide_banks[u, 0][:, 0 : count * SHORT].rearrange("p (j c) -> p j c", c=SHORT),
             )
@@ -260,28 +270,27 @@ def tile_moe_bdx_lin_none_kernel(tc, dyT, w_words, w_scales, gate, offs, out):
                 plain_gather(planes[:, PACK - 1, lo:hi], a, PACK - 1, lo, hi - lo)
         g0, f1 = by_plane(gated0[:]), by_plane(first1[:])
         first = T - U
-        for t in range(PACK - 1):
-            gated_gather(g0[:, t, :], 0, t, PLAIN[0], T - PLAIN[0])
-        gated_gather(g0[:, PACK - 1, C:], 0, PACK - 1, 3 * C, C)
-        gated_gather(g0[:, PACK - 1, 0:C], 0, PACK - 1, HALF, C)
-        interleave(rounded0, 3 * C, g0[:, :, C:])
+        for t in range(PACK):
+            gated_gather(g0[:, t, :], 0, t, HALF, HALF)
+        gpsimd_interleave(3 * C, g0[:, :, C:])
+        gate_and_interleave(rounded0, 0, p0[:, :, 0:C], 0)
+        gate_and_interleave(rounded0, C, p0[:, :, C : C + U], C)
+        nc.vector.tensor_copy(slow_gates[:].rearrange("m (c i) -> m c i", i=LINE), banked_gates(SLOW, P))
+        quantise(0, 0, C, rounded0, 0)
         gated_gather(f1[:, 0, :], 1, 0, first, U)
         quantise(0, 3 * C, C, rounded0, 3 * C)
-        gate_and_interleave(rounded0, 0, p0[:, :, 0:C], 0)
         gated_gather(f1[:, 1, :], 1, 1, first, U)
-        nc.vector.tensor_copy(slow_gates[:, 0:P].rearrange("m (c i) -> m c i", i=LINE), banked_gates(SLOW, P))
-        quantise(0, 0, C, rounded0, 0)
         gated_gather(f1[:, 2, :], 1, 2, first, U)
         for h in range(2):
             gated_gather(f1[:, 3, h * P : (h + 1) * P], 1, 3, first + h * P, P)
-        room = C + P
-        astride = [room, HALF]
+        room = 3 * C
+        astride = [room, HALF - P // 2]
         for h in range(2):
             interleave(rounded0, astride[h], f1[:, :, h * P : (h + 1) * P])
         for h in range(2):
             quantise(1, first + h * P, P, rounded0, astride[h])
         wide_products(ORDER[0], U, (0, 2, 3))
-        scalar_share(ORDER[0], U, staged[:, 0 : 2 * U], 0, PACK)
+        scalar_share(ORDER[0], U, staged[:, 0 : 2 * U], 0, PACK, nc.scalar.copy)
 
         def finish(k, tile, at):
             quantise(1, ORDER[k] * U, U, tile, at)
@@ -291,25 +300,22 @@ def tile_moe_bdx_lin_none_kernel(tc, dyT, w_words, w_scales, gate, offs, out):
             for j in range(lo, hi):
                 step(j)
 
-        gpsimd_share(room + SLOW, p1[:, :, SLOW:C], SLOW)
-        gate_and_interleave(rounded0, room, p1[:, :, 0:SLOW], 0)
-        nc.vector.tensor_copy(slow_gates[:, P:].rearrange("m (c i) -> m c i", i=LINE), banked_gates(C, U))
-        run(0, 1)
+        gpsimd_interleave(HALF, g0[:, :, 0:C])
+        gate_and_interleave(rounded0, room, p1[:, :, 0:C], 0)
+        gate_and_interleave(rounded0, C + U, p0[:, :, C + U : HALF], C + U)
         quantise(1, 0, C, rounded0, room)
         wide_products(0, C, (1, 4, 5))
-        scalar_share(0, C, staged[:, 2 * U : 6 * U], PACK, 2 * PACK)
-        gpsimd_share(C, p0[:, :, C : C + U], C)
-        gate_and_interleave(rounded0, HALF, p1[:, :, C:HALF], C)
-        gate_and_interleave(rounded0, C + U, p0[:, :, C + U : HALF], C + U)
-        quantise(1, C, C, rounded0, HALF)
-        quantise(0, C, C, rounded0, C)
+        gpsimd_share(room + SLOW - C, p1[:, :, SLOW:HALF], SLOW)
+        gate_and_interleave(rounded0, room, p1[:, :, C:SLOW], C)
+        scalar_share(0, C, staged[:, 2 * U : 6 * U], PACK, 2 * PACK, nc.vector.tensor_copy)
+        quantise(0, C, HALF, rounded0, C)
+        run(0, 1)
+        quantise(1, C, C, rounded0, room)
         wide_products(2, C, (0, 2, 3))
-        scalar_share(2, C, staged[:, 6 * U : 10 * U], 3 * PACK, steps - 3 * PACK)
+        scalar_share(2, C, staged[:, 6 * U : 10 * U], 3 * PACK, steps - 3 * PACK, nc.scalar.copy)
         run(1, 9)
         woven_interleave(0)
-        interleave(rounded0, HALF, g0[:, :, 0:C])
         woven_interleave(1)
-        quantise(0, HALF, C, rounded0, HALF)
         run(9, 10)
         finish(5, rounded1, 0)
         late_share(5)

@@ -65,7 +65,7 @@ def tile_moe_bdx_lin_none_kernel(tc, dyT, w_words, w_scales, gate, offs, out):
         late = held.tile([P, 2 * sum(WOVEN) + 3 * U], F32, name="late", align_bytes=MX_ALIGN)
         rounded1 = late[:, 0 : 2 * sum(WOVEN)].bitcast(BF16)
         rest = late[:, 2 * sum(WOVEN) - U :]
-        last = held.tile([P, 3 * U], F32, name="last")
+        last = held.tile([P, 6 * U], F32, name="last")
         gated0 = held.tile([P, PACK * HALF], F32, name="gated0")
         gates = held.tile([P, HALF], F32, name="gates")
         first1 = held.tile([P, PACK * U], F32, name="first1")
@@ -243,11 +243,6 @@ def tile_moe_bdx_lin_none_kernel(tc, dyT, w_words, w_scales, gate, offs, out):
                 for i in range(2):
                     scalar_scatter(1 + i, u * U + lo, U, room[:, i * n + lo : i * n + lo + U])
 
-        def late_share(k):
-            room = staged[:, (k - 5) * U : (k - 4) * U]
-            nc.scalar.copy(room, pair_bank[k][:, 0:U])
-            scalar_scatter(1, ORDER[k] * U, U, room)
-
         heads = regions[:].rearrange("p (j c) -> p j c", c=REGION)
 
         starts = [PLAIN[1] + sum(WOVEN[:w]) for w in range(len(WOVEN))]
@@ -318,29 +313,29 @@ def tile_moe_bdx_lin_none_kernel(tc, dyT, w_words, w_scales, gate, offs, out):
         woven_interleave(1)
         run(9, 10)
         finish(5, rounded1, 0)
-        late_share(5)
+        nc.scalar.copy(rest[:, U : 2 * U], first_bank[5][:, 0:U])
         run(10, 13)
         woven_interleave(2)
-        nc.vector.tensor_copy(rest[:, U : 2 * U], first_bank[5][:, 0:U])
+        nc.vector.tensor_copy(last[:, 0:U], pair_bank[5][:, 0:U])
+        scalar_scatter(1, ORDER[5] * U, U, last[:, 0:U])
         finish(6, rounded1, U)
-        late_share(6)
+        nc.scalar.copy(rest[:, 2 * U : 3 * U], first_bank[6][:, 0:U])
         run(13, 17)
         woven_interleave(3)
-        nc.vector.tensor_copy(rest[:, 2 * U : 3 * U], first_bank[6][:, 0:U])
+        nc.vector.tensor_copy(last[:, U:C], pair_bank[6][:, 0:U])
+        scalar_scatter(1, ORDER[6] * U, U, last[:, U:C])
         finish(7, rounded1, 2 * U)
         lo = ORDER[4] * U + SHORT
-        nc.vector.tensor_copy(last[:, U : 2 * U], first_bank[8][:, 0:U])
         nc.vector.tensor_copy(rest[:, SHORT:U], wide_banks[2, 0][:, U + SHORT : C])
         nc.vector.tensor_copy(outs[0][:].indirect(listed(lo, 2 * U - SHORT)), rest[:, SHORT : 2 * U])
-        room = staged[:, 2 * U : 3 * U]
-        nc.scalar.copy(room, pair_bank[7][:, 0:U])
         nc.vector.tensor_copy(rest[:, 3 * U : 4 * U], first_bank[7][:, 0:U])
         nc.vector.tensor_copy(outs[0][:].indirect(listed(ORDER[6] * U, 2 * U)), rest[:, 2 * U : 4 * U])
-        nc.scalar.copy(last[:, 0:U], pair_bank[7][:, U : 2 * U])
-        scalar_scatter(1, ORDER[7] * U, U, room)
-        nc.scalar.copy(last[:, 2 * U : 3 * U], first_bank[7][:, U : 2 * U])
+        nc.scalar.copy(last[:, C:HALF], pair_bank[7][:])
+        nc.scalar.copy(last[:, HALF : HALF + U], first_bank[8][:, 0:U])
+        scalar_scatter(1, ORDER[7] * U, U, last[:, C : C + U])
+        nc.scalar.copy(last[:, HALF + U : 3 * C], first_bank[7][:, U:C])
         for i in range(2):
-            scalar_scatter(2, ORDER[5] * U + i * WIDE, WIDE, last[:, i * WIDE : (i + 1) * WIDE])
+            scalar_scatter(2, ORDER[5] * U + i * WIDE, WIDE, last[:, (2 + i) * WIDE : (3 + i) * WIDE])
         nc.scalar.dma_start(out[P : 2 * P, :], outs[1][:])
         nc.sync.dma_start(out[0:P, :], outs[0][:])
         nc.sync.dma_start(out[2 * P : 3 * P, 0 : T // 2], outs[2][:, 0 : T // 2])

@@ -31,12 +31,9 @@ QUADRANTS = 4
 MX_ALIGN = 64
 
 U = 256
-PLAIN = [HALF, HALF]
-SHORT = 64
-WOVEN = [192, 192, 192, 192]
-REGION = max(WOVEN)
-ORDER = [7, 0, 1, 2, 3, 4, 5, 6]
-SLOW = HALF - P
+SPLIT = 3 * C
+AHEAD = 384
+SHARES = [128, 192]
 WIDE = 384
 
 
@@ -51,34 +48,34 @@ def tile_moe_bdx_lin_none_kernel(tc, dyT, w_words, w_scales, gate, offs, out):
 
         offsets = held.tile([P, T // PER_COLUMN], U16, name="offsets")
         dy = {(a, t): held.tile([P, T], F32, name=f"dy{a}{t}") for a in range(PASSES) for t in range(PACK)}
-        parts = [(GROUPS - PASSES, GROUPS), (0, GROUPS - PASSES)]
+        parts = [(GROUPS - PASSES, GROUPS), (0, PASSES), (PASSES, GROUPS - PASSES)]
         words = [held.tile([P, (hi - lo) * 2 * K], U8, name=f"words{lo}", align_bytes=MX_ALIGN) for lo, hi in parts]
         word_scales = [held.tile([P, (hi - lo) * K], U8, name=f"word_scales{lo}", align_bytes=MX_ALIGN) for lo, hi in parts]
         outs = [held.tile([P, T], F32, name=f"outs{kt}") for kt in range(KT)]
-        slow_gates = held.tile([P, P], F32, name="slow_gates")
         gate_cols = [held.tile([P, 2 * LINE], F32, name=f"gate_cols{h}") for h in range(2)]
         identity = held.tile([P, P], F32, name="identity")
-        zeros = held.tile([P, SHORT], F32, name="zeros")
         code_scales = [held.tile([P, T], U8, name=f"code_scales{a}", align_bytes=MX_ALIGN) for a in range(PASSES)]
-        codes = [held.tile([P, T], U32, name=f"codes{a}", align_bytes=MX_ALIGN) for a in range(PASSES)]
-        rounded0 = held.tile([P, PACK * T], BF16, name="rounded0", align_bytes=MX_ALIGN)
-        late = held.tile([P, 2 * sum(WOVEN) + 3 * U], F32, name="late", align_bytes=MX_ALIGN)
-        rounded1 = late[:, 0 : 2 * sum(WOVEN)].bitcast(BF16)
-        rest = late[:, 2 * sum(WOVEN) - U :]
-        last = held.tile([P, 6 * U], F32, name="last")
+        codes0 = held.tile([P, HALF], U32, name="codes0", align_bytes=MX_ALIGN)
+        codes11 = held.tile([P, C], U32, name="codes11", align_bytes=MX_ALIGN)
+        codes21 = held.tile([P, C], U32, name="codes21", align_bytes=MX_ALIGN)
+        gates0 = held.tile([P, C - SHARES[0]], F32, name="gates_first", tag="gates_first", align_bytes=MX_ALIGN)
+        codes01 = held.tile([P, C], U32, name="codes01", align_bytes=MX_ALIGN)
+        gates2 = held.tile([P, AHEAD], F32, name="gates2", tag="gates2", align_bytes=MX_ALIGN)
+        room = held.tile([P, 7 * C], F32, name="room", align_bytes=MX_ALIGN)
+        rounded = room[:].bitcast(BF16)
         gated0 = held.tile([P, PACK * HALF], F32, name="gated0")
-        gates = held.tile([P, HALF], F32, name="gates")
-        first1 = held.tile([P, PACK * U], F32, name="first1")
-        plain0 = held.tile([P, PACK * PLAIN[0]], F32, name="plain0")
-        plain1 = held.tile([P, PACK * PLAIN[1]], F32, name="plain1")
-        steps = PACK * len(WOVEN) + 1
-        regions = held.tile([P, steps * REGION], F32, name="regions")
-        staged = held.tile([P, 10 * U], F32, name="staged")
+        gates = [held.tile([P, HALF], F32, name=f"gates{h}") for h in range(2)]
+        plain0 = held.tile([P, PACK * HALF], F32, name="plain0", tag="plain0", align_bytes=MX_ALIGN)
+        plain1 = held.tile([P, PACK * HALF], F32, name="plain1", tag="plain1")
+        first1 = held.tile([P, PACK * C], F32, name="first1")
+        staged = held.tile([P, 15 * U], F32, name="staged")
+        firsts = held.tile([P, 7 * U], F32, name="firsts")
 
         dy_rows = dyT.rearrange("(a p t) c -> a t p c", a=PASSES, p=P, t=PACK)
         landing = [(a, t) for a in range(PASSES) for t in range(PACK)]
 
         warm = held.tile([P, 1], F32, name="warm")
+        zeros = held.tile([P, P], F32, name="zeros")
         nc.vector.memset(zeros[:], 0.0)
         nc.scalar.activation(warm[:], zeros[:, 0:1], COPY)
         for plane in word_scales:
@@ -106,13 +103,16 @@ def tile_moe_bdx_lin_none_kernel(tc, dyT, w_words, w_scales, gate, offs, out):
         for at in landing[1:3]:
             nc.sync.dma_start(dy[at][:], dy_rows[at])
         nc.sync.dma_start(gate_cols[0][:].rearrange("p (e i) -> p e i", e=2), gate_rows[0])
-        for at in landing[3:-1]:
+        for at in landing[3:]:
             nc.sync.dma_start(dy[at][:], dy_rows[at])
-        load_scales(0)
-        nc.sync.dma_start(dy[landing[-1]][:], dy_rows[landing[-1]])
-        load_words(0)
-        load_words(1)
-        load_scales(1)
+        nc.sync.dma_start(gates2[:], gate[0:P, HALF - AHEAD : HALF])
+        for part in range(2):
+            load_scales(part)
+            load_words(part)
+        nc.sync.dma_start(gates0[:], gate[P : 2 * P, SHARES[0] : C])
+        nc.sync.dma_start(gates[0][:, C + SHARES[1] :], gate[P : 2 * P, C + SHARES[1] : HALF])
+        load_scales(2)
+        load_words(2)
 
         def bank_tile(b):
             return psum.tile([P, C], F32, name="bank", tag=f"bank{b}")
@@ -120,24 +120,21 @@ def tile_moe_bdx_lin_none_kernel(tc, dyT, w_words, w_scales, gate, offs, out):
         make_identity(nc, identity[:])
         gate_banks = {}
         for e in reversed(range(E)):
-            bank = bank_tile([6, 7, 0, 1][e])
+            bank = bank_tile(e)
             for i in range(LINE):
                 col = e % 2 * LINE + i
                 nc.tensor.transpose(bank[:, i * P : (i + 1) * P], gate_cols[e // 2][:, col : col + 1].to_broadcast([P, P]), identity[:])
             gate_banks[e] = bank[:].rearrange("m (i c) -> m c i", i=LINE)
 
         def gate_row(lo, n):
-            return gates[:, lo - PLAIN[1] : lo - PLAIN[1] + n]
+            return gates[lo // HALF][:, lo % HALF : lo % HALF + n]
 
         def banked_gates(lo, n):
             e, c = divmod(lo, C)
             return gate_banks[e][:, c // LINE : (c + n) // LINE, :]
 
-        def copy_gates(lo, hi):
-            nc.vector.tensor_copy(gate_row(lo, hi - lo).rearrange("m (c i) -> m c i", i=LINE), banked_gates(lo, hi - lo))
-
-        copy_gates(3 * C, T)
-        copy_gates(HALF, 3 * C)
+        for lo in (3 * C, 2 * C):
+            nc.vector.tensor_copy(gate_row(lo, C).rearrange("m (c i) -> m c i", i=LINE), banked_gates(lo, C))
 
         def listed(lo, n):
             return offsets[:, lo // PER_COLUMN : (lo + n) // PER_COLUMN]
@@ -145,198 +142,176 @@ def tile_moe_bdx_lin_none_kernel(tc, dyT, w_words, w_scales, gate, offs, out):
         def window(a, t, lo, n):
             return dy[a, t][:].indirect(listed(lo, n))
 
-        def gated_gather(dst, a, t, lo, n):
-            nc.vector.tensor_tensor(dst, window(a, t, lo, n), gate_row(lo, n), MULT)
+        def words_at(at, n):
+            return rounded[:, PACK * at : PACK * (at + n)]
 
-        def plain_gather(dst, a, t, lo, n):
-            nc.scalar.activation(dst, window(a, t, lo, n), COPY)
+        def vector_gate(at, planes, lo, n, base=0):
+            nc.vector.tensor_tensor(
+                words_at(at, n).rearrange("p (c i t) -> p c t i", i=LINE, t=PACK),
+                planes[:, :, lo - base : lo - base + n].rearrange("p t (c i) -> p c t i", i=LINE),
+                banked_gates(lo, n).unsqueeze(2).to_broadcast([P, n // LINE, PACK, LINE]),
+                MULT,
+            )
 
-        def walk_out(tile, at, n):
-            return tile[:, PACK * at : PACK * (at + n)].rearrange("p (c i t) -> p c t i", i=LINE, t=PACK)
-
-        def walk_in(src):
-            return src.rearrange("p t (c i) -> p c t i", i=LINE)
-
-        def interleave(tile, at, src):
-            nc.vector.tensor_copy(walk_out(tile, at, src.shape[2]), walk_in(src))
-
-        def gate_and_interleave(tile, at, src, lo):
-            n = src.shape[2]
-            row = banked_gates(lo, n) if lo < HALF else gate_row(lo, n).rearrange("p (c i) -> p c i", i=LINE)
-            nc.vector.tensor_tensor(walk_out(tile, at, n), walk_in(src), row.unsqueeze(2).to_broadcast([P, n // LINE, PACK, LINE]), MULT)
-
-        def gpsimd_share(at, src, lo):
-            n = src.shape[2]
+        def gpsimd_gate(at, planes, lo, n, row=None, base=0):
             nc.gpsimd.tensor_tensor(
-                rounded0[:, PACK * at : PACK * (at + n)].rearrange("p (s t) -> p s t", t=PACK),
-                src.rearrange("p t s -> p s t"),
-                slow_gates[:, lo - SLOW : lo - SLOW + n].unsqueeze(2).to_broadcast([P, n, PACK]),
+                words_at(at, n).rearrange("p (s t) -> p s t", t=PACK),
+                planes[:, :, lo - base : lo - base + n].rearrange("p t s -> p s t"),
+                (gate_row(lo, n) if row is None else row).unsqueeze(2).to_broadcast([P, n, PACK]),
                 MULT,
             )
 
         def gpsimd_interleave(at, src):
             nc.gpsimd.tensor_scalar(
-                rounded0[:, PACK * at : PACK * (at + src.shape[2])].rearrange("p (s t) -> p s t", t=PACK),
-                src.rearrange("p t s -> p s t"),
-                1.0,
-                0.0,
-                MULT,
-                ADD,
+                words_at(at, src.shape[2]).rearrange("p (s t) -> p s t", t=PACK), src.rearrange("p t s -> p s t"), 1.0, 0.0, MULT, ADD
             )
 
-        def quantise(a, lo, n, tile, at):
-            nc.vector.quantize_mx(
-                out=codes[a][:, lo : lo + n].bitcast(FP8X4),
-                scales=code_scales[a][:, lo : lo + n],
-                in_=tile[:, PACK * at : PACK * (at + n)],
+        def quantise(dst, scales, at, n):
+            nc.vector.quantize_mx(out=dst.bitcast(FP8X4), scales=scales, in_=words_at(at, n))
+
+        code_of = {}
+        banks = {}
+
+        def one_pass(dst, e, a, kt, lo, n, start, stop):
+            part = [1, 2, 2, 0][e]
+            words_e, scales_e = code_of[e, a]
+            w0 = (e * PASSES + a - parts[part][0]) * K + P * kt
+            nc.tensor.matmul_mx(
+                out=dst,
+                lhsT=words[part][:, 2 * w0 : 2 * (w0 + P)].bitcast(FP4X4),
+                lhsT_scale=word_scales[part][:, w0 : w0 + P],
+                rhs=words_e[:, lo : lo + n].bitcast(FP8X4),
+                rhs_scale=scales_e[:, lo : lo + n],
+                start=start,
+                stop=stop,
             )
 
-        def product(dst, u, kt, n=U):
-            e = u * U // C
-            part = 0 if e == E - 1 else 1
-            for a in range(PASSES):
-                w0 = (e * PASSES + a - parts[part][0]) * K + P * kt
-                nc.tensor.matmul_mx(
-                    out=dst,
-                    lhsT=words[part][:, 2 * w0 : 2 * (w0 + P)].bitcast(FP4X4),
-                    lhsT_scale=word_scales[part][:, w0 : w0 + P],
-                    rhs=codes[a][:, u * U : u * U + n].bitcast(FP8X4),
-                    rhs_scale=code_scales[a][:, u * U : u * U + n],
-                    start=(a == 0),
-                    stop=(a == PASSES - 1),
-                )
-
-        pair_bank, first_bank = {}, {}
-
-        wide_banks = {}
-
-        def wide_products(u, n, banks):
-            for kt, b in zip((1, 2, 0), banks):
-                wide_banks[u, kt] = bank_tile(b)
-                product(wide_banks[u, kt][:, 0:n], u, kt, n)
-
-        def products(k):
-            pair_bank[k] = bank_tile({5: 1, 6: 4, 7: 0}[k])
-            product(pair_bank[k][:, 0:U], ORDER[k], 1)
-            if k < 7:
-                first_bank[k] = bank_tile({5: 2, 6: 5}[k])
-                product(first_bank[k][:, 0:U], ORDER[k], 0)
-            else:
-                product(pair_bank[k][:, U : 2 * U], ORDER[5], 2)
-                first_bank[8] = bank_tile(7)
-                product(first_bank[8][:, 0:U], ORDER[6], 2)
-                first_bank[k] = bank_tile(6)
-                product(first_bank[k][:, 0:U], ORDER[k], 0)
-                product(first_bank[k][:, U : 2 * U], ORDER[k], 2)
+        def passes(e, a, where, h=None):
+            key, lo, n = (e, 0, C) if h is None else ((e, h), h * U, U)
+            for kt, b in where:
+                if a == 0:
+                    banks[key, kt] = bank_tile(b)
+                if kt in (0, 1, 2):
+                    one_pass(banks[key, kt][:, 0:n], e, a, kt, lo, n, a == 0, a == 1)
+                else:
+                    for i in range(2):
+                        one_pass(banks[key, kt][:, i * U : (i + 1) * U], e, a, 1 + i, (kt - 3) * U, U, a == 0 and i == 0, a == 1 and i == 1)
 
         def scalar_scatter(kt, lo, n, src):
             nc.scalar.activation(outs[kt][:].indirect(listed(lo, n)), src, COPY)
 
-        def scalar_share(u, n, room, first_step, count, spread):
-            for i in range(2):
-                nc.scalar.copy(room[:, i * n : (i + 1) * n], wide_banks[u, 1 + i][:, 0:n])
-            spread(
-                heads[:, first_step : first_step + count, 0:SHORT],
-                wide_banks[u, 0][:, 0 : count * SHORT].rearrange("p (j c) -> p j c", c=SHORT),
-            )
-            for lo in range(0, n, U):
-                for i in range(2):
-                    scalar_scatter(1 + i, u * U + lo, U, room[:, i * n + lo : i * n + lo + U])
+        def vector_scatter(lo, n, src):
+            nc.vector.tensor_copy(outs[0][:].indirect(listed(lo, n)), src)
 
-        heads = regions[:].rearrange("p (j c) -> p j c", c=REGION)
+        p0, p1, g0, f1 = by_plane(plain0[:]), by_plane(plain1[:]), by_plane(gated0[:]), by_plane(first1[:])
+        woven = [by_plane(staged[:, 5 * h * U : (5 * h + PACK) * U]) for h in range(2)]
 
-        starts = [PLAIN[1] + sum(WOVEN[:w]) for w in range(len(WOVEN))]
+        def weave(h, t):
+            nc.scalar.activation(woven[h][:, t, :], window(1, t, HALF + h * U, U), COPY)
 
-        def step(j):
-            k, i = divmod(j, PACK)
-            nc.vector.tensor_tensor(outs[0][:].indirect(listed(ORDER[k] * U + i * SHORT, SHORT)), heads[:, j, 0:SHORT], zeros[:], ADD)
-            if j:
-                w, t = divmod(j - 1, PACK)
-                gated_gather(heads[:, j - 1, 0 : WOVEN[w]], 1, t, starts[w], WOVEN[w])
-
-        def woven_interleave(w):
-            interleave(rounded1, starts[w] - PLAIN[1], heads[:, PACK * w : PACK * (w + 1), 0 : WOVEN[w]])
-
-        p0, p1 = by_plane(plain0[:]), by_plane(plain1[:])
         for a, planes in enumerate([p0, p1]):
-            for t in range(PACK - 1):
-                plain_gather(planes[:, t, :], a, t, 0, PLAIN[a])
-            for lo, hi in [(0, C), (C, PLAIN[a])]:
-                plain_gather(planes[:, PACK - 1, lo:hi], a, PACK - 1, lo, hi - lo)
-        g0, f1 = by_plane(gated0[:]), by_plane(first1[:])
-        first = T - U
+            for t in range(PACK):
+                for lo, hi in [(0, HALF)] if t < PACK - 1 else [(0, C), (C, HALF)]:
+                    nc.scalar.activation(planes[:, t, lo:hi], window(a, t, lo, hi - lo), COPY)
+        for h in range(2):
+            weave(h, 0)
         for t in range(PACK):
-            gated_gather(g0[:, t, :], 0, t, HALF, HALF)
-        gpsimd_interleave(3 * C, g0[:, :, C:])
-        gate_and_interleave(rounded0, 0, p0[:, :, 0:C], 0)
-        gate_and_interleave(rounded0, C, p0[:, :, C : C + U], C)
-        nc.vector.tensor_copy(slow_gates[:].rearrange("m (c i) -> m c i", i=LINE), banked_gates(SLOW, P))
-        quantise(0, 0, C, rounded0, 0)
-        gated_gather(f1[:, 0, :], 1, 0, first, U)
-        quantise(0, 3 * C, C, rounded0, 3 * C)
-        gated_gather(f1[:, 1, :], 1, 1, first, U)
-        gated_gather(f1[:, 2, :], 1, 2, first, U)
-        for h in range(2):
-            gated_gather(f1[:, 3, h * P : (h + 1) * P], 1, 3, first + h * P, P)
-        room = 3 * C
-        astride = [room, HALF - P // 2]
-        for h in range(2):
-            interleave(rounded0, astride[h], f1[:, :, h * P : (h + 1) * P])
-        for h in range(2):
-            quantise(1, first + h * P, P, rounded0, astride[h])
-        wide_products(ORDER[0], U, (0, 2, 3))
-        scalar_share(ORDER[0], U, staged[:, 0 : 2 * U], 0, PACK, nc.scalar.copy)
+            nc.vector.tensor_tensor(g0[:, t, :], window(0, t, HALF, HALF), gates[1][:], MULT)
+        for i, e in enumerate([0, 3]):
+            code_of[e, 0] = codes0[:, i * C : (i + 1) * C], code_scales[0][:, i * C : (i + 1) * C]
 
-        def finish(k, tile, at):
-            quantise(1, ORDER[k] * U, U, tile, at)
-            products(k)
+        gpsimd_interleave(0, g0[:, :, 0:C])
+        start = HALF - AHEAD
+        gpsimd_interleave(start + C, g0[:, :, C:])
+        vector_gate(start, p0, 0, C)
+        vector_gate(C, p0, C, C - AHEAD)
+        for t in range(PACK - 1):
+            nc.vector.tensor_copy(f1[:, t, :], window(1, t, SPLIT, T - SPLIT))
+        quantise(codes0[:, 0:HALF], code_scales[0][:, 0:HALF], start, HALF)
+        gpsimd_gate(start, p0, start, AHEAD, gates2[:])
+        nc.vector.tensor_copy(f1[:, PACK - 1, :], window(1, PACK - 1, SPLIT, T - SPLIT))
+        where = {3: [(3, 4), (4, 5), (0, 6)], 0: [(3, 7), (4, 3), (0, 4)], 1: [(1, 5), (2, 0), (0, 6)], (2, 0): [(1, 7), (0, 3), (2, 4)], (2, 1): [(1, 1), (2, 2), (0, 5)]}
+        passes(3, 0, where[3])
+        vector_gate(2 * C, f1, 3 * C, C, SPLIT)
+        codes31 = held.tile([P, C], U32, name="codes31", tag="gates2", align_bytes=MX_ALIGN)
+        code_of[3, 1] = codes31[:], code_scales[1][:, 3 * C :]
+        quantise(*code_of[3, 1], 2 * C, C)
+        passes(3, 1, where[3])
 
-        def run(lo, hi):
-            for j in range(lo, hi):
-                step(j)
+        def empty(dst, e, kt, lo=0, n=C):
+            nc.vector.tensor_copy(dst, banks[e, kt][:, lo : lo + n])
 
-        gpsimd_interleave(HALF, g0[:, :, 0:C])
-        gate_and_interleave(rounded0, room, p1[:, :, 0:C], 0)
-        gate_and_interleave(rounded0, C + U, p0[:, :, C + U : HALF], C + U)
-        quantise(1, 0, C, rounded0, room)
-        wide_products(0, C, (1, 4, 5))
-        gpsimd_share(room + SLOW - C, p1[:, :, SLOW:HALF], SLOW)
-        gate_and_interleave(rounded0, room, p1[:, :, C:SLOW], C)
-        scalar_share(0, C, staged[:, 2 * U : 6 * U], PACK, 2 * PACK, nc.vector.tensor_copy)
-        quantise(0, C, HALF, rounded0, C)
-        run(0, 1)
-        quantise(1, C, C, rounded0, room)
-        wide_products(2, C, (0, 2, 3))
-        scalar_share(2, C, staged[:, 6 * U : 10 * U], 3 * PACK, steps - 3 * PACK, nc.scalar.copy)
-        run(1, 9)
-        woven_interleave(0)
-        woven_interleave(1)
-        run(9, 10)
-        finish(5, rounded1, 0)
-        nc.scalar.copy(rest[:, U : 2 * U], first_bank[5][:, 0:U])
-        run(10, 13)
-        woven_interleave(2)
-        nc.vector.tensor_copy(last[:, 0:U], pair_bank[5][:, 0:U])
-        scalar_scatter(1, ORDER[5] * U, U, last[:, 0:U])
-        finish(6, rounded1, U)
-        nc.scalar.copy(rest[:, 2 * U : 3 * U], first_bank[6][:, 0:U])
-        run(13, 17)
-        woven_interleave(3)
-        nc.vector.tensor_copy(last[:, U:C], pair_bank[6][:, 0:U])
-        scalar_scatter(1, ORDER[6] * U, U, last[:, U:C])
-        finish(7, rounded1, 2 * U)
-        lo = ORDER[4] * U + SHORT
-        nc.vector.tensor_copy(rest[:, SHORT:U], wide_banks[2, 0][:, U + SHORT : C])
-        nc.vector.tensor_copy(outs[0][:].indirect(listed(lo, 2 * U - SHORT)), rest[:, SHORT : 2 * U])
-        nc.vector.tensor_copy(rest[:, 3 * U : 4 * U], first_bank[7][:, 0:U])
-        nc.vector.tensor_copy(outs[0][:].indirect(listed(ORDER[6] * U, 2 * U)), rest[:, 2 * U : 4 * U])
-        nc.scalar.copy(last[:, C:HALF], pair_bank[7][:])
-        nc.scalar.copy(last[:, HALF : HALF + U], first_bank[8][:, 0:U])
-        scalar_scatter(1, ORDER[7] * U, U, last[:, C : C + U])
-        nc.scalar.copy(last[:, HALF + U : 3 * C], first_bank[7][:, U:C])
-        for i in range(2):
-            scalar_scatter(2, ORDER[5] * U + i * WIDE, WIDE, last[:, (2 + i) * WIDE : (3 + i) * WIDE])
-        nc.scalar.dma_start(out[P : 2 * P, :], outs[1][:])
+        def scatters(e, h):
+            for j in range(4):
+                scalar_scatter(1 + j % 2, e * C + j // 2 * U, U, staged[:, (5 * h + 1 + j) * U : (5 * h + 2 + j) * U])
+                if j:
+                    weave(h, j)
+
+        gpsimd_gate(2 * C + SHARES[0], p1, SHARES[0], C - SHARES[0], gates0[:])
+        passes(0, 0, where[0])
+        empty(staged[:, U : 3 * U], 3, 3)
+        empty(staged[:, 3 * U : 5 * U], 3, 4)
+        empty(firsts[:, 0:C], 3, 0)
+        vector_gate(2 * C, p1, 0, SHARES[0])
+        scatters(3, 0)
+        vector_scatter(3 * C, C, firsts[:, 0:C])
+        code_of[0, 1] = codes01[:], code_scales[1][:, 0:C]
+        quantise(*code_of[0, 1], 2 * C, C)
+        passes(0, 1, where[0])
+        later0 = held.tile([P, HALF], U32, name="later0", tag="gates_first", align_bytes=MX_ALIGN)
+        for i, e in enumerate([2, 1]):
+            code_of[e, 0] = later0[:, i * C : (i + 1) * C], code_scales[0][:, HALF + i * C : HALF + (i + 1) * C]
+        quantise(later0[:], code_scales[0][:, HALF:T], 0, HALF)
+
+        gpsimd_gate(SHARES[1], p1, C + SHARES[1], C - SHARES[1])
+        passes(1, 0, where[1])
+        empty(staged[:, 6 * U : 8 * U], 0, 3)
+        empty(staged[:, 8 * U : 10 * U], 0, 4)
+        empty(firsts[:, C : C + U], 0, 0, 0, U)
+        scatters(0, 1)
+        vector_gate(0, p1, C, SHARES[1])
+        vector_scatter(0, U, firsts[:, C : C + U])
+        empty(p1[:, 0, C + U : 2 * C], 0, 0, U, U)
+        code_of[1, 1] = codes11[:], code_scales[1][:, C : 2 * C]
+        quantise(*code_of[1, 1], 0, C)
+        passes(1, 1, where[1])
+        vector_scatter(U, U, p1[:, 0, C + U : 2 * C])
+
+        code_of[2, 1] = codes21[:], code_scales[1][:, 2 * C : 3 * C]
+        ones = staged[:, 5 * C : 7 * C]
+        own = firsts[:, 3 * U :]
+
+        def unit(h):
+            quantise(codes21[:, h * U : (h + 1) * U], code_scales[1][:, 2 * C + h * U : 2 * C + (h + 1) * U], 0, U)
+            passes(2, 1, where[2, h], h)
+
+        gpsimd_gate(0, woven[0], 2 * C, U, base=2 * C)
+        for h in range(2):
+            passes(2, 0, where[2, h], h)
+        empty(ones[:, 0:C], 1, 1)
+        empty(staged[:, 7 * C : 7 * C + U], 1, 2, 0, U)
+        empty(own[:, 0:C], 1, 0)
+        scalar_scatter(1, C, WIDE, ones[:, 0:WIDE])
+        scalar_scatter(2, C, U, staged[:, 7 * C : 7 * C + U])
+        unit(0)
+        gpsimd_gate(0, woven[1], 2 * C + U, U, base=2 * C + U)
+        vector_scatter(C, WIDE, own[:, 0:WIDE])
+        empty(ones[:, C : C + U], (2, 0), 1, 0, U)
+        empty(own[:, C : C + U], (2, 0), 0, 0, U)
+        scalar_scatter(1, C + WIDE, WIDE, ones[:, WIDE : 2 * WIDE])
+        unit(1)
+        late = staged[:, 6 * U : 9 * U]
+        empty(late[:, 0:U], 1, 2, U, U)
+        empty(late[:, U:C], (2, 0), 2, 0, U)
+        empty(ones[:, C + U :], (2, 1), 1, 0, U)
+        empty(late[:, C:], (2, 1), 2, 0, U)
+        empty(own[:, C + U :], (2, 1), 0, 0, U)
+        nc.vector.tensor_tensor(outs[2][:].indirect(listed(6 * U - P, P)), late[:, 3 * U - P :], zeros[:], ADD)
+        vector_scatter(C + WIDE, HALF - WIDE, own[:, WIDE:])
+        scalar_scatter(1, 5 * U, U, ones[:, C + U :])
+        for lo, n in [(0, U), (U, WIDE)]:
+            scalar_scatter(2, 3 * U + lo, n, late[:, lo : lo + n])
+        nc.sync.dma_start(out[P : 2 * P, :], outs[1][:])
         nc.sync.dma_start(out[0:P, :], outs[0][:])
         nc.sync.dma_start(out[2 * P : 3 * P, 0 : T // 2], outs[2][:, 0 : T // 2])
         nc.scalar.dma_start(out[2 * P : 3 * P, T // 2 : T], outs[2][:, T // 2 : T])

@@ -32,8 +32,8 @@ MX_ALIGN = 64
 
 U = 256
 SPLIT = 3 * C
-AHEAD = 384
-SHARES = [128, 192]
+AHEAD = 160
+SHARE = 160
 WIDE = 384
 
 
@@ -55,13 +55,14 @@ def tile_moe_bdx_lin_none_kernel(tc, dyT, w_words, w_scales, gate, offs, out):
         gate_cols = [held.tile([P, 2 * LINE], F32, name=f"gate_cols{h}") for h in range(2)]
         identity = held.tile([P, P], F32, name="identity")
         code_scales = [held.tile([P, T], U8, name=f"code_scales{a}", align_bytes=MX_ALIGN) for a in range(PASSES)]
-        codes0 = held.tile([P, HALF], U32, name="codes0", align_bytes=MX_ALIGN)
+        codes30 = held.tile([P, C], U32, name="codes30", align_bytes=MX_ALIGN)
+        halves = [held.tile([P, PACK * U], BF16, name=f"half{h}", tag=f"half{h}", align_bytes=MX_ALIGN) for h in range(2)]
         codes11 = held.tile([P, C], U32, name="codes11", align_bytes=MX_ALIGN)
         codes21 = held.tile([P, C], U32, name="codes21", align_bytes=MX_ALIGN)
-        gates0 = held.tile([P, C - SHARES[0]], F32, name="gates_first", tag="gates_first", align_bytes=MX_ALIGN)
+        gates0 = held.tile([P, C - SHARE], F32, name="gates_first", tag="gates_first", align_bytes=MX_ALIGN)
         codes01 = held.tile([P, C], U32, name="codes01", align_bytes=MX_ALIGN)
         gates2 = held.tile([P, AHEAD], F32, name="gates2", tag="gates2", align_bytes=MX_ALIGN)
-        room = held.tile([P, 7 * C], F32, name="room", align_bytes=MX_ALIGN)
+        room = held.tile([P, 6 * C], F32, name="room", align_bytes=MX_ALIGN)
         rounded = room[:].bitcast(BF16)
         gated0 = held.tile([P, PACK * HALF], F32, name="gated0")
         gates = [held.tile([P, HALF], F32, name=f"gates{h}") for h in range(2)]
@@ -69,15 +70,14 @@ def tile_moe_bdx_lin_none_kernel(tc, dyT, w_words, w_scales, gate, offs, out):
         plain1 = held.tile([P, PACK * HALF], F32, name="plain1", tag="plain1")
         first1 = held.tile([P, PACK * C], F32, name="first1")
         staged = held.tile([P, 15 * U], F32, name="staged")
-        firsts = held.tile([P, 7 * U], F32, name="firsts")
+        firsts = held.tile([P, 3 * C], F32, name="firsts")
 
         dy_rows = dyT.rearrange("(a p t) c -> a t p c", a=PASSES, p=P, t=PACK)
         landing = [(a, t) for a in range(PASSES) for t in range(PACK)]
 
-        warm = held.tile([P, 1], F32, name="warm")
-        zeros = held.tile([P, P], F32, name="zeros")
-        nc.vector.memset(zeros[:], 0.0)
-        nc.scalar.activation(warm[:], zeros[:, 0:1], COPY)
+        warm = held.tile([P, 2], F32, name="warm")
+        nc.vector.memset(warm[:, 0:1], 0.0)
+        nc.scalar.activation(warm[:, 1:2], warm[:, 0:1], COPY)
         for plane in word_scales:
             nc.vector.memset(plane[:].bitcast(I32), 0)
 
@@ -103,14 +103,16 @@ def tile_moe_bdx_lin_none_kernel(tc, dyT, w_words, w_scales, gate, offs, out):
         for at in landing[1:3]:
             nc.sync.dma_start(dy[at][:], dy_rows[at])
         nc.sync.dma_start(gate_cols[0][:].rearrange("p (e i) -> p e i", e=2), gate_rows[0])
-        for at in landing[3:]:
+        for at in landing[3:-1]:
             nc.sync.dma_start(dy[at][:], dy_rows[at])
-        nc.sync.dma_start(gates2[:], gate[0:P, HALF - AHEAD : HALF])
-        for part in range(2):
-            load_scales(part)
-            load_words(part)
-        nc.sync.dma_start(gates0[:], gate[P : 2 * P, SHARES[0] : C])
-        nc.sync.dma_start(gates[0][:, C + SHARES[1] :], gate[P : 2 * P, C + SHARES[1] : HALF])
+        load_scales(0)
+        nc.sync.dma_start(dy[landing[-1]][:], dy_rows[landing[-1]])
+        nc.sync.dma_start(gates2[:], gate[0:P, C - AHEAD : C])
+        load_words(0)
+        load_scales(1)
+        load_words(1)
+        nc.sync.dma_start(gates0[:], gate[P : 2 * P, SHARE : C])
+        nc.sync.dma_start(gates[0][:, C:], gate[P : 2 * P, C:HALF])
         load_scales(2)
         load_words(2)
 
@@ -119,12 +121,16 @@ def tile_moe_bdx_lin_none_kernel(tc, dyT, w_words, w_scales, gate, offs, out):
 
         make_identity(nc, identity[:])
         gate_banks = {}
-        for e in reversed(range(E)):
-            bank = bank_tile(e)
+
+        def spread_gates(e, b):
+            bank = bank_tile(b)
             for i in range(LINE):
                 col = e % 2 * LINE + i
                 nc.tensor.transpose(bank[:, i * P : (i + 1) * P], gate_cols[e // 2][:, col : col + 1].to_broadcast([P, P]), identity[:])
             gate_banks[e] = bank[:].rearrange("m (i c) -> m c i", i=LINE)
+
+        for e in (3, 2, 0):
+            spread_gates(e, e)
 
         def gate_row(lo, n):
             return gates[lo // HALF][:, lo % HALF : lo % HALF + n]
@@ -143,7 +149,7 @@ def tile_moe_bdx_lin_none_kernel(tc, dyT, w_words, w_scales, gate, offs, out):
             return dy[a, t][:].indirect(listed(lo, n))
 
         def words_at(at, n):
-            return rounded[:, PACK * at : PACK * (at + n)]
+            return halves[-at - 1][:] if at < 0 else rounded[:, PACK * at : PACK * (at + n)]
 
         def vector_gate(at, planes, lo, n, base=0):
             nc.vector.tensor_tensor(
@@ -217,26 +223,30 @@ def tile_moe_bdx_lin_none_kernel(tc, dyT, w_words, w_scales, gate, offs, out):
             weave(h, 0)
         for t in range(PACK):
             nc.vector.tensor_tensor(g0[:, t, :], window(0, t, HALF, HALF), gates[1][:], MULT)
-        for i, e in enumerate([0, 3]):
-            code_of[e, 0] = codes0[:, i * C : (i + 1) * C], code_scales[0][:, i * C : (i + 1) * C]
-
+        code_of[3, 0] = codes30[:], code_scales[0][:, C:HALF]
+        zero = 3 * U
+        gpsimd_interleave(0, g0[:, :, C:])
+        vector_gate(zero, p0, 0, C - AHEAD)
+        nc.vector.tensor_copy(f1[:, 0, :], window(1, 0, SPLIT, C))
+        quantise(*code_of[3, 0], 0, C)
         gpsimd_interleave(0, g0[:, :, 0:C])
-        start = HALF - AHEAD
-        gpsimd_interleave(start + C, g0[:, :, C:])
-        vector_gate(start, p0, 0, C)
-        vector_gate(C, p0, C, C - AHEAD)
-        for t in range(PACK - 1):
-            nc.vector.tensor_copy(f1[:, t, :], window(1, t, SPLIT, T - SPLIT))
-        quantise(codes0[:, 0:HALF], code_scales[0][:, 0:HALF], start, HALF)
-        gpsimd_gate(start, p0, start, AHEAD, gates2[:])
-        nc.vector.tensor_copy(f1[:, PACK - 1, :], window(1, PACK - 1, SPLIT, T - SPLIT))
-        where = {3: [(3, 4), (4, 5), (0, 6)], 0: [(3, 7), (4, 3), (0, 4)], 1: [(1, 5), (2, 0), (0, 6)], (2, 0): [(1, 7), (0, 3), (2, 4)], (2, 1): [(1, 1), (2, 2), (0, 5)]}
+        gpsimd_gate(zero + C - AHEAD, p0, C - AHEAD, AHEAD, gates2[:])
+        for t in range(1, PACK - 1):
+            nc.vector.tensor_copy(f1[:, t, :], window(1, t, SPLIT, C))
+        for h in range(2):
+            nc.vector.tensor_copy(f1[:, PACK - 1, h * U : (h + 1) * U], window(1, PACK - 1, SPLIT + h * U, U))
+        where = {3: [(3, 4), (4, 5), (0, 6)], 0: [(3, 7), (4, 3), (0, 1)], 1: [(1, 5), (2, 0), (0, 6)], (2, 0): [(1, 7), (0, 3), (2, 4)], (2, 1): [(1, 1), (2, 2), (0, 5)]}
         passes(3, 0, where[3])
-        vector_gate(2 * C, f1, 3 * C, C, SPLIT)
+        for h in range(2):
+            vector_gate(-1 - h, f1, SPLIT + h * U, U, SPLIT)
         codes31 = held.tile([P, C], U32, name="codes31", tag="gates2", align_bytes=MX_ALIGN)
         code_of[3, 1] = codes31[:], code_scales[1][:, 3 * C :]
-        quantise(*code_of[3, 1], 2 * C, C)
+        for h in range(2):
+            quantise(codes31[:, h * U : (h + 1) * U], code_scales[1][:, SPLIT + h * U : SPLIT + (h + 1) * U], -1 - h, U)
         passes(3, 1, where[3])
+        codes00 = held.tile([P, C], U32, name="codes00", tag="half0", align_bytes=MX_ALIGN)
+        code_of[0, 0] = codes00[:], code_scales[0][:, 0:C]
+        quantise(*code_of[0, 0], zero, C)
 
         def empty(dst, e, kt, lo=0, n=C):
             nc.vector.tensor_copy(dst, banks[e, kt][:, lo : lo + n])
@@ -247,14 +257,14 @@ def tile_moe_bdx_lin_none_kernel(tc, dyT, w_words, w_scales, gate, offs, out):
                 if j:
                     weave(h, j)
 
-        gpsimd_gate(2 * C + SHARES[0], p1, SHARES[0], C - SHARES[0], gates0[:])
+        gpsimd_gate(2 * C + SHARE, p1, SHARE, C - SHARE, gates0[:])
         passes(0, 0, where[0])
         empty(staged[:, U : 3 * U], 3, 3)
+        spread_gates(1, 4)
         empty(staged[:, 3 * U : 5 * U], 3, 4)
-        empty(firsts[:, 0:C], 3, 0)
-        vector_gate(2 * C, p1, 0, SHARES[0])
+        vector_gate(2 * C, p1, 0, SHARE)
         scatters(3, 0)
-        vector_scatter(3 * C, C, firsts[:, 0:C])
+        vector_gate(C, p0, C, C)
         code_of[0, 1] = codes01[:], code_scales[1][:, 0:C]
         quantise(*code_of[0, 1], 2 * C, C)
         passes(0, 1, where[0])
@@ -263,23 +273,22 @@ def tile_moe_bdx_lin_none_kernel(tc, dyT, w_words, w_scales, gate, offs, out):
             code_of[e, 0] = later0[:, i * C : (i + 1) * C], code_scales[0][:, HALF + i * C : HALF + (i + 1) * C]
         quantise(later0[:], code_scales[0][:, HALF:T], 0, HALF)
 
-        gpsimd_gate(SHARES[1], p1, C + SHARES[1], C - SHARES[1])
-        passes(1, 0, where[1])
+        gpsimd_gate(0, p1, C, C)
         empty(staged[:, 6 * U : 8 * U], 0, 3)
         empty(staged[:, 8 * U : 10 * U], 0, 4)
-        empty(firsts[:, C : C + U], 0, 0, 0, U)
         scatters(0, 1)
-        vector_gate(0, p1, C, SHARES[1])
-        vector_scatter(0, U, firsts[:, C : C + U])
-        empty(p1[:, 0, C + U : 2 * C], 0, 0, U, U)
+        empty(p1[:, 0, 0:C], 3, 0)
+        empty(firsts[:, 0:C], 0, 0)
+        passes(1, 0, where[1])
+        vector_scatter(3 * C, C, p1[:, 0, 0:C])
         code_of[1, 1] = codes11[:], code_scales[1][:, C : 2 * C]
         quantise(*code_of[1, 1], 0, C)
         passes(1, 1, where[1])
-        vector_scatter(U, U, p1[:, 0, C + U : 2 * C])
+        vector_scatter(0, U, firsts[:, 0:U])
 
         code_of[2, 1] = codes21[:], code_scales[1][:, 2 * C : 3 * C]
         ones = staged[:, 5 * C : 7 * C]
-        own = firsts[:, 3 * U :]
+        own = firsts[:, C:]
 
         def unit(h):
             quantise(codes21[:, h * U : (h + 1) * U], code_scales[1][:, 2 * C + h * U : 2 * C + (h + 1) * U], 0, U)
@@ -295,7 +304,7 @@ def tile_moe_bdx_lin_none_kernel(tc, dyT, w_words, w_scales, gate, offs, out):
         scalar_scatter(2, C, U, staged[:, 7 * C : 7 * C + U])
         unit(0)
         gpsimd_gate(0, woven[1], 2 * C + U, U, base=2 * C + U)
-        vector_scatter(C, WIDE, own[:, 0:WIDE])
+        vector_scatter(U, WIDE, firsts[:, U : U + WIDE])
         empty(ones[:, C : C + U], (2, 0), 1, 0, U)
         empty(own[:, C : C + U], (2, 0), 0, 0, U)
         scalar_scatter(1, C + WIDE, WIDE, ones[:, WIDE : 2 * WIDE])
@@ -306,10 +315,9 @@ def tile_moe_bdx_lin_none_kernel(tc, dyT, w_words, w_scales, gate, offs, out):
         empty(ones[:, C + U :], (2, 1), 1, 0, U)
         empty(late[:, C:], (2, 1), 2, 0, U)
         empty(own[:, C + U :], (2, 1), 0, 0, U)
-        nc.vector.tensor_tensor(outs[2][:].indirect(listed(6 * U - P, P)), late[:, 3 * U - P :], zeros[:], ADD)
-        vector_scatter(C + WIDE, HALF - WIDE, own[:, WIDE:])
+        vector_scatter(U + WIDE, SPLIT - U - WIDE, firsts[:, U + WIDE :])
         scalar_scatter(1, 5 * U, U, ones[:, C + U :])
-        for lo, n in [(0, U), (U, WIDE)]:
+        for lo, n in [(WIDE, WIDE), (0, WIDE)]:
             scalar_scatter(2, 3 * U + lo, n, late[:, lo : lo + n])
         nc.sync.dma_start(out[P : 2 * P, :], outs[1][:])
         nc.sync.dma_start(out[0:P, :], outs[0][:])

@@ -32,8 +32,9 @@ MX_ALIGN = 64
 
 U = 256
 SPLIT = 3 * C
-AHEAD = 160
-SHARE = 160
+AHEAD = 192
+SHARE = 128
+LATER = 64
 WIDE = 384
 
 
@@ -69,8 +70,8 @@ def tile_moe_bdx_lin_none_kernel(tc, dyT, w_words, w_scales, gate, offs, out):
         plain0 = held.tile([P, PACK * HALF], F32, name="plain0", tag="plain0", align_bytes=MX_ALIGN)
         plain1 = held.tile([P, PACK * HALF], F32, name="plain1", tag="plain1")
         first1 = held.tile([P, PACK * C], F32, name="first1")
-        staged = held.tile([P, 15 * U], F32, name="staged")
-        firsts = held.tile([P, 3 * C], F32, name="firsts")
+        staged = held.tile([P, 18 * U], F32, name="staged")
+        firsts = held.tile([P, 7 * U], F32, name="firsts")
 
         dy_rows = dyT.rearrange("(a p t) c -> a t p c", a=PASSES, p=P, t=PACK)
         landing = [(a, t) for a in range(PASSES) for t in range(PACK)]
@@ -107,12 +108,12 @@ def tile_moe_bdx_lin_none_kernel(tc, dyT, w_words, w_scales, gate, offs, out):
             nc.sync.dma_start(dy[at][:], dy_rows[at])
         load_scales(0)
         nc.sync.dma_start(dy[landing[-1]][:], dy_rows[landing[-1]])
-        nc.sync.dma_start(gates2[:], gate[0:P, C - AHEAD : C])
+        nc.sync.dma_start(gates2[:], gate[0:P, C : C + AHEAD])
         load_words(0)
         load_scales(1)
         load_words(1)
         nc.sync.dma_start(gates0[:], gate[P : 2 * P, SHARE : C])
-        nc.sync.dma_start(gates[0][:, C:], gate[P : 2 * P, C:HALF])
+        nc.sync.dma_start(gates[0][:, C + LATER :], gate[P : 2 * P, C + LATER : HALF])
         load_scales(2)
         load_words(2)
 
@@ -226,16 +227,16 @@ def tile_moe_bdx_lin_none_kernel(tc, dyT, w_words, w_scales, gate, offs, out):
         code_of[3, 0] = codes30[:], code_scales[0][:, C:HALF]
         zero = 3 * U
         gpsimd_interleave(0, g0[:, :, C:])
-        vector_gate(zero, p0, 0, C - AHEAD)
+        vector_gate(zero, p0, 0, C)
         nc.vector.tensor_copy(f1[:, 0, :], window(1, 0, SPLIT, C))
         quantise(*code_of[3, 0], 0, C)
         gpsimd_interleave(0, g0[:, :, 0:C])
-        gpsimd_gate(zero + C - AHEAD, p0, C - AHEAD, AHEAD, gates2[:])
+        gpsimd_gate(C, p0, C, AHEAD, gates2[:])
         for t in range(1, PACK - 1):
             nc.vector.tensor_copy(f1[:, t, :], window(1, t, SPLIT, C))
         for h in range(2):
             nc.vector.tensor_copy(f1[:, PACK - 1, h * U : (h + 1) * U], window(1, PACK - 1, SPLIT + h * U, U))
-        where = {3: [(3, 4), (4, 5), (0, 6)], 0: [(3, 7), (4, 3), (0, 1)], 1: [(1, 5), (2, 0), (0, 6)], (2, 0): [(1, 7), (0, 3), (2, 4)], (2, 1): [(1, 1), (2, 2), (0, 5)]}
+        where = {3: [(3, 4), (4, 5), (0, 6)], 0: [(3, 7), (4, 3), (0, 1)], 1: [(1, 5), (2, 0), (0, 6)], (2, 0): [(3, 7), (0, 3)], (2, 1): [(4, 1), (0, 2)]}
         passes(3, 0, where[3])
         for h in range(2):
             vector_gate(-1 - h, f1, SPLIT + h * U, U, SPLIT)
@@ -262,9 +263,11 @@ def tile_moe_bdx_lin_none_kernel(tc, dyT, w_words, w_scales, gate, offs, out):
         empty(staged[:, U : 3 * U], 3, 3)
         spread_gates(1, 4)
         empty(staged[:, 3 * U : 5 * U], 3, 4)
+        empty(firsts[:, 3 * C :], 3, 0, 0, U)
         vector_gate(2 * C, p1, 0, SHARE)
         scatters(3, 0)
-        vector_gate(C, p0, C, C)
+        vector_gate(C + AHEAD, p0, C + AHEAD, C - AHEAD)
+        vector_scatter(3 * C, U, firsts[:, 3 * C :])
         code_of[0, 1] = codes01[:], code_scales[1][:, 0:C]
         quantise(*code_of[0, 1], 2 * C, C)
         passes(0, 1, where[0])
@@ -273,52 +276,55 @@ def tile_moe_bdx_lin_none_kernel(tc, dyT, w_words, w_scales, gate, offs, out):
             code_of[e, 0] = later0[:, i * C : (i + 1) * C], code_scales[0][:, HALF + i * C : HALF + (i + 1) * C]
         quantise(later0[:], code_scales[0][:, HALF:T], 0, HALF)
 
-        gpsimd_gate(0, p1, C, C)
+        gpsimd_gate(LATER, p1, C + LATER, C - LATER)
         empty(staged[:, 6 * U : 8 * U], 0, 3)
         empty(staged[:, 8 * U : 10 * U], 0, 4)
         scatters(0, 1)
-        empty(p1[:, 0, 0:C], 3, 0)
+        empty(p1[:, 0, U:C], 3, 0, U, U)
         empty(firsts[:, 0:C], 0, 0)
         passes(1, 0, where[1])
-        vector_scatter(3 * C, C, p1[:, 0, 0:C])
+        vector_scatter(3 * C + U, U, p1[:, 0, U:C])
+        vector_gate(0, p1, C, LATER)
+        vector_scatter(0, U, firsts[:, 0:U])
         code_of[1, 1] = codes11[:], code_scales[1][:, C : 2 * C]
         quantise(*code_of[1, 1], 0, C)
         passes(1, 1, where[1])
-        vector_scatter(0, U, firsts[:, 0:U])
+        vector_scatter(U, U, firsts[:, U:C])
 
         code_of[2, 1] = codes21[:], code_scales[1][:, 2 * C : 3 * C]
         ones = staged[:, 5 * C : 7 * C]
-        own = firsts[:, C:]
+        twos = staged[:, 7 * C : 9 * C]
+        both = staged[:, 5 * C :].rearrange("p (i s) -> p i s", i=2)
 
         def unit(h):
             quantise(codes21[:, h * U : (h + 1) * U], code_scales[1][:, 2 * C + h * U : 2 * C + (h + 1) * U], 0, U)
             passes(2, 1, where[2, h], h)
 
+        def empty_unit(h):
+            lo = C + h * U
+            nc.vector.tensor_copy(both[:, :, lo : lo + U], banks[(2, h), 3 + h][:].rearrange("p (i s) -> p i s", i=2))
+            empty(firsts[:, C + lo : C + lo + U], (2, h), 0, 0, U)
+
         gpsimd_gate(0, woven[0], 2 * C, U, base=2 * C)
         for h in range(2):
             passes(2, 0, where[2, h], h)
         empty(ones[:, 0:C], 1, 1)
-        empty(staged[:, 7 * C : 7 * C + U], 1, 2, 0, U)
-        empty(own[:, 0:C], 1, 0)
+        empty(twos[:, 0:C], 1, 2)
+        empty(firsts[:, C : 2 * C], 1, 0)
         scalar_scatter(1, C, WIDE, ones[:, 0:WIDE])
-        scalar_scatter(2, C, U, staged[:, 7 * C : 7 * C + U])
+        scalar_scatter(2, C, U, twos[:, 0:U])
         unit(0)
         gpsimd_gate(0, woven[1], 2 * C + U, U, base=2 * C + U)
-        vector_scatter(U, WIDE, firsts[:, U : U + WIDE])
-        empty(ones[:, C : C + U], (2, 0), 1, 0, U)
-        empty(own[:, C : C + U], (2, 0), 0, 0, U)
+        vector_scatter(C, WIDE, firsts[:, C : C + WIDE])
+        empty_unit(0)
         scalar_scatter(1, C + WIDE, WIDE, ones[:, WIDE : 2 * WIDE])
         unit(1)
-        late = staged[:, 6 * U : 9 * U]
-        empty(late[:, 0:U], 1, 2, U, U)
-        empty(late[:, U:C], (2, 0), 2, 0, U)
-        empty(ones[:, C + U :], (2, 1), 1, 0, U)
-        empty(late[:, C:], (2, 1), 2, 0, U)
-        empty(own[:, C + U :], (2, 1), 0, 0, U)
-        vector_scatter(U + WIDE, SPLIT - U - WIDE, firsts[:, U + WIDE :])
+        vector_scatter(C + WIDE, U, firsts[:, C + WIDE : C + WIDE + U])
+        empty_unit(1)
+        vector_scatter(SPLIT - WIDE, WIDE, firsts[:, SPLIT - WIDE : SPLIT])
         scalar_scatter(1, 5 * U, U, ones[:, C + U :])
-        for lo, n in [(WIDE, WIDE), (0, WIDE)]:
-            scalar_scatter(2, 3 * U + lo, n, late[:, lo : lo + n])
+        for lo in (U + WIDE, U):
+            scalar_scatter(2, C + lo, WIDE, twos[:, lo : lo + WIDE])
         nc.sync.dma_start(out[P : 2 * P, :], outs[1][:])
         nc.sync.dma_start(out[0:P, :], outs[0][:])
         nc.sync.dma_start(out[2 * P : 3 * P, 0 : T // 2], outs[2][:, 0 : T // 2])

@@ -70,8 +70,8 @@ def tile_moe_bdx_lin_none_kernel(tc, dyT, w_words, w_scales, gate, offs, out):
         plain0 = held.tile([P, PACK * HALF], F32, name="plain0", tag="plain0", align_bytes=MX_ALIGN)
         plain1 = held.tile([P, PACK * HALF], F32, name="plain1", tag="plain1")
         first1 = held.tile([P, PACK * C], F32, name="first1")
-        staged = held.tile([P, 18 * U], F32, name="staged")
-        firsts = held.tile([P, 7 * U], F32, name="firsts")
+        staged = held.tile([P, 19 * U], F32, name="staged")
+        firsts = held.tile([P, 3 * U], F32, name="firsts")
 
         dy_rows = dyT.rearrange("(a p t) c -> a t p c", a=PASSES, p=P, t=PACK)
         landing = [(a, t) for a in range(PASSES) for t in range(PACK)]
@@ -211,7 +211,7 @@ def tile_moe_bdx_lin_none_kernel(tc, dyT, w_words, w_scales, gate, offs, out):
             nc.vector.tensor_copy(outs[0][:].indirect(listed(lo, n)), src)
 
         p0, p1, g0, f1 = by_plane(plain0[:]), by_plane(plain1[:]), by_plane(gated0[:]), by_plane(first1[:])
-        woven = [by_plane(staged[:, 5 * h * U : (5 * h + PACK) * U]) for h in range(2)]
+        woven = [by_plane(staged[:, 6 * h * U : (6 * h + PACK) * U]) for h in range(2)]
 
         def weave(h, t):
             nc.scalar.activation(woven[h][:, t, :], window(1, t, HALF + h * U, U), COPY)
@@ -254,7 +254,7 @@ def tile_moe_bdx_lin_none_kernel(tc, dyT, w_words, w_scales, gate, offs, out):
 
         def scatters(e, h):
             for j in range(4):
-                scalar_scatter(1 + j % 2, e * C + j // 2 * U, U, staged[:, (5 * h + 1 + j) * U : (5 * h + 2 + j) * U])
+                scalar_scatter(1 + j % 2, e * C + j // 2 * U, U, staged[:, (6 * h + 1 + j) * U : (6 * h + 2 + j) * U])
                 if j:
                     weave(h, j)
 
@@ -263,11 +263,11 @@ def tile_moe_bdx_lin_none_kernel(tc, dyT, w_words, w_scales, gate, offs, out):
         empty(staged[:, U : 3 * U], 3, 3)
         spread_gates(1, 4)
         empty(staged[:, 3 * U : 5 * U], 3, 4)
-        empty(firsts[:, 3 * C :], 3, 0, 0, U)
+        empty(firsts[:, C:], 3, 0, 0, U)
         vector_gate(2 * C, p1, 0, SHARE)
         scatters(3, 0)
         vector_gate(C + AHEAD, p0, C + AHEAD, C - AHEAD)
-        vector_scatter(3 * C, U, firsts[:, 3 * C :])
+        vector_scatter(3 * C, U, firsts[:, C:])
         code_of[0, 1] = codes01[:], code_scales[1][:, 0:C]
         quantise(*code_of[0, 1], 2 * C, C)
         passes(0, 1, where[0])
@@ -277,8 +277,8 @@ def tile_moe_bdx_lin_none_kernel(tc, dyT, w_words, w_scales, gate, offs, out):
         quantise(later0[:], code_scales[0][:, HALF:T], 0, HALF)
 
         gpsimd_gate(LATER, p1, C + LATER, C - LATER)
-        empty(staged[:, 6 * U : 8 * U], 0, 3)
-        empty(staged[:, 8 * U : 10 * U], 0, 4)
+        empty(staged[:, 7 * U : 9 * U], 0, 3)
+        empty(staged[:, 9 * U : 11 * U], 0, 4)
         scatters(0, 1)
         empty(p1[:, 0, U:C], 3, 0, U, U)
         empty(firsts[:, 0:C], 0, 0)
@@ -292,39 +292,39 @@ def tile_moe_bdx_lin_none_kernel(tc, dyT, w_words, w_scales, gate, offs, out):
         vector_scatter(U, U, firsts[:, U:C])
 
         code_of[2, 1] = codes21[:], code_scales[1][:, 2 * C : 3 * C]
-        ones = staged[:, 5 * C : 7 * C]
-        twos = staged[:, 7 * C : 9 * C]
-        both = staged[:, 5 * C :].rearrange("p (i s) -> p i s", i=2)
+        own = staged[:, 4 * U : 8 * U]
+        both = staged[:, 11 * U :].rearrange("p (i s) -> p i s", i=2)
+        ones, twos = both[:, 0, :], both[:, 1, :]
 
         def unit(h):
             quantise(codes21[:, h * U : (h + 1) * U], code_scales[1][:, 2 * C + h * U : 2 * C + (h + 1) * U], 0, U)
             passes(2, 1, where[2, h], h)
 
-        def empty_unit(h):
-            lo = C + h * U
-            nc.vector.tensor_copy(both[:, :, lo : lo + U], banks[(2, h), 3 + h][:].rearrange("p (i s) -> p i s", i=2))
-            empty(firsts[:, C + lo : C + lo + U], (2, h), 0, 0, U)
+        def empty_pair(h):
+            nc.vector.tensor_copy(both[:, :, C + h * U : C + (h + 1) * U], banks[(2, h), 3 + h][:].rearrange("p (i s) -> p i s", i=2))
 
         gpsimd_gate(0, woven[0], 2 * C, U, base=2 * C)
         for h in range(2):
             passes(2, 0, where[2, h], h)
         empty(ones[:, 0:C], 1, 1)
         empty(twos[:, 0:C], 1, 2)
-        empty(firsts[:, C : 2 * C], 1, 0)
+        empty(own[:, 0:C], 1, 0)
         scalar_scatter(1, C, WIDE, ones[:, 0:WIDE])
-        scalar_scatter(2, C, U, twos[:, 0:U])
+        scalar_scatter(2, C, WIDE, twos[:, 0:WIDE])
         unit(0)
         gpsimd_gate(0, woven[1], 2 * C + U, U, base=2 * C + U)
-        vector_scatter(C, WIDE, firsts[:, C : C + WIDE])
-        empty_unit(0)
+        vector_scatter(C, WIDE, own[:, 0:WIDE])
+        empty_pair(0)
         scalar_scatter(1, C + WIDE, WIDE, ones[:, WIDE : 2 * WIDE])
+        empty(own[:, C : C + U], (2, 0), 0, 0, U)
         unit(1)
-        vector_scatter(C + WIDE, U, firsts[:, C + WIDE : C + WIDE + U])
-        empty_unit(1)
-        vector_scatter(SPLIT - WIDE, WIDE, firsts[:, SPLIT - WIDE : SPLIT])
+        vector_scatter(C + WIDE, U, own[:, WIDE : WIDE + U])
+        empty_pair(1)
+        empty(own[:, C + U :], (2, 1), 0, 0, U)
+        vector_scatter(SPLIT - WIDE, WIDE, own[:, HALF - WIDE :])
         scalar_scatter(1, 5 * U, U, ones[:, C + U :])
-        for lo in (U + WIDE, U):
-            scalar_scatter(2, C + lo, WIDE, twos[:, lo : lo + WIDE])
+        for lo, hi in [(HALF - WIDE, HALF), (WIDE, HALF - WIDE)]:
+            scalar_scatter(2, C + lo, hi - lo, twos[:, lo:hi])
         nc.sync.dma_start(out[P : 2 * P, :], outs[1][:])
         nc.sync.dma_start(out[0:P, :], outs[0][:])
         nc.sync.dma_start(out[2 * P : 3 * P, 0 : T // 2], outs[2][:, 0 : T // 2])

@@ -70,8 +70,8 @@ def tile_moe_bdx_lin_none_kernel(tc, dyT, w_words, w_scales, gate, offs, out):
         plain0 = held.tile([P, PACK * HALF], F32, name="plain0", tag="plain0", align_bytes=MX_ALIGN)
         plain1 = held.tile([P, PACK * HALF], F32, name="plain1", tag="plain1")
         first1 = held.tile([P, PACK * C], F32, name="first1")
-        staged = held.tile([P, 19 * U], F32, name="staged")
-        firsts = held.tile([P, 3 * U], F32, name="firsts")
+        staged = held.tile([P, 21 * U], F32, name="staged")
+        firsts = held.tile([P, 5 * U], F32, name="firsts")
 
         dy_rows = dyT.rearrange("(a p t) c -> a t p c", a=PASSES, p=P, t=PACK)
         landing = [(a, t) for a in range(PASSES) for t in range(PACK)]
@@ -207,8 +207,8 @@ def tile_moe_bdx_lin_none_kernel(tc, dyT, w_words, w_scales, gate, offs, out):
         def scalar_scatter(kt, lo, n, src):
             nc.scalar.activation(outs[kt][:].indirect(listed(lo, n)), src, COPY)
 
-        def vector_scatter(lo, n, src):
-            nc.vector.tensor_copy(outs[0][:].indirect(listed(lo, n)), src)
+        def vector_scatter(lo, n, src, kt=0):
+            nc.vector.tensor_copy(outs[kt][:].indirect(listed(lo, n)), src)
 
         p0, p1, g0, f1 = by_plane(plain0[:]), by_plane(plain1[:]), by_plane(gated0[:]), by_plane(first1[:])
         woven = [by_plane(staged[:, 6 * h * U : (6 * h + PACK) * U]) for h in range(2)]
@@ -236,7 +236,7 @@ def tile_moe_bdx_lin_none_kernel(tc, dyT, w_words, w_scales, gate, offs, out):
             nc.vector.tensor_copy(f1[:, t, :], window(1, t, SPLIT, C))
         for h in range(2):
             nc.vector.tensor_copy(f1[:, PACK - 1, h * U : (h + 1) * U], window(1, PACK - 1, SPLIT + h * U, U))
-        where = {3: [(3, 4), (4, 5), (0, 6)], 0: [(3, 7), (4, 3), (0, 1)], 1: [(1, 5), (2, 0), (0, 6)], (2, 0): [(3, 7), (0, 3)], (2, 1): [(4, 1), (0, 2)]}
+        where = {3: [(3, 4), (4, 5), (0, 6)], 0: [(3, 7), (4, 3), (0, 1)], 1: [(2, 0), (1, 5), (0, 6)], (2, 0): [(3, 7), (0, 3)], (2, 1): [(4, 1), (0, 2)]}
         passes(3, 0, where[3])
         for h in range(2):
             vector_gate(-1 - h, f1, SPLIT + h * U, U, SPLIT)
@@ -252,22 +252,22 @@ def tile_moe_bdx_lin_none_kernel(tc, dyT, w_words, w_scales, gate, offs, out):
         def empty(dst, e, kt, lo=0, n=C):
             nc.vector.tensor_copy(dst, banks[e, kt][:, lo : lo + n])
 
-        def scatters(e, h):
-            for j in range(4):
-                scalar_scatter(1 + j % 2, e * C + j // 2 * U, U, staged[:, (6 * h + 1 + j) * U : (6 * h + 2 + j) * U])
-                if j:
-                    weave(h, j)
+        def scatters(e, h, steps):
+            for kt, u, at, t in steps:
+                scalar_scatter(kt, e * C + u * U, U, staged[:, at * U : (at + 1) * U])
+                if t:
+                    weave(h, t)
 
         gpsimd_gate(2 * C + SHARE, p1, SHARE, C - SHARE, gates0[:])
         passes(0, 0, where[0])
         empty(staged[:, U : 3 * U], 3, 3)
         spread_gates(1, 4)
         empty(staged[:, 3 * U : 5 * U], 3, 4)
-        empty(firsts[:, C:], 3, 0, 0, U)
+        empty(firsts[:, HALF:], 3, 0, 0, U)
         vector_gate(2 * C, p1, 0, SHARE)
-        scatters(3, 0)
+        scatters(3, 0, [(1, 0, 1, 0), (2, 0, 2, 1), (1, 1, 3, 2), (2, 1, 4, 3)])
         vector_gate(C + AHEAD, p0, C + AHEAD, C - AHEAD)
-        vector_scatter(3 * C, U, firsts[:, C:])
+        vector_scatter(3 * C, U, firsts[:, HALF:])
         code_of[0, 1] = codes01[:], code_scales[1][:, 0:C]
         quantise(*code_of[0, 1], 2 * C, C)
         passes(0, 1, where[0])
@@ -278,22 +278,23 @@ def tile_moe_bdx_lin_none_kernel(tc, dyT, w_words, w_scales, gate, offs, out):
 
         gpsimd_gate(LATER, p1, C + LATER, C - LATER)
         empty(staged[:, 7 * U : 9 * U], 0, 3)
-        empty(staged[:, 9 * U : 11 * U], 0, 4)
-        scatters(0, 1)
+        empty(staged[:, 11 * U : 13 * U], 0, 4)
+        scatters(0, 1, [(2, 0, 8, 0), (1, 0, 7, 2), (2, 1, 12, 1), (1, 1, 11, 0)])
         empty(p1[:, 0, U:C], 3, 0, U, U)
-        empty(firsts[:, 0:C], 0, 0)
+        empty(staged[:, 9 * U : 11 * U], 0, 0)
         passes(1, 0, where[1])
         vector_scatter(3 * C + U, U, p1[:, 0, U:C])
         vector_gate(0, p1, C, LATER)
-        vector_scatter(0, U, firsts[:, 0:U])
+        vector_scatter(0, U, staged[:, 9 * U : 10 * U])
         code_of[1, 1] = codes11[:], code_scales[1][:, C : 2 * C]
         quantise(*code_of[1, 1], 0, C)
         passes(1, 1, where[1])
-        vector_scatter(U, U, firsts[:, U:C])
+        vector_scatter(U, U, staged[:, 10 * U : 11 * U])
+        nc.vector.tensor_copy(woven[1][:, 3, :], window(1, 3, HALF + U, U))
 
         code_of[2, 1] = codes21[:], code_scales[1][:, 2 * C : 3 * C]
-        own = staged[:, 4 * U : 8 * U]
-        both = staged[:, 11 * U :].rearrange("p (i s) -> p i s", i=2)
+        own = firsts[:, 0:HALF]
+        both = staged[:, 13 * U :].rearrange("p (i s) -> p i s", i=2)
         ones, twos = both[:, 0, :], both[:, 1, :]
 
         def unit(h):
@@ -306,24 +307,25 @@ def tile_moe_bdx_lin_none_kernel(tc, dyT, w_words, w_scales, gate, offs, out):
         gpsimd_gate(0, woven[0], 2 * C, U, base=2 * C)
         for h in range(2):
             passes(2, 0, where[2, h], h)
+        empty(twos[:, 0:U], 1, 2, 0, U)
         empty(ones[:, 0:C], 1, 1)
-        empty(twos[:, 0:C], 1, 2)
         empty(own[:, 0:C], 1, 0)
+        scalar_scatter(2, C, U, twos[:, 0:U])
         scalar_scatter(1, C, WIDE, ones[:, 0:WIDE])
-        scalar_scatter(2, C, WIDE, twos[:, 0:WIDE])
         unit(0)
         gpsimd_gate(0, woven[1], 2 * C + U, U, base=2 * C + U)
         vector_scatter(C, WIDE, own[:, 0:WIDE])
         empty_pair(0)
         scalar_scatter(1, C + WIDE, WIDE, ones[:, WIDE : 2 * WIDE])
         empty(own[:, C : C + U], (2, 0), 0, 0, U)
+        empty(woven[1][:, 0, :], 1, 2, U, U)
         unit(1)
-        vector_scatter(C + WIDE, U, own[:, WIDE : WIDE + U])
+        vector_scatter(C + U, U, woven[1][:, 0, :], 2)
         empty_pair(1)
         empty(own[:, C + U :], (2, 1), 0, 0, U)
-        vector_scatter(SPLIT - WIDE, WIDE, own[:, HALF - WIDE :])
+        vector_scatter(C + WIDE, HALF - WIDE, own[:, WIDE:])
         scalar_scatter(1, 5 * U, U, ones[:, C + U :])
-        for lo, hi in [(HALF - WIDE, HALF), (WIDE, HALF - WIDE)]:
+        for lo, hi in [(C + U, HALF), (C, C + U)]:
             scalar_scatter(2, C + lo, hi - lo, twos[:, lo:hi])
         nc.sync.dma_start(out[P : 2 * P, :], outs[1][:])
         nc.sync.dma_start(out[0:P, :], outs[0][:])

@@ -76,9 +76,10 @@ def tile_moe_bdx_lin_none_kernel(tc, dyT, w_words, w_scales, gate, offs, out):
         dy_rows = dyT.rearrange("(a p t) c -> a t p c", a=PASSES, p=P, t=PACK)
         landing = [(a, t) for a in range(PASSES) for t in range(PACK)]
 
-        warm = held.tile([P, 2], F32, name="warm")
-        nc.vector.memset(warm[:, 0:1], 0.0)
-        nc.scalar.activation(warm[:, 1:2], warm[:, 0:1], COPY)
+        warm = held.tile([P, 1], F32, name="warm")
+        zeros = held.tile([P, P], F32, name="zeros")
+        nc.vector.memset(zeros[:], 0.0)
+        nc.scalar.activation(warm[:], zeros[:, 0:1], COPY)
         for plane in word_scales:
             nc.vector.memset(plane[:].bitcast(I32), 0)
 
@@ -207,8 +208,8 @@ def tile_moe_bdx_lin_none_kernel(tc, dyT, w_words, w_scales, gate, offs, out):
         def scalar_scatter(kt, lo, n, src):
             nc.scalar.activation(outs[kt][:].indirect(listed(lo, n)), src, COPY)
 
-        def vector_scatter(lo, n, src, kt=0):
-            nc.vector.tensor_copy(outs[kt][:].indirect(listed(lo, n)), src)
+        def vector_scatter(lo, n, src):
+            nc.vector.tensor_copy(outs[0][:].indirect(listed(lo, n)), src)
 
         p0, p1, g0, f1 = by_plane(plain0[:]), by_plane(plain1[:]), by_plane(gated0[:]), by_plane(first1[:])
         woven = [by_plane(staged[:, 6 * h * U : (6 * h + PACK) * U]) for h in range(2)]
@@ -307,10 +308,10 @@ def tile_moe_bdx_lin_none_kernel(tc, dyT, w_words, w_scales, gate, offs, out):
         gpsimd_gate(0, woven[0], 2 * C, U, base=2 * C)
         for h in range(2):
             passes(2, 0, where[2, h], h)
-        empty(twos[:, 0:U], 1, 2, 0, U)
+        empty(twos[:, P:C], 1, 2, P, C - P)
         empty(ones[:, 0:C], 1, 1)
         empty(own[:, 0:C], 1, 0)
-        scalar_scatter(2, C, U, twos[:, 0:U])
+        scalar_scatter(2, C + P, U, twos[:, P : P + U])
         scalar_scatter(1, C, WIDE, ones[:, 0:WIDE])
         unit(0)
         gpsimd_gate(0, woven[1], 2 * C + U, U, base=2 * C + U)
@@ -318,14 +319,14 @@ def tile_moe_bdx_lin_none_kernel(tc, dyT, w_words, w_scales, gate, offs, out):
         empty_pair(0)
         scalar_scatter(1, C + WIDE, WIDE, ones[:, WIDE : 2 * WIDE])
         empty(own[:, C : C + U], (2, 0), 0, 0, U)
-        empty(woven[1][:, 0, :], 1, 2, U, U)
+        empty(woven[1][:, 0, 0:P], 1, 2, 0, P)
         unit(1)
-        vector_scatter(C + U, U, woven[1][:, 0, :], 2)
+        nc.vector.tensor_tensor(outs[2][:].indirect(listed(C, P)), woven[1][:, 0, 0:P], zeros[:], ADD)
         empty_pair(1)
         empty(own[:, C + U :], (2, 1), 0, 0, U)
         vector_scatter(C + WIDE, HALF - WIDE, own[:, WIDE:])
         scalar_scatter(1, 5 * U, U, ones[:, C + U :])
-        for lo, hi in [(C + U, HALF), (C, C + U)]:
+        for lo, hi in [(HALF - WIDE, HALF), (WIDE, HALF - WIDE)]:
             scalar_scatter(2, C + lo, hi - lo, twos[:, lo:hi])
         nc.sync.dma_start(out[P : 2 * P, :], outs[1][:])
         nc.sync.dma_start(out[0:P, :], outs[0][:])

from contextlib import ExitStack

import concourse.mybir as mybir
from concourse.masks import make_identity

K, T, E, C, N = 384, 2048, 4, 512, 1024
FLOPS = 2 * K * N * E * C
BYTES = 4 * N * T + 2 * E * N * K // 4 + E * N // 32 * K + 4 * T + 2 * 128 * T // 16 + 4 * K * T

F32 = mybir.dt.float32
BF16 = mybir.dt.bfloat16
I32 = mybir.dt.int32
U32 = mybir.dt.uint32
U16 = mybir.dt.uint16
U8 = mybir.dt.uint8
FP8X4 = mybir.dt.float8_e5m2_x4
FP4X4 = mybir.dt.float4_e2m1fn_x4
MULT = mybir.AluOpType.mult
ADD = mybir.AluOpType.add
COPY = mybir.ActivationFunctionType.Copy

P = 128
PACK = 4
PASSES = N // (P * PACK)
KT = K // P
GROUPS = E * PASSES
HALF = 2 * C
PER_COLUMN = 16
LINE = 4
QUADRANTS = 4
MX_ALIGN = 64

U = 256
SPLIT = 3 * C
AHEAD = 192
SHARE = 128
LATER = 64
WIDE = 384


def tile_moe_bdx_lin_none_kernel(tc, dyT, w_words, w_scales, gate, offs, out):
    nc = tc.nc
    with ExitStack() as ctx:
        held = ctx.enter_context(tc.tile_pool(name="held", bufs=1))
        psum = ctx.enter_context(tc.psum_pool(name="psum", bufs=1))

        def by_plane(ap):
            return ap.rearrange("p (t s) -> p t s", t=PACK)

        offsets = held.tile([P, T // PER_COLUMN], U16, name="offsets")
        dy = {(a, t): held.tile([P, T], F32, name=f"dy{a}{t}") for a in range(PASSES) for t in range(PACK)}
        parts = [(GROUPS - PASSES, GROUPS), (0, PASSES), (PASSES, GROUPS - PASSES)]
        words = [held.tile([P, (hi - lo) * 2 * K], U8, name=f"words{lo}", align_bytes=MX_ALIGN) for lo, hi in parts]
        word_scales = [held.tile([P, (hi - lo) * K], U8, name=f"word_scales{lo}", align_bytes=MX_ALIGN) for lo, hi in parts]
        outs = [held.tile([P, T], F32, name=f"outs{kt}") for kt in range(KT)]
        gate_cols = [held.tile([P, 2 * LINE], F32, name=f"gate_cols{h}") for h in range(2)]
        identity = held.tile([P, P], F32, name="identity")
        code_scales = [held.tile([P, T], U8, name=f"code_scales{a}", align_bytes=MX_ALIGN) for a in range(PASSES)]
        codes30 = held.tile([P, C], U32, name="codes30", align_bytes=MX_ALIGN)
        halves = [held.tile([P, PACK * U], BF16, name=f"half{h}", tag=f"half{h}", align_bytes=MX_ALIGN) for h in range(2)]
        codes11 = held.tile([P, C], U32, name="codes11", align_bytes=MX_ALIGN)
        codes21 = held.tile([P, C], U32, name="codes21", align_bytes=MX_ALIGN)
        gates0 = held.tile([P, C - SHARE], F32, name="gates_first", tag="gates_first", align_bytes=MX_ALIGN)
        codes01 = held.tile([P, C], U32, name="codes01", align_bytes=MX_ALIGN)
        gates2 = held.tile([P, AHEAD], F32, name="gates2", tag="gates2", align_bytes=MX_ALIGN)
        room = held.tile([P, 6 * C], F32, name="room", align_bytes=MX_ALIGN)
        rounded = room[:].bitcast(BF16)
        gated0 = held.tile([P, PACK * HALF], F32, name="gated0")
        gates = [held.tile([P, HALF], F32, name=f"gates{h}") for h in range(2)]
        plain0 = held.tile([P, PACK * HALF], F32, name="plain0", tag="plain0", align_bytes=MX_ALIGN)
        plain1 = held.tile([P, PACK * HALF], F32, name="plain1", tag="plain1")
        first1 = held.tile([P, PACK * C], F32, name="first1")
        staged = held.tile([P, 21 * U], F32, name="staged")
        firsts = held.tile([P, 5 * U], F32, name="firsts")

        dy_rows = dyT.rearrange("(a p t) c -> a t p c", a=PASSES, p=P, t=PACK)
        landing = [(a, t) for a in range(PASSES) for t in range(PACK)]

        warm = held.tile([P, 1], F32, name="warm")
        zeros = held.tile([P, P], F32, name="zeros")
        nc.vector.memset(zeros[:], 0.0)
        nc.scalar.activation(warm[:], zeros[:, 0:1], COPY)
        for plane in word_scales:
            nc.vector.memset(plane[:].bitcast(I32), 0)

        gate_rows = gate[0, :].rearrange("(h e p i) -> h p e i", h=2, e=2, i=LINE)
        nc.sync.dma_start(gate_cols[1][:].rearrange("p (e i) -> p e i", e=2), gate_rows[1])
        nc.sync.dma_start(dy[landing[0]][:], dy_rows[landing[0]])
        nc.sync.dma_start(offsets[:], offs)
        word_rows = w_words.bitcast(I32).rearrange("e a p b -> p (e a) b")
        scale_rows = w_scales.bitcast(I32).rearrange("e a f k -> f (e a) k")

        def load_words(part):
            lo, hi = parts[part]
            nc.sync.dma_start(words[part][:].bitcast(I32).rearrange("p (g b) -> p g b", g=hi - lo), word_rows[:, lo:hi, :])

        def load_scales(part):
            lo, hi = parts[part]
            for q in range(QUADRANTS):
                nc.sync.dma_start(
                    word_scales[part][32 * q : 32 * q + 4, :].bitcast(I32).rearrange("p (g k) -> p g k", g=hi - lo),
                    scale_rows[4 * q : 4 * q + 4, lo:hi, :],
                )

        for at in landing[1:3]:
            nc.sync.dma_start(dy[at][:], dy_rows[at])
        nc.sync.dma_start(gate_cols[0][:].rearrange("p (e i) -> p e i", e=2), gate_rows[0])
        for at in landing[3:-1]:
            nc.sync.dma_start(dy[at][:], dy_rows[at])
        load_scales(0)
        nc.sync.dma_start(dy[landing[-1]][:], dy_rows[landing[-1]])
        nc.sync.dma_start(gates2[:], gate[0:P, C : C + AHEAD])
        load_words(0)
        load_scales(1)
        load_words(1)
        nc.sync.dma_start(gates0[:], gate[P : 2 * P, SHARE : C])
        nc.sync.dma_start(gates[0][:, C + LATER :], gate[P : 2 * P, C + LATER : HALF])
        load_scales(2)
        load_words(2)

        def bank_tile(b):
            return psum.tile([P, C], F32, name="bank", tag=f"bank{b}")

        make_identity(nc, identity[:])
        gate_banks = {}

        def spread_gates(e, b):
            bank = bank_tile(b)
            for i in range(LINE):
                col = e % 2 * LINE + i
                nc.tensor.transpose(bank[:, i * P : (i + 1) * P], gate_cols[e // 2][:, col : col + 1].to_broadcast([P, P]), identity[:])
            gate_banks[e] = bank[:].rearrange("m (i c) -> m c i", i=LINE)

        for e in (3, 2, 0):
            spread_gates(e, e)

        def gate_row(lo, n):
            return gates[lo // HALF][:, lo % HALF : lo % HALF + n]

        def banked_gates(lo, n):
            e, c = divmod(lo, C)
            return gate_banks[e][:, c // LINE : (c + n) // LINE, :]

        for lo in (3 * C, 2 * C):
            nc.vector.tensor_copy(gate_row(lo, C).rearrange("m (c i) -> m c i", i=LINE), banked_gates(lo, C))

        def listed(lo, n):
            return offsets[:, lo // PER_COLUMN : (lo + n) // PER_COLUMN]

        def window(a, t, lo, n):
            return dy[a, t][:].indirect(listed(lo, n))

        def words_at(at, n):
            return halves[-at - 1][:] if at < 0 else rounded[:, PACK * at : PACK * (at + n)]

        def vector_gate(at, planes, lo, n, base=0):
            nc.vector.tensor_tensor(
                words_at(at, n).rearrange("p (c i t) -> p c t i", i=LINE, t=PACK),
                planes[:, :, lo - base : lo - base + n].rearrange("p t (c i) -> p c t i", i=LINE),
                banked_gates(lo, n).unsqueeze(2).to_broadcast([P, n // LINE, PACK, LINE]),
                MULT,
            )

        def gpsimd_gate(at, planes, lo, n, row=None, base=0):
            nc.gpsimd.tensor_tensor(
                words_at(at, n).rearrange("p (s t) -> p s t", t=PACK),
                planes[:, :, lo - base : lo - base + n].rearrange("p t s -> p s t"),
                (gate_row(lo, n) if row is None else row).unsqueeze(2).to_broadcast([P, n, PACK]),
                MULT,
            )

        def gpsimd_interleave(at, src):
            nc.gpsimd.tensor_scalar(
                words_at(at, src.shape[2]).rearrange("p (s t) -> p s t", t=PACK), src.rearrange("p t s -> p s t"), 1.0, 0.0, MULT, ADD
            )

        def quantise(dst, scales, at, n):
            nc.vector.quantize_mx(out=dst.bitcast(FP8X4), scales=scales, in_=words_at(at, n))

        code_of = {}
        banks = {}

        def one_pass(dst, e, a, kt, lo, n, start, stop):
            part = [1, 2, 2, 0][e]
            words_e, scales_e = code_of[e, a]
            w0 = (e * PASSES + a - parts[part][0]) * K + P * kt
            nc.tensor.matmul_mx(
                out=dst,
                lhsT=words[part][:, 2 * w0 : 2 * (w0 + P)].bitcast(FP4X4),
                lhsT_scale=word_scales[part][:, w0 : w0 + P],
                rhs=words_e[:, lo : lo + n].bitcast(FP8X4),
                rhs_scale=scales_e[:, lo : lo + n],
                start=start,
                stop=stop,
            )

        def passes(e, a, where, h=None):
            key, lo, n = (e, 0, C) if h is None else ((e, h), h * U, U)
            for kt, b in where:
                if a == 0:
                    banks[key, kt] = bank_tile(b)
                if kt in (0, 1, 2):
                    one_pass(banks[key, kt][:, 0:n], e, a, kt, lo, n, a == 0, a == 1)
                else:
                    for i in range(2):
                        one_pass(banks[key, kt][:, i * U : (i + 1) * U], e, a, 1 + i, (kt - 3) * U, U, a == 0 and i == 0, a == 1 and i == 1)

        def scalar_scatter(kt, lo, n, src):
            nc.scalar.activation(outs[kt][:].indirect(listed(lo, n)), src, COPY)

        def vector_scatter(lo, n, src):
            nc.vector.tensor_copy(outs[0][:].indirect(listed(lo, n)), src)

        p0, p1, g0, f1 = by_plane(plain0[:]), by_plane(plain1[:]), by_plane(gated0[:]), by_plane(first1[:])
        woven = [by_plane(staged[:, 6 * h * U : (6 * h + PACK) * U]) for h in range(2)]

        def weave(h, t):
            nc.scalar.activation(woven[h][:, t, :], window(1, t, HALF + h * U, U), COPY)

        for a, planes in enumerate([p0, p1]):
            for t in range(PACK):
                for lo, hi in [(0, HALF)] if t < PACK - 1 else [(0, C), (C, HALF)]:
                    nc.scalar.activation(planes[:, t, lo:hi], window(a, t, lo, hi - lo), COPY)
        for h in range(2):
            weave(h, 0)
        for t in range(PACK):
            nc.vector.tensor_tensor(g0[:, t, :], window(0, t, HALF, HALF), gates[1][:], MULT)
        code_of[3, 0] = codes30[:], code_scales[0][:, C:HALF]
        zero = 3 * U
        gpsimd_interleave(0, g0[:, :, C:])
        vector_gate(zero, p0, 0, C)
        nc.vector.tensor_copy(f1[:, 0, :], window(1, 0, SPLIT, C))
        quantise(*code_of[3, 0], 0, C)
        gpsimd_interleave(0, g0[:, :, 0:C])
        gpsimd_gate(C, p0, C, AHEAD, gates2[:])
        for t in range(1, PACK - 1):
            nc.vector.tensor_copy(f1[:, t, :], window(1, t, SPLIT, C))
        for h in range(2):
            nc.vector.tensor_copy(f1[:, PACK - 1, h * U : (h + 1) * U], window(1, PACK - 1, SPLIT + h * U, U))
        where = {3: [(3, 4), (4, 5), (0, 6)], 0: [(3, 7), (4, 3), (0, 1)], 1: [(2, 0), (1, 5), (0, 6)], (2, 0): [(3, 7), (0, 3)], (2, 1): [(4, 1), (0, 2)]}
        passes(3, 0, where[3])
        for h in range(2):
            vector_gate(-1 - h, f1, SPLIT + h * U, U, SPLIT)
        codes31 = held.tile([P, C], U32, name="codes31", tag="gates2", align_bytes=MX_ALIGN)
        code_of[3, 1] = codes31[:], code_scales[1][:, 3 * C :]
        for h in range(2):
            quantise(codes31[:, h * U : (h + 1) * U], code_scales[1][:, SPLIT + h * U : SPLIT + (h + 1) * U], -1 - h, U)
        passes(3, 1, where[3])
        codes00 = held.tile([P, C], U32, name="codes00", tag="half0", align_bytes=MX_ALIGN)
        code_of[0, 0] = codes00[:], code_scales[0][:, 0:C]
        quantise(*code_of[0, 0], zero, C)

        def empty(dst, e, kt, lo=0, n=C):
            nc.vector.tensor_copy(dst, banks[e, kt][:, lo : lo + n])

        def scatters(e, h, steps):
            for kt, u, at, t in steps:
                scalar_scatter(kt, e * C + u * U, U, staged[:, at * U : (at + 1) * U])
                if t:
                    weave(h, t)

        gpsimd_gate(2 * C + SHARE, p1, SHARE, C - SHARE, gates0[:])
        passes(0, 0, where[0])
        empty(staged[:, U : 3 * U], 3, 3)
        spread_gates(1, 4)
        empty(staged[:, 3 * U : 5 * U], 3, 4)
        empty(firsts[:, HALF:], 3, 0, 0, U)
        vector_gate(2 * C, p1, 0, SHARE)
        scatters(3, 0, [(1, 0, 1, 0), (2, 0, 2, 1), (1, 1, 3, 2), (2, 1, 4, 3)])
        vector_gate(C + AHEAD, p0, C + AHEAD, C - AHEAD)
        vector_scatter(3 * C, U, firsts[:, HALF:])
        code_of[0, 1] = codes01[:], code_scales[1][:, 0:C]
        quantise(*code_of[0, 1], 2 * C, C)
        passes(0, 1, where[0])
        later0 = held.tile([P, HALF], U32, name="later0", tag="gates_first", align_bytes=MX_ALIGN)
        for i, e in enumerate([2, 1]):
            code_of[e, 0] = later0[:, i * C : (i + 1) * C], code_scales[0][:, HALF + i * C : HALF + (i + 1) * C]
        quantise(later0[:], code_scales[0][:, HALF:T], 0, HALF)

        gpsimd_gate(LATER, p1, C + LATER, C - LATER)
        empty(staged[:, 7 * U : 9 * U], 0, 3)
        empty(staged[:, 11 * U : 13 * U], 0, 4)
        scatters(0, 1, [(2, 0, 8, 0), (1, 0, 7, 2), (2, 1, 12, 1), (1, 1, 11, 0)])
        empty(p1[:, 0, U:C], 3, 0, U, U)
        empty(staged[:, 9 * U : 11 * U], 0, 0)
        passes(1, 0, where[1])
        vector_scatter(3 * C + U, U, p1[:, 0, U:C])
        vector_gate(0, p1, C, LATER)
        vector_scatter(0, U, staged[:, 9 * U : 10 * U])
        code_of[1, 1] = codes11[:], code_scales[1][:, C : 2 * C]
        quantise(*code_of[1, 1], 0, C)
        passes(1, 1, where[1])
        vector_scatter(U, U, staged[:, 10 * U : 11 * U])
        nc.vector.tensor_copy(woven[1][:, 3, :], window(1, 3, HALF + U, U))

        code_of[2, 1] = codes21[:], code_scales[1][:, 2 * C : 3 * C]
        own = firsts[:, 0:HALF]
        both = staged[:, 13 * U :].rearrange("p (i s) -> p i s", i=2)
        ones, twos = both[:, 0, :], both[:, 1, :]

        def unit(h):
            quantise(codes21[:, h * U : (h + 1) * U], code_scales[1][:, 2 * C + h * U : 2 * C + (h + 1) * U], 0, U)
            passes(2, 1, where[2, h], h)

        def empty_pair(h):
            nc.vector.tensor_copy(both[:, :, C + h * U : C + (h + 1) * U], banks[(2, h), 3 + h][:].rearrange("p (i s) -> p i s", i=2))

        gpsimd_gate(0, woven[0], 2 * C, U, base=2 * C)
        for h in range(2):
            passes(2, 0, where[2, h], h)
        empty(twos[:, P:C], 1, 2, P, C - P)
        empty(ones[:, 0:C], 1, 1)
        empty(own[:, 0:C], 1, 0)
        scalar_scatter(2, C + P, U, twos[:, P : P + U])
        scalar_scatter(1, C, WIDE, ones[:, 0:WIDE])
        unit(0)
        gpsimd_gate(0, woven[1], 2 * C + U, U, base=2 * C + U)
        vector_scatter(C, WIDE, own[:, 0:WIDE])
        empty_pair(0)
        scalar_scatter(1, C + WIDE, WIDE, ones[:, WIDE : 2 * WIDE])
        empty(own[:, C : C + U], (2, 0), 0, 0, U)
        empty(woven[1][:, 0, 0:P], 1, 2, 0, P)
        unit(1)
        nc.vector.tensor_tensor(outs[2][:].indirect(listed(C, P)), woven[1][:, 0, 0:P], zeros[:], ADD)
        empty_pair(1)
        empty(own[:, C + U :], (2, 1), 0, 0, U)
        vector_scatter(C + WIDE, HALF - WIDE, own[:, WIDE:])
        scalar_scatter(1, 5 * U, U, ones[:, C + U :])
        for lo, hi in [(HALF - WIDE, HALF), (WIDE, HALF - WIDE)]:
            scalar_scatter(2, C + lo, hi - lo, twos[:, lo:hi])
        nc.sync.dma_start(out[P : 2 * P, :], outs[1][:])
        nc.sync.dma_start(out[0:P, :], outs[0][:])
        nc.sync.dma_start(out[2 * P : 3 * P, 0 : T // 2], outs[2][:, 0 : T // 2])
        nc.scalar.dma_start(out[2 * P : 3 * P, T // 2 : T], outs[2][:, T // 2 : T])
